import numpy as np, ml_dtypes
CORES = [83,85,87,115,117,119]
N = 6
import mx_ref
BF = ml_dtypes.bfloat16
def cols(t, e):
    v = np.concatenate([t.reshape(128, -1, 4), np.zeros((128, 1, 4), BF)], axis=1)
    return np.ascontiguousarray(v[:, e]).reshape(128, -1)
def cut(t, i, w=512):
    return t[:, w * i:w * i + w]
def pick(q, e):
    c = np.concatenate([q[0].reshape(128, -1, 4), np.zeros((128, 1, 4), np.uint8)], axis=1); s = np.concatenate([q[1], np.ones((16, 1), np.uint8)], axis=1)
    return (np.ascontiguousarray(c[:, e].reshape(128, -1)), np.ascontiguousarray(s[:, e]))
def join(*qs):
    return (np.concatenate([q[0] for q in qs], axis=1), np.concatenate([q[1] for q in qs], axis=1))
def put(q, e, v):
    c, s = q[0].reshape(128, -1, 4).copy(), q[1].copy(); c[:, e] = v[0].reshape(128, -1, 4); s[:, e] = v[1]
    return (c.reshape(128, -1), s)
def pk(c, s):
    return (np.ascontiguousarray(c), mx_ref.live(s))
def emit(q):
    return q[0], q[1]
def decode(q):
    o = []
    for b in range(4):
        e = np.zeros((128, 128, 4), np.float32); e[np.arange(128), np.arange(128), b] = 1
        o.append(mx_ref.matmul(mx_ref.quantize(e.reshape(128, 512).astype(BF)), q))
    return np.stack(o, axis=2).reshape(128, -1)
def f(rng, *shape):
    return mx_ref.flush((rng.standard_normal(shape, dtype=np.float32) * np.exp2(rng.integers(-2, 3, shape[:-1] + (1,)))).astype(BF))
def wide(rng, *shape, cols=0):
    v = rng.standard_normal(shape, dtype=np.float32) * np.exp2(rng.integers(-12, 13, shape)).astype(np.float32)
    if cols: v *= np.repeat(np.exp2(rng.integers(-cols, cols + 1, shape[:-2] + (1, shape[-1] // 4))) * (rng.random(shape[:-2] + (1, shape[-1] // 4)) > 0.0625), 4, axis=-1).astype(np.float32)
    return mx_ref.flush(v.astype(BF))
P, K, R, O = 192, 48, 2, 2
def big(v):
    v = v.astype(np.float32)
    v[np.abs(v) < np.float32(2.0 ** -16)] = 0
    return v.astype(BF)
def times(t, k):
    return mx_ref.flush((t.astype(np.float32) * np.float32(k)).astype(BF))
def signs(d, v, s):
    g = np.where(d["u"][0, :, :4].astype(np.float32) < 0, -1, 1)
    a = np.abs(v.astype(np.float32)).reshape(N, 128, -1, 4) * g[None, :, None, :] * s[:, None, :, None]
    return big(a.reshape(N, 128, -1))
def counted(rng, d):
    n = P // 2 + rng.permutation(K)[:N]
    return signs(d, d["tb"], np.stack([np.where(rng.permutation(P) < n[r], 1, -1) for r in range(N)]))
def setup_inputs(rng):
    v = np.zeros((128, 512), np.float32)
    v[:, :4] = f(rng, 128, 4).astype(np.float32)
    return {"tb": big(f(rng, N, 128, 4 * P)), "nz": big(f(rng, N, 128, 4 * R * K)), "u": np.stack([v.astype(BF)] * N), "w": f(rng, N, 128, 512 * O)}
def setup_inputs_down(rng):
    d = setup_inputs(rng)
    d["tb"] = counted(rng, d)
    d["nz"] = signs(d, 64 * (1 + rng.random((N, 128, 4 * R * K))), np.full((N, R * K), -1))
    return d
def setup_inputs_spread(rng):
    d = setup_inputs(rng)
    t, r = big(wide(rng, N, 128, 4 * P, cols=6)), int(rng.integers(0, N))
    x = (1 + rng.random((N, 128, 4 * P))) * np.exp2(rng.integers(12, 18, (N, 128, 4 * P)) + np.repeat(rng.integers(0, 4, (N, 1, P)), 4, axis=2))
    t[r] = signs(d, x, np.ones((N, P), np.int64))[r]
    return {**d, "tb": t, "nz": big(wide(rng, N, 128, 4 * R * K, cols=6)), "u": times(d["u"], 2.0 ** 24)}
def setup_inputs_swap(rng):
    d = setup_inputs(rng)
    d["tb"] = counted(rng, d)
    d["nz"] = signs(d, 64 * (1 + rng.random((N, 128, 4 * R * K))), np.full((N, R * K), 1))
    return d
def setup_inputs_ties(rng):
    d = setup_inputs(rng)
    a = rng.permutation(N) <= N // 2
    d["tb"] = np.stack([cols(d["tb"][int(a[r])], rng.permutation(P) % (P // (K + 1))) for r in range(N)])
    d["nz"] = np.stack([d["nz"][0]] * N)
    return d
def setup_inputs_zero(rng):
    d = setup_inputs(rng)
    d["u"] = times(np.abs(d["u"].astype(np.float32)), 2.0 ** -26)
    d["tb"], d["nz"] = big(times(d["tb"], 2.0 ** -10)), big(times(d["nz"], 2.0 ** -10))
    s, a = np.zeros((N, P), np.int64), rng.permutation(N)
    for i in range(N - 1):
        m, n, e = P // 2 - 4 * i, K // 2 - i, rng.permutation(P)
        s[a[i], e[:m]] = 1
        s[a[i], e[m:m + n]] = -1
    d["tb"] = signs(d, d["tb"], s)
    for r in range(N):
        d["tb"][r].reshape(128, P, 4)[:, np.flatnonzero(s[r] == 0)[1::2]] = BF(-0.0)
    d["nz"] = big(d["nz"].astype(np.float32) * np.repeat(rng.random((N, 1, R * K)) > 0.25, 4, axis=2))
    return d
def check_inputs(d):
    b = []
    for k, low, high in (("tb", -16, 26), ("nz", -16, 26), ("u", -30, 30), ("w", -30, 30)):
        v = np.abs(d[k].astype(np.float32))
        if not (np.isfinite(v).all() and ((v == 0) | (v >= 2.0 ** low) & (v <= 2.0 ** high)).all()): b.append("a value of " + k)
    v = d["u"].astype(np.float32)
    if (v[:, :, 4:] != 0).any(): b.append("u has numbers behind its column 0")
    if (v != v[:1]).any(): b.append("u isn't the same on all ranks")
    return b
def reference(tb, nz, u, w):
    T = [mx_ref.quantize(tb[r]) for r in range(N)]
    qu = [mx_ref.quantize(u[r]) for r in range(N)]
    od = np.zeros((N, R, N), np.float32)
    for t in range(R):
        s = [mx_ref.matmul(qu[r], T[r])[0] + np.float32(0) for r in range(N)]
        fitness = np.array([np.count_nonzero(s[r] > 0) for r in range(N)])
        place = np.argsort(-fitness, kind="stable")
        od[:, t] = place
        new = T[:]
        for i in range(N // 2):
            a, b = place[i], place[N - 1 - i]
            j = np.argsort(s[a], kind="stable")[:K]
            noise = mx_ref.quantize(np.ascontiguousarray(nz[b][:, 4 * t * K:4 * (t + 1) * K]))
            v = np.float32(0.5) * decode(pick(T[a], j)) + np.float32(0.5) * decode(noise)
            new[b] = put(T[a], j, mx_ref.quantize(np.ascontiguousarray(v.astype(BF))))
        T = new
    oc, osc, y = np.zeros((N, 128, 4 * P), np.uint8), np.zeros((N, 16, P), np.uint8), np.zeros((N, 128, O * P), np.float32)
    for r in range(N):
        oc[r], osc[r] = emit(T[r])
        for o in range(O):
            y[r, :, o * P:(o + 1) * P] = mx_ref.matmul(mx_ref.quantize(np.ascontiguousarray(cut(w[r], o))), T[r])
    return {"oc": oc, "osc": osc, "od": od, "y": y}

@@ -1,0 +1,526 @@
+from concourse.bass import DstId, RemoteDMATransfer
+from concourse.mybir import dt, AluOpType as O, AxisListType, ActivationFunctionType as F
+
+P, K, N = 192, 48, 6
+LX, HX, NX = 288, 576, 672
+BIG = 1e29
+
+SCRATCH = {"mdr": ("dram", [16, 48], "uint16")}
+ARENA = {}
+for _d, _l in (
+        ("bfloat16", "ut 4 tbt 768 nzt 704 wt 1024 ubt 512 onet 512 eht 2048 vt 512 ct 784"),
+        ("int32", "ipd 196 pi 2 pa 8 ia 196 hi 8 fb 8 hw 48"),
+        ("float32", "ir 800 m16 12 bi 48 ai 48 r16 192 x48 288 ri 96 ones 128 qf 2 cf 16 bm 192 dm 192 wm 194 wa 194 nw 12 r6 48 "
+                    "wgt 48 wgt1 48 sm 192 sm1 64 rd 194 sc 192 prm 192 pd 192 sc2 192 msgf 2 sw 584 st 192 g32 32 m32 32 sq 32 "
+                    "lrow 192 ysb 384 odt 16 pos 288 psc 288 ps 48 rho 96 qa 96 qb 96 y0 96"),
+        ("uint16", "msg 2 land 8 rw 48 l1 4 l2 4 l3 4 l4 4 rof 12 ol 12 oll 4 om 4 ox 4 ob 6 oa 6 og 2 osl 12 o32 2 oh 6 ol1 4 ofin 12")):
+    _w = _l.split()
+    for _k, _n in zip(_w[::2], _w[1::2]):
+        SCRATCH[_k] = ("sbuf", [128, int(_n)], _d)
+_w = ("tq 192 nq 176 wq 256 uq 128 oneq 128 eq 512 cq 196 ls 48 nb 192 hb 96 hp 96 hs 96 lb 128 lc 128 xs 48 w0 800 fin 192").split()
+for _k, _n in zip(_w[::2], _w[1::2]):
+    SCRATCH[_k] = ("sbuf", [128, int(_n)], "float8_e4m3fn_x4")
+    SCRATCH[_k + "_s"] = ("sbuf", [128, int(_n)], "uint8")
+for _k in range(8):
+    SCRATCH["ps%d" % _k] = ("psum", [128, 512], "float32")
+_o = 0
+for _k in "k1 k2 gg gw p1 p2 su ee ew dts od1 od2 kd b1 b2 wb hd vf tmp".split():
+    ARENA[_k] = (_o, 48)
+    _o += 48
+for _k in "y0g c1x loc".split():
+    ARENA[_k] = (_o, 96)
+    _o += 96
+for _k in "t0 base f8 t8 apre c1 hrow np hl key tk tkq i48".split():
+    ARENA[_k] = (_o, 8)
+    _o += 8
+for _k in "l16 rk fl fm".split():
+    ARENA[_k] = (_o, 16)
+    _o += 16
+SCRATCH["ar"] = ("sbuf", [128, _o], "float32")
+
+DMAS = ["du", "dtb", "dnz", "dw", "dls", "dhb", "dmd", "drw", "dxs", "dhs", "dout"]
+SEMAPHORES = ["cv", "ca", "ct", "cg", "am", "al", "ah", "ax", "a3", "left"] + DMAS
+
+
+def r(name, a=0, b=None, step=1, p=0, q=128):
+    o, n = ARENA[name] if name in ARENA else (0, SCRATCH[name][1][1])
+    return ("ar" if name in ARENA else name, p, min(q, SCRATCH[name][1][0]) if name in SCRATCH else q,
+            o + a, o + (n if b is None else b), step)
+
+
+def meet(x, y):
+    return (x[0] == y[0] and x[1] < y[2] and y[1] < x[2] and x[3] < y[4] and y[3] < x[4]
+            and not (x[5] == y[5] and (x[3] - y[3]) % x[5]))
+
+
+def covers(x, y):
+    return x[1] <= y[1] and y[2] <= x[2] and x[3] <= y[3] and y[4] <= x[4] and (x[5] == 1 or x[5] == y[5] and x[3] == y[3])
+
+
+def rank_program(g, core, T, topo):
+    me = T.rank_of(core)
+    if me is None:
+        return
+    queue = {"v": g.vector, "a": g.scalar, "t": g.tensor, "g": g, "s": g.sync}
+    V, A, X = g.vector, g.scalar, g.tensor
+    count = {"v": 0, "a": 0, "t": 0, "g": 0}
+    clk = {q: {} for q in queue}
+    snap, wr, rd, due = {}, {}, {}, {}
+
+    def wait(q, s, v):
+        if clk[q].get(s, 0) < v:
+            queue[q].wait_ge(T.sem[s], v)
+            for s2, v2 in snap.get((s, v), {}).items():
+                clk[q][s2] = max(clk[q].get(s2, 0), v2)
+            clk[q][s] = v
+
+    def before(q, reads, writes):
+        need = {}
+        for x in reads + writes:
+            hits = list(wr.get(x[0], ()))
+            if x in writes or SCRATCH[x[0]][0] == "psum" if x[0] in SCRATCH else False:
+                hits += rd.get(x[0], ())
+            for y, tok in hits:
+                bank = x[0] in SCRATCH and SCRATCH[x[0]][0] == "psum"
+                if meet(x, y) or bank and tok[0] != "c" + q:
+                    need[tok[0]] = max(need.get(tok[0], 0), tok[1])
+        for s in sorted(need):
+            wait(q, s, need[s])
+
+    def wrote(x, tok):
+        for d in (wr, rd):
+            d[x[0]] = [e for e in d.get(x[0], ()) if not covers(x, e[0])]
+        wr[x[0]].append((x, tok))
+
+    def issue(q, reads, writes, fn, sem=None, total=0):
+        before(q, reads, writes)
+        if sem is None:
+            count[q] += 1
+            tok = ("c" + q, count[q])
+            fn().then_inc(T.sem[tok[0]], 1)
+            snap[tok] = dict(clk[q])
+        else:
+            tok = (sem, total)
+            fn().then_inc(T.sem[sem], 16)
+            due[sem] = total
+        for x in reads:
+            rd.setdefault(x[0], []).append((x, tok))
+        for x in writes:
+            wrote(x, tok)
+
+    def ap(x, bits=None):
+        v = T[x[0]][x[1]:x[2], x[3]:x[4]:x[5]] if x[5] > 1 else T[x[0]][x[1]:x[2], x[3]:x[4]]
+        return v.bitcast(bits or dt.uint8) if x[0] in SCRATCH and SCRATCH[x[0]][2] == "float8_e4m3fn_x4" else v
+
+    def mx(x):
+        return T[x[0]][:, x[3]:x[4]]
+
+    def num(s):
+        return ap(s) if isinstance(s, tuple) else s
+
+    def ts(out, in0, s1, op0, s2=None, op1=None):
+        rs = [in0] + [s for s in (s1, s2) if isinstance(s, tuple)]
+        if op1 is None:
+            issue("v", rs, [out], lambda: V.tensor_scalar(ap(out), ap(in0), num(s1), None, op0))
+        else:
+            issue("v", rs, [out], lambda: V.tensor_scalar(ap(out), ap(in0), num(s1), num(s2), op0, op1))
+
+    def tt(out, a, b, op):
+        issue("v", [a, b], [out], lambda: V.tensor_tensor(ap(out), ap(a), ap(b), op))
+
+    def cp(out, in_):
+        issue("v", [in_], [out], lambda: V.tensor_copy(ap(out), ap(in_)))
+
+    def ac(out, in_):
+        issue("a", [in_], [out], lambda: A.activation(ap(out), ap(in_), F.Copy))
+
+    def gather(out, win, off):
+        issue("v", [win, off], [out], lambda: V.tensor_copy(ap(out), ap(win).indirect(ap(off))))
+
+    def scan(out, keep, add):
+        issue("v", [keep, add], [out], lambda: V.tensor_tensor_scan(ap(out), ap(keep), ap(add), 0.0, O.mult, O.add))
+
+    def fill(x, c):
+        issue("v", [], [x], lambda: V.memset(ap(x), c))
+
+    def both(name, a, b):
+        return [r(name, a, b), r(name + "_s", a, b)]
+
+    def qz(cod, o, n, tile):
+        c, s = both(cod, o, o + n)
+        issue("v", [tile], [c, s], lambda: V.quantize_mx(mx(c), mx(s), ap(tile)))
+
+    def mm(k, lhs, lo, rhs, ro, n, start=True, stop=True):
+        w, x, out = both(lhs, lo, lo + 128), both(rhs, ro, ro + n), r("ps%d" % k, 0, n)
+        issue("t", w + x, [out], lambda: X.matmul_mx(ap(out), mx(w[0]), mx(w[1]), mx(x[0]), mx(x[1]), start, stop))
+
+    def pick(dst, c, n, src, a, b, off, parts):
+        do, so, wc, ws = r(dst, c, c + n), r(dst + "_s", c, c + n), r(src, a, b), r(src + "_s", a, b)
+        issue("v", [r(src, x, y) for x, y in parts] + [off], [do], lambda: V.tensor_copy(
+            ap(do, dt.uint32), ap(wc, dt.uint32).indirect(ap(off))))
+        issue("a", [r(src + "_s", x, y) for x, y in parts] + [off], [so], lambda: A.activation(
+            ap(so), ap(ws).indirect(ap(off)), F.Copy))
+
+    def iota(x, pattern, base, cm):
+        if SCRATCH[x[0]][2] == "int32":
+            issue("g", [], [x], lambda: g.iota(ap(x), pattern, base, cm))
+        else:
+            issue("g", [], [x], lambda: g.iota(ap(x), pattern, base, cm, allow_small_or_imprecise_dtypes=True))
+
+    def dma(q, out, in_, sem, total=16):
+        issue(q, [in_] if isinstance(in_, tuple) else [], [out] if isinstance(out, tuple) else [],
+              lambda: queue[q].dma_start(num(out), num(in_)), sem, total)
+
+    def move(dst, a, src, b, n, sem):
+        for x, y in zip(both(dst, a, a + n), both(src, b, b + n)):
+            dma("s", x, y, sem, 32)
+
+    others = [x for x in range(N) if x != me]
+
+    def far_of(x):
+        return [y for y in range(N) if topo.chip(T.cores[y]) != topo.chip(T.cores[x])]
+    far = far_of(me)
+    near = [x for x in others if x not in far]
+    out_eng = topo.engines(core, T.cores[far[0]])
+    in_eng = [e for e in topo.engines(core, T.cores[near[0]]) if e not in out_eng]
+
+    def mask(es):
+        return sum(1 << e for e in es)
+
+    def dst(x):
+        a = topo.addr(T.cores[x])
+        return DstId(rid=a[0], pnc=a[1])
+
+    def send(transfers, src):
+        before("g", [src], [])
+        for x, es, s, to in transfers:
+            due["left"] = due.get("left", 0) + len(es)
+        return [RemoteDMATransfer(dst_ids=[dst(y) for y in x], dma_engine_mask=mask(es), remote_sem=T.sem[sem_of[0]],
+                                  srcs=[ap(s)], dsts=[ap(to)] * len(x)) for x, es, s, to in transfers]
+    sem_of = [None]
+
+    def spread(src, to, sem):
+        sem_of[0] = sem
+        g.remote_dma_fused(send([(far, out_eng, src, to), (near, in_eng, src, to)], src), local_sem=T.sem["left"])
+
+    half = len(in_eng) // 2
+
+    def far_share(x, y):
+        k = far_of(x).index(y)
+        n = [4 if j == x % 3 else 2 for j in range(3)]
+        return sum(n[:k]), n[k]
+
+    def share(y):
+        if y in near:
+            k = near.index(y)
+            return in_eng[half * k:half * k + half]
+        a, n = far_share(me, y)
+        return out_eng[a:a + n]
+
+    def pieces(name, to, sem):
+        sem_of[0] = sem
+        g.remote_dma_fused(send([([y], share(y), r(name, 16 * y, 16 * y + 16), to) for y in others], r(name)),
+                           local_sem=T.sem["left"])
+
+    n_all = sum(len(out_eng) if x in far else len(in_eng) for x in others)
+    n_pcs = sum(half if x in near else far_share(x, me)[1] for x in others)
+    for sem, tot, buf, base, w in (("al", 2 * n_all, "w0", 0, K), ("ax", 2 * n_all, "w0", LX, K), ("ah", 2 * n_pcs, "hp", 0, 16),
+                                   ("a3", 2 * n_pcs, "w0", HX, 16)):
+        due[sem] = tot
+        for x in others:
+            for e in both(buf, base + w * x, base + w * x + w):
+                wrote(e, (sem, tot))
+    due["am"] = n_all
+    for x in others:
+        wrote(r("land", x, x + 1), ("am", n_all))
+
+    dma("a", r("tbt"), T.tb[:, :], "dtb")
+    dma("s", r("ut"), T.u[:, 0:4], "du")
+    dma("s", r("nzt", 0, 384), T.nz[:, :], "dnz")
+    dma("s", r("wt"), T.w[:, :], "dw")
+
+    iota(r("pi"), [[0, 2]], 0, 1)
+    iota(r("ipd"), [[1, 196]], 0, -1)
+    iota(r("r16"), [[0, 12], [1, 16]], 0, 0)
+    iota(r("ir", 0, 196), [[1, 196]], 0, 0)
+    fill(r("ones"), 1.0)
+    fill(r("onet"), 1.0)
+    fill(r("ct"), 0.0)
+    qz("oneq", 0, 128, r("onet"))
+    ts(r("bm"), r("ipd", 0, 192), 0.0, O.is_le, 3e29, O.mult)
+    for k in range(4):
+        ts(r("ubt", k, 512, 4), r("ones"), r("ut", k, k + 1), O.mult)
+    qz("uq", 0, 128, r("ubt"))
+    ts(r("ia"), r("ipd"), 15, O.bitwise_and)
+    ts(r("dm"), r("ia", 0, 192), 0.0, O.is_equal)
+    ts(r("r16"), r("r16"), 0.0, O.is_gt)
+
+    qz("tq", 0, 192, r("tbt"))
+    mm(1, "tq", 0, "uq", 0, 128)
+    mm(0, "uq", 0, "tq", 0, 192)
+    mm(2, "tq", 64, "uq", 0, 128)
+    ts(r("pa", 0, 2), r("pi"), 3, O.arith_shift_right)
+    ts(r("pa", 2, 4), r("pi"), 7, O.bitwise_and)
+    ts(r("pa", 4, 6), r("pi"), 15, O.bitwise_and)
+    cp(r("cf", 2, 4), r("pa", 0, 2))
+    ts(r("cf", 4, 6), r("pa", 2, 4), 16.0, O.mult, r("cf", 2, 3), O.add)
+    ts(r("cf", 6, 8), r("pa", 2, 4), 4.0, O.is_ge)
+    ts(r("cf", 10, 12), r("cf", 4, 6), -128.0, O.add, r("cf", 6, 7), O.mult)
+    ts(r("cf", 12, 14), r("cf", 10, 12), 192.0, O.add)
+    cp(r("qf"), r("pa", 4, 6))
+
+    def sort(src, sp0, sp1, n):
+        def lower(x, a=0, b=192):
+            return r(x[0], a, b, 1, 64, 128)
+        ts(r("ct", 0, 768, 4), src, sp0, O.is_gt)
+        tt(r("sm"), src, r("bm"), O.add)
+        tt(r("sm1", 0, 64, 1, 64), lower(src, 128), r("bm", 64, 128, 1, 64), O.add)
+        ts(r("ct", 1, 768, 4, 64), lower(src), sp1, O.is_gt)
+        ts(r("ct", 2, 768, 4), r("sm"), sp0, O.is_equal)
+        ts(r("ct", 515, 768, 4, 64), r("sm1", 0, 64, 1, 64), sp1, O.is_equal)
+        if n > 192:
+            ts(r("ct", 768, 769), sp0, 0.0, O.is_gt)
+            ts(r("ct", 769, 770, 1, 64), sp1, 0.0, O.is_gt)
+        qz("cq", 0, n, r("ct", 0, 4 * n))
+        mm(3, "oneq", 0, "cq", 0, n)
+
+    def ranks():
+        tt(r("rd", 0, 192), r("ps3", 0, 192), r("dm"), O.mult)
+        scan(r("sc"), r("r16"), r("rd", 0, 192))
+        cp(r("rof"), r("sc", 15, 192, 16))
+
+    def scatter(val):
+        issue("v", [val, r("rof")], [r("prm")], lambda: V.tensor_copy(ap(r("prm")).indirect(ap(r("rof"))), ap(val)))
+
+    def order(out, a, b):
+        tt(r("pd", a, b), r("prm", a, b), r("dm", a, b), O.mult)
+        scan(r("sc2", a, b), r("r16", a, b), r("pd", a, b))
+        cp(out, r("sc2", a + 15, b, 16))
+
+    sort(r("ps0", 0, 192), r("ps1", 0, 1), r("ps2", 0, 1, 1, 64), 194)
+    ts(r("wa"), r("ir", 0, 194), r("cf", 12, 13), O.is_equal, 256.0, O.mult)
+    ts(r("wm"), r("ir", 0, 194), r("cf", 4, 5), O.is_equal)
+    tt(r("wm"), r("wm"), r("wa"), O.add)
+    tt(r("rd"), r("ps3", 0, 194), r("wm"), O.mult)
+    issue("v", [r("rd")], [r("msgf", 0, 1)], lambda: V.tensor_reduce(ap(r("msgf", 0, 1)), ap(r("rd")), AxisListType.X, O.add))
+    cp(r("msg", 0, 1), r("msgf", 0, 1))
+    spread(r("msg", 0, 1), r("land", me, me + 1), "am")
+    ranks()
+    scatter(r("ir", 0, 192))
+    order(r("ol", 0, 3), 0, 48)
+    pick("ls", 0, 48, "tq", 0, 192, r("ol", 0, 3), [(0, 192)])
+    for x, y in zip(both("ls", 0, K), both("w0", K * me, K * me + K)):
+        spread(x, y, "al")
+    move("w0", K * me, "ls", 0, K, "dls")
+    order(r("ol", 6, 12), 96, 192)
+    pick("hb", 0, 96, "tq", 0, 192, r("ol", 6, 12), [(0, 192)])
+    for x, y in zip(("hb", "hb_s"), both("hp", 16 * me, 16 * me + 16)):
+        pieces(x, y, "ah")
+    move("hp", 16 * me, "hb", 16 * me, 16, "dhb")
+    order(r("om", 0, 3), 48, 96)
+    pick("nb", 0, 48, "tq", 0, 192, r("om", 0, 3), [(0, 192)])
+
+    iota(r("m16"), [[16, 12]], 0, 0)
+    iota(r("bi"), [[0, 8], [1, 6]], 0, 0)
+    iota(r("ai"), [[1, 8], [0, 6]], 0, 0)
+    ts(r("nw"), r("m16"), r("qf", 0, 1), O.add)
+    ts(r("hi", 0, 3), r("nw", 0, 3), 1.0 / 6, O.mult, -2.5 / 6, O.add)
+    ts(r("l2", 0, 3), r("hi", 0, 3), 1.0, O.mult)
+    ts(r("l4", 0, 3), r("hi", 0, 3), 6.0, O.mult, 5.0, O.add)
+    ts(r("wa", 0, 3), r("hi", 0, 3), -6.0, O.mult)
+    tt(r("wa", 4, 7), r("wa", 0, 3), r("nw", 0, 3), O.add)
+    ts(r("l1", 0, 3), r("wa", 4, 7), 1.0, O.mult)
+    ts(r("l3", 0, 3), r("wa", 4, 7), 6.0, O.mult, 5.0, O.add)
+    ts(r("r6"), r("bi"), 0.0, O.is_gt)
+    tt(r("wgt1"), r("bi"), r("ai"), O.subtract)
+    ts(r("wgt"), r("wgt1"), 48.0, O.mult)
+    ts(r("wgt1"), r("wgt1"), 16.0, O.mult)
+    for x in ("key", "ps", "c1", "base"):
+        fill(r(x), 0.0)
+    fill(r("vt"), 0.0)
+    fill(r("eht"), 0.0)
+    for k in range(4):
+        ts(r("eht", 513 * k, 512 * k + 512, 4), r("ipd", 0, 128), 0.0, O.is_equal, 0.5, O.mult)
+    qz("eq", 0, 512, r("eht"))
+    fill(r("nzt", 384, 704), 0.0)
+    qz("nq", 0, 176, r("nzt"))
+    qz("lb", 0, 128, r("vt"))
+    qz("lc", 0, 128, r("vt"))
+
+    def noise(t):
+        for k in range(4):
+            mm(4 + k, "eq", 128 * k, "nq", K * t, 128, True, False)
+    noise(0)
+
+    def places(w):
+        gather(r("k1"), r("key"), r("l1", 0, 3))
+        gather(r("k2"), r("key"), r("l2", 0, 3))
+        tt(r("gg", 0, 36), r("k1", 0, 36), r("k2", 0, 36), O.is_gt)
+        scan(r("ps", 0, 36), r("r6", 0, 36), r("gg", 0, 36))
+        gather(r("p1"), r("ps"), r("l3", 0, 3))
+        gather(r("p2"), r("ps"), r("l4", 0, 3))
+        tt(r("gw", 0, 36), r("gg", 0, 36), r(w, 0, 36), O.mult)
+        tt(r("su", 0, 36), r("p1", 0, 36), r("p2", 0, 36), O.add)
+        ts(r("ee", 0, 36), r("su", 0, 36), 5.0, O.is_equal)
+        tt(r("ew", 0, 36), r("ee", 0, 36), r("gw", 0, 36), O.mult)
+        scan(r("dts", 0, 36), r("r6", 0, 36), r("ew", 0, 36))
+
+    def note(k):
+        tt(r("od1", 0, 36), r("p1", 0, 36), r("ai", 0, 36), O.is_equal)
+        tt(r("od2", 0, 36), r("od1", 0, 36), r("bi", 0, 36), O.mult)
+        scan(r("od1", 0, 36), r("r6", 0, 36), r("od2", 0, 36))
+        cp(r("odt", 6 * k, 6 * k + 6), r("od1", 5, 36, 6))
+
+    own = 6 * me + 5
+    my_dts, my_ps = r("dts", own, own + 1), r("ps", own, own + 1)
+
+    def anew(buf, off, parts, end, out, o):
+        pick(buf, 0, 48, "w0", 0, end, off, parts)
+        for k in range(4):
+            mm(4 + k, "eq", 128 * k, buf, 0, 128, False, True)
+
+    def pack(out, o):
+        for k in range(4):
+            (cp if k % 2 == 0 else ac)(r("vt", k, 192, 4), r("ps%d" % (4 + k), 0, 48))
+        qz(out, o, 128, r("vt"))
+
+    fill(r("i48"), float(K * me))
+    wait("v", "am", n_all)
+    cp(r("land", me, me + 1), r("msgf", 0, 1))
+    ts(r("hi", 0, 6), r("land", 0, 6), 1.0 / 256, O.mult, -127.5 / 256, O.add)
+    issue("g", [r("hi", 0, 6)], [r("fb", 0, 6)], lambda: g.partition_broadcast(
+        ap(r("fb", 0, 6)), ap(r("hi", 0, 6, 1, 0, 1)), 128))
+    ts(r("tmp", 0, 6), r("fb", 0, 6), 8.0, O.mult)
+    tt(r("key", 0, 6), r("tmp", 0, 6), r("ir", 0, 6), O.subtract)
+    places("wgt")
+    ts(r("oll", 0, 3), r("nw", 0, 3), my_dts, O.add, r("i48", 0, 1), O.add)
+
+    dma("s", ("mdr", 0, 16, 0, 48, 1), r("land", 0, 6), "dmd")
+    for k in range(8):
+        dma("s", r("rw", 0, 48, 1, 16 * k, 16 * k + 16), ("mdr", 0, 16, 0, 48, 1), "drw", 128)
+
+    anew("lb", r("oll", 0, 3), [(0, 288)], 288, "nb", 64)
+    ts(r("tk", 0, 1), my_ps, 3.0, O.is_ge, 64.0, O.mult)
+    ts(r("ox", 0, 3), r("nw", 0, 3), r("tk", 0, 1), O.add)
+    pack("nb", 64)
+    pick("xs", 0, 48, "nb", 0, 192, r("ox", 0, 3), [(0, 48), (64, 192)])
+    for x, y in zip(both("xs", 0, K), both("w0", LX + K * me, LX + K * me + K)):
+        spread(x, y, "ax")
+    move("w0", LX + K * me, "xs", 0, K, "dxs")
+    iota(r("ir", 196, 800), [[1, 604]], 196, 0)
+    iota(r("x48"), [[0, 6], [1, 48]], 0, 0)
+    iota(r("ri"), [[0, 16], [1, 6]], 0, 0)
+    noise(1)
+    mm(1, "uq", 0, "w0", 0, 288)
+    ac(r("sw", 0, 288), r("ps1", 0, 288))
+
+    six = (0, 6)
+    ts(r("x48"), r("x48"), 0.0, O.is_gt)
+    ts(r("t0", *six), r("ps", 5, 36, 6), 3.0, O.is_ge)
+    ts(r("tmp", *six), r("dts", 5, 36, 6), 1.0 / 48, O.mult)
+    tt(r("hi", *six), r("tmp", *six), r("ir", *six), O.add)
+    cp(r("base", *six), r("hi", *six))
+    tt(r("kd", 0, 36), r("k1", 0, 36), r("k2", 0, 36), O.subtract)
+    tt(r("tmp", 0, 36), r("ee", 0, 36), r("gg", 0, 36), O.mult)
+    tt(r("kd", 0, 36), r("kd", 0, 36), r("tmp", 0, 36), O.mult)
+    scan(r("tmp", 0, 36), r("r6", 0, 36), r("kd", 0, 36))
+    tt(r("f8", *six), r("tmp", 5, 36, 6), r("key", *six), O.add)
+    tt(r("f8", *six), r("f8", *six), r("base", *six), O.add)
+    ts(r("apre", *six), r("f8", *six), float(-8 * (P - K)), O.add, 0.0, O.max)
+    tt(r("apre", *six), r("apre", *six), r("t0", *six), O.mult)
+    tt(r("apre", *six), r("f8", *six), r("apre", *six), O.subtract)
+    tt(r("apre", *six), r("apre", *six), r("ir", *six), O.subtract)
+    ts(r("t8", *six), r("t0", *six), 8.0, O.mult)
+    ts(r("c1", *six), r("t0", *six), float(LX), O.mult)
+    ts(r("f8", *six), r("ir", *six), float(K), O.mult)
+    tt(r("c1", *six), r("c1", *six), r("f8", *six), O.add)
+    gather(r("b1"), r("base"), r("l1", 0, 3))
+    gather(r("b2"), r("base"), r("l2", 0, 3))
+    tt(r("wb"), r("b1"), r("b2"), O.subtract)
+    ts(r("wb"), r("wb"), 16.0, O.mult)
+    ts(r("hrow", *six), r("base", *six), 16.0, O.mult, r("qf", 0, 1), O.add)
+    ts(r("tkq", 0, 1), r("qf", 0, 1), 6.0, O.mult)
+    ts(r("tkq", 1, 2), r("qf", 0, 1), float(16 * me), O.add)
+    ts(r("ob"), r("base", *six), r("tkq", 0, 1), O.add)
+    ts(r("oa"), r("ir", *six), 1.0, O.mult)
+    note(0)
+    fill(r("sw", 576, 584), BIG)
+    ts(r("cf", 14, 16), r("pi"), 64.0, O.is_ge, 64.0, O.mult)
+    ts(r("o32", 0, 1), r("pi", 0, 1), 1.0, O.mult)
+    ts(r("o32", 1, 2), r("pi", 0, 1), r("cf", 14, 15), O.add)
+    ts(r("qa"), r("ri"), 48.0, O.mult, 240.0, O.add)
+    ts(r("qb"), r("qa"), -1.0, O.mult, 480.0, O.add)
+    qz("wq", 0, 256, r("wt"))
+    fill(r("rho"), 0.0)
+    cp(r("vf"), r("rw"))
+    ts(r("hw"), r("rw"), 1.0 / 256, O.mult, -127.5 / 256, O.add)
+    ts(r("y0", 0, 48), r("hw"), -256.0, O.mult)
+    tt(r("rho", 0, 48), r("y0", 0, 48), r("vf"), O.add)
+    cp(r("rho", 48, 72), r("hw", 24, 48))
+    ts(r("y0"), r("rho"), 48.0, O.is_ge)
+    tt(r("y0"), r("y0"), r("qa"), O.mult)
+    ts(r("y0g"), r("rho"), 96.0, O.is_ge)
+    tt(r("y0g"), r("y0g"), r("qb"), O.mult)
+    tt(r("y0"), r("y0"), r("y0g"), O.add)
+    tt(r("y0"), r("y0"), r("rho"), O.add)
+    gather(r("y0g"), r("y0"), r("ob"))
+    gather(r("c1x"), r("c1"), r("oa"))
+    ts(r("loc"), r("y0g"), 48.0, O.is_lt)
+    tt(r("loc"), r("loc"), r("c1x"), O.mult)
+    tt(r("loc"), r("loc"), r("y0g"), O.add)
+
+    mm(0, "uq", 0, "w0", LX, 288)
+    ts(r("pos"), r("ps0", 0, 288), 0.0, O.is_gt)
+    ac(r("sw", 288, 576), r("ps0", 0, 288))
+    scan(r("psc"), r("x48"), r("pos"))
+    tt(r("np", *six), r("psc", 47, 288, 48), r("t8", *six), O.mult)
+    tt(r("key", *six), r("np", *six), r("apre", *six), O.add)
+    places("wgt1")
+    ts(r("og", 0, 1), r("tkq", 1, 2), my_dts, O.add)
+    gather(r("l16"), r("loc"), r("og", 0, 1))
+    ts(r("osl"), r("l16", 0, 12), float(HX), O.min)
+    issue("a", [r("ir"), r("osl")], [r("lrow")], lambda: A.activation(ap(r("lrow")), ap(r("ir")).indirect(ap(r("osl"))), F.Copy))
+    tt(r("gw", 0, 36), r("gg", 0, 36), r("wb", 0, 36), O.mult)
+    tt(r("ew", 0, 36), r("ee", 0, 36), r("gw", 0, 36), O.mult)
+    scan(r("hd", 0, 36), r("r6", 0, 36), r("ew", 0, 36))
+    tt(r("hl", *six), r("hd", 5, 36, 6), r("hrow", *six), O.add)
+    cp(r("oh"), r("hl", *six))
+    pick("hs", 0, 96, "hp", 0, 96, r("oh"), [(0, 96)])
+    for x, y in zip(("hs", "hs_s"), both("w0", HX + 16 * me, HX + 16 * me + 16)):
+        pieces(x, y, "a3")
+    move("w0", HX + 16 * me, "hs", 16 * me, 16, "dhs")
+    gather(r("st"), r("sw"), r("osl"))
+    gather(r("g32"), r("st"), r("o32"))
+    tt(r("m32"), r("g32"), r("dm", 0, 32), O.mult)
+    scan(r("sq"), r("r16", 0, 32), r("m32"))
+    sort(r("st"), r("sq", 15, 16), r("sq", 31, 32, 1, 64), 192)
+    ranks()
+    scatter(r("lrow"))
+    order(r("ol1", 0, 3), 0, 48)
+    anew("lc", r("ol1", 0, 3), [(0, 576)], 576, "w0", NX)
+    ts(r("tk", 0, 1), my_dts, 0.0, O.not_equal)
+    ts(r("fm", 0, 12), r("sc", 15, 192, 16), 48.0, O.is_lt, r("tk", 0, 1), O.mult)
+    ts(r("rk", 0, 12), r("sc", 15, 192, 16), float(NX), O.add)
+    tt(r("rk", 0, 12), r("rk", 0, 12), r("l16", 0, 12), O.subtract)
+    tt(r("rk", 0, 12), r("rk", 0, 12), r("fm", 0, 12), O.mult)
+    tt(r("fl", 0, 12), r("rk", 0, 12), r("l16", 0, 12), O.add)
+    cp(r("ofin"), r("fl", 0, 12))
+    pack("w0", NX)
+    pick("fin", 0, 192, "w0", 0, 800, r("ofin"), [(0, 800)])
+
+    dma("s", T.oc[:, :], r("fin"), "dout", 128)
+    mm(1, "wq", 0, "fin", 0, 192)
+    mm(2, "wq", 128, "fin", 0, 192)
+    for k in range(4):
+        dma("s" if k < 2 else "a", T.osc[4 * k:4 * k + 4, :], r("fin_s", 0, 192, 1, 32 * k, 32 * k + 4), "dout", 128)
+    cp(r("ysb", 0, 192), r("ps1", 0, 192))
+    dma("s", T.y[:, 0:192], r("ysb", 0, 192), "dout", 128)
+    ac(r("ysb", 192, 384), r("ps2", 0, 192))
+    dma("a", T.y[:, 192:384], r("ysb", 192, 384), "dout", 128)
+    note(1)
+    dma("s", T.od[:, :], r("odt", 0, 12, 1, 0, 1), "dout", 128)
+
+    for q in count:
+        due["c" + q] = count[q]
+    for s in sorted(due):
+        g.wait_ge(T.sem[s], due[s])

@@ -1,19 +1,21 @@
 from concourse.bass import DstId, RemoteDMATransfer
-from concourse.mybir import dt, AluOpType as O, AxisListType, ActivationFunctionType as F
+from concourse.mybir import dt, AluOpType as O, ActivationFunctionType as F
 
 P, K, N = 192, 48, 6
 LX, HX, NX = 288, 576, 672
 BIG = 1e29
+WHOLE = 12582912.0
 
 SCRATCH = {"mdr": ("dram", [16, 48], "uint16")}
 ARENA = {}
 for _d, _l in (
-        ("bfloat16", "ut 4 tbt 768 nzt 704 wt 1024 ubt 512 onet 512 eht 2048 vt 512 ct 784"),
-        ("int32", "ipd 196 pi 2 pa 8 ia 196 hi 8 fb 8 hw 48"),
-        ("float32", "ir 800 m16 12 bi 48 ai 48 r16 192 x48 288 ri 96 ones 128 qf 2 cf 16 bm 192 dm 192 wm 194 wa 194 nw 12 r6 48 "
-                    "wgt 48 wgt1 48 sm 192 sm1 64 rd 194 sc 192 prm 192 pd 192 sc2 192 msgf 2 sw 584 st 192 g32 32 m32 32 sq 32 "
-                    "lrow 192 ysb 384 odt 16 pos 288 psc 288 ps 48 rho 96 qa 96 qb 96 y0 96"),
-        ("uint16", "msg 2 land 8 rw 48 l1 4 l2 4 l3 4 l4 4 rof 12 ol 12 oll 4 om 4 ox 4 ob 6 oa 6 og 2 osl 12 o32 2 oh 6 ol1 4 ofin 12")):
+        ("bfloat16", "ut 4 tbt 768 nzt 704 wt 1024 ubt 512 onet 512 eht 2048 vt 512 ct 784 idt 128"),
+        ("int32", "ipd 196 pi 2 pa 12 ia 196 hi 8 fb 8"),
+        ("float32", "ir 800 m16 4 lf 24 bi 48 ai 48 r8k 48 r16 192 x48 288 ones 128 paf 12 cf 16 bm 192 dm 192 wm 194 wa 194 nw 4 "
+                    "r8 48 rsq 32 wgt 48 wgt1 48 th 48 c48 8 sm 192 sm1 64 rd 192 rdm 194 junk 194 sc 192 prm 192 pd 192 sc2 192 "
+                    "msgf 2 sw 584 st 192 g32 32 m32 32 sq 32 lrow 192 ysb 384 odt 16 pos 288 psc 288 ps 64 rho 96 qa 96 qb 96 "
+                    "y0 96"),
+        ("uint16", "land 48 v6 8 rw 48 lists 24 rof 12 ol 12 oll 4 om 4 ox 4 ob 6 og 2 osl 12 oh 6 ol1 4 ofin 12")):
     _w = _l.split()
     for _k, _n in zip(_w[::2], _w[1::2]):
         SCRATCH[_k] = ("sbuf", [128, int(_n)], _d)
@@ -24,28 +26,20 @@ for _k, _n in zip(_w[::2], _w[1::2]):
 for _k in range(8):
     SCRATCH["ps%d" % _k] = ("psum", [128, 512], "float32")
 _o = 0
-for _k in "k1 k2 gg gw p1 p2 su ee ew dts od1 od2 kd b1 b2 wb hd vf tmp".split():
-    ARENA[_k] = (_o, 48)
-    _o += 48
-for _k in "y0g c1x loc".split():
-    ARENA[_k] = (_o, 96)
-    _o += 96
-for _k in "t0 base f8 t8 apre c1 hrow np hl key tk tkq i48".split():
-    ARENA[_k] = (_o, 8)
-    _o += 8
-for _k in "l16 rk fl fm".split():
-    ARENA[_k] = (_o, 16)
-    _o += 16
+for _n, _l in ((48, "k1 k2 dd gg gw p1 p2 su ee ew dts od1 od2 kd fs b1 b2 wb hd vf hf h2"), (96, "y0g c1x lt s1 s2"),
+               (8, "t0 bt base fn mx t8 apre c1 hrow np hl key tk tkq i48"), (16, "l16 rk fl fm")):
+    for _k in _l.split():
+        ARENA[_k] = (_o, _n)
+        _o += _n
 SCRATCH["ar"] = ("sbuf", [128, _o], "float32")
 
-DMAS = ["du", "dtb", "dnz", "dw", "dls", "dhb", "dmd", "drw", "dxs", "dhs", "dout"]
+DMAS = ["du", "dtb", "dnz", "dw", "dpv", "dpad", "dls", "dhb", "dmd", "drw", "dxs", "dhs", "dout"]
 SEMAPHORES = ["cv", "ca", "ct", "cg", "am", "al", "ah", "ax", "a3", "left"] + DMAS
 
 
 def r(name, a=0, b=None, step=1, p=0, q=128):
     o, n = ARENA[name] if name in ARENA else (0, SCRATCH[name][1][1])
-    return ("ar" if name in ARENA else name, p, min(q, SCRATCH[name][1][0]) if name in SCRATCH else q,
-            o + a, o + (n if b is None else b), step)
+    return ("ar" if name in ARENA else name, p, q, o + a, o + (n if b is None else b), step)
 
 
 def meet(x, y):
@@ -55,6 +49,13 @@ def meet(x, y):
 
 def covers(x, y):
     return x[1] <= y[1] and y[2] <= x[2] and x[3] <= y[3] and y[4] <= x[4] and (x[5] == 1 or x[5] == y[5] and x[3] == y[3])
+
+
+def weave(*chains):
+    for k in range(max(len(c) for c in chains)):
+        for c in chains:
+            if k < len(c):
+                c[k]()
 
 
 def rank_program(g, core, T, topo):
@@ -77,11 +78,11 @@ def rank_program(g, core, T, topo):
     def before(q, reads, writes):
         need = {}
         for x in reads + writes:
+            bank = SCRATCH[x[0]][0] == "psum"
             hits = list(wr.get(x[0], ()))
-            if x in writes or SCRATCH[x[0]][0] == "psum" if x[0] in SCRATCH else False:
+            if bank or x in writes:
                 hits += rd.get(x[0], ())
             for y, tok in hits:
-                bank = x[0] in SCRATCH and SCRATCH[x[0]][0] == "psum"
                 if meet(x, y) or bank and tok[0] != "c" + q:
                     need[tok[0]] = max(need.get(tok[0], 0), tok[1])
         for s in sorted(need):
@@ -110,7 +111,7 @@ def rank_program(g, core, T, topo):
 
     def ap(x, bits=None):
         v = T[x[0]][x[1]:x[2], x[3]:x[4]:x[5]] if x[5] > 1 else T[x[0]][x[1]:x[2], x[3]:x[4]]
-        return v.bitcast(bits or dt.uint8) if x[0] in SCRATCH and SCRATCH[x[0]][2] == "float8_e4m3fn_x4" else v
+        return v.bitcast(bits or dt.uint8) if SCRATCH[x[0]][2] == "float8_e4m3fn_x4" else v
 
     def mx(x):
         return T[x[0]][:, x[3]:x[4]]
@@ -134,14 +135,21 @@ def rank_program(g, core, T, topo):
     def ac(out, in_):
         issue("a", [in_], [out], lambda: A.activation(ap(out), ap(in_), F.Copy))
 
+    def lin(out, in_, scale, bias, func=F.Identity):
+        rs = [in_] + ([bias] if isinstance(bias, tuple) else [])
+        issue("a", rs, [out], lambda: A.activation(ap(out), ap(in_), func, bias=num(bias), scale=scale))
+
     def gather(out, win, off):
         issue("v", [win, off], [out], lambda: V.tensor_copy(ap(out), ap(win).indirect(ap(off))))
 
-    def scan(out, keep, add):
-        issue("v", [keep, add], [out], lambda: V.tensor_tensor_scan(ap(out), ap(keep), ap(add), 0.0, O.mult, O.add))
+    def scan(out, keep, add, op0=O.min):
+        issue("v", [keep, add], [out], lambda: V.tensor_tensor_scan(ap(out), ap(keep), ap(add), 0.0, op0, O.add))
 
     def fill(x, c):
         issue("v", [], [x], lambda: V.memset(ap(x), c))
+
+    def zero(x, src):
+        lin(x, src, 0.0, 0.0)
 
     def both(name, a, b):
         return [r(name, a, b), r(name + "_s", a, b)]
@@ -171,9 +179,9 @@ def rank_program(g, core, T, topo):
         issue(q, [in_] if isinstance(in_, tuple) else [], [out] if isinstance(out, tuple) else [],
               lambda: queue[q].dma_start(num(out), num(in_)), sem, total)
 
-    def move(dst, a, src, b, n, sem):
+    def move(dst, a, src, b, n, sem, total=32):
         for x, y in zip(both(dst, a, a + n), both(src, b, b + n)):
-            dma("s", x, y, sem, 32)
+            dma("s", x, y, sem, total)
 
     others = [x for x in range(N) if x != me]
 
@@ -191,17 +199,15 @@ def rank_program(g, core, T, topo):
         a = topo.addr(T.cores[x])
         return DstId(rid=a[0], pnc=a[1])
 
-    def send(transfers, src):
+    def send(transfers, src, sem):
         before("g", [src], [])
-        for x, es, s, to in transfers:
-            due["left"] = due.get("left", 0) + len(es)
-        return [RemoteDMATransfer(dst_ids=[dst(y) for y in x], dma_engine_mask=mask(es), remote_sem=T.sem[sem_of[0]],
-                                  srcs=[ap(s)], dsts=[ap(to)] * len(x)) for x, es, s, to in transfers]
-    sem_of = [None]
+        due["left"] = due.get("left", 0) + sum(len(e[1]) for e in transfers)
+        g.remote_dma_fused([RemoteDMATransfer(dst_ids=[dst(y) for y in x], dma_engine_mask=mask(es), remote_sem=T.sem[sem],
+                                              srcs=[ap(s)], dsts=[ap(to)] * len(x)) for x, es, s, to in transfers],
+                           local_sem=T.sem["left"])
 
     def spread(src, to, sem):
-        sem_of[0] = sem
-        g.remote_dma_fused(send([(far, out_eng, src, to), (near, in_eng, src, to)], src), local_sem=T.sem["left"])
+        send([(far, out_eng, src, to), (near, in_eng, src, to)], src, sem)
 
     half = len(in_eng) // 2
 
@@ -218,9 +224,7 @@ def rank_program(g, core, T, topo):
         return out_eng[a:a + n]
 
     def pieces(name, to, sem):
-        sem_of[0] = sem
-        g.remote_dma_fused(send([([y], share(y), r(name, 16 * y, 16 * y + 16), to) for y in others], r(name)),
-                           local_sem=T.sem["left"])
+        send([([y], share(y), r(name, 16 * y, 16 * y + 16), to) for y in others], r(name), sem)
 
     n_all = sum(len(out_eng) if x in far else len(in_eng) for x in others)
     n_pcs = sum(half if x in near else far_share(x, me)[1] for x in others)
@@ -232,149 +236,170 @@ def rank_program(g, core, T, topo):
                 wrote(e, (sem, tot))
     due["am"] = n_all
     for x in others:
-        wrote(r("land", x, x + 1), ("am", n_all))
+        wrote(r("land", 8 * x, 8 * x + 1), ("am", n_all))
 
+    mdr = ("mdr", 0, 16, 0, 48, 1)
     dma("a", r("tbt"), T.tb[:, :], "dtb")
     dma("s", r("ut"), T.u[:, 0:4], "du")
-    dma("s", r("nzt", 0, 384), T.nz[:, :], "dnz")
+    dma("s", r("nzt", 0, 384), T.nz[:, :], "dnz", 32)
+    dma("s", r("nzt", 384, 704), T.nz[:, 0:320], "dnz", 32)
+    dma("s", r("vt", 192, 512), T.tb[:, 0:320], "dpv")
     dma("s", r("wt"), T.w[:, :], "dw")
 
     iota(r("pi"), [[0, 2]], 0, 1)
     iota(r("ipd"), [[1, 196]], 0, -1)
-    iota(r("r16"), [[0, 12], [1, 16]], 0, 0)
     iota(r("ir", 0, 196), [[1, 196]], 0, 0)
+    iota(r("r16"), [[0, 12], [1000, 16]], 0, 0)
+    iota(r("m16"), [[16, 4]], 0, 0)
+    iota(r("bi"), [[0, 6], [1, 8]], 0, 0)
+    iota(r("ai"), [[1, 6], [0, 8]], 0, 0)
+    iota(r("r8k"), [[0, 6], [1000, 8]], 0, 0)
+    iota(r("wgt"), [[-48, 6], [48, 8]], 0, 0)
+    iota(r("wgt1"), [[-16, 6], [16, 8]], 0, 0)
+    iota(r("qa"), [[0, 16], [48, 6]], 240, 0)
+    iota(r("qb"), [[0, 16], [-48, 6]], 240, 0)
+    iota(r("c48"), [[48, 8]], 0, 0)
+    iota(r("ir", 196, 800), [[1, 604]], 196, 0)
+    iota(r("x48"), [[0, 6], [1000, 48]], 0, 0)
+
     fill(r("ones"), 1.0)
     fill(r("onet"), 1.0)
-    fill(r("ct"), 0.0)
+    zero(r("ct", 0, 512), r("onet"))
     qz("oneq", 0, 128, r("onet"))
-    ts(r("bm"), r("ipd", 0, 192), 0.0, O.is_le, 3e29, O.mult)
-    for k in range(4):
-        ts(r("ubt", k, 512, 4), r("ones"), r("ut", k, k + 1), O.mult)
-    qz("uq", 0, 128, r("ubt"))
+    ts(r("pa", 0, 2), r("pi"), 3, O.arith_shift_right)
+    for k, b in enumerate((7, 15, 8, 64, 127)):
+        ts(r("pa", 2 * k + 2, 2 * k + 4), r("pi"), b, O.bitwise_and)
     ts(r("ia"), r("ipd"), 15, O.bitwise_and)
+    cp(r("paf"), r("pa"))
+    ts(r("bm"), r("ipd", 0, 192), 0.0, O.is_le, 3e29, O.mult)
+    ts(r("cf", 0, 1), r("paf", 2, 3), 16.0, O.mult, r("paf", 0, 1), O.add)
+    ts(r("cf", 1, 2), r("paf", 2, 3), 4.0, O.is_ge)
     ts(r("dm"), r("ia", 0, 192), 0.0, O.is_equal)
-    ts(r("r16"), r("r16"), 0.0, O.is_gt)
+    ts(r("cf", 2, 3), r("cf", 0, 1), -128.0, O.add, r("cf", 1, 2), O.mult)
+    ts(r("wm"), r("ir", 0, 194), r("cf", 0, 1), O.is_equal)
+    ts(r("cf", 3, 4), r("cf", 2, 3), 192.0, O.add)
+    for k in range(4):
+        if k % 2:
+            lin(r("ubt", k, 512, 4), r("ones"), 0.0, r("ut", k, k + 1))
+        else:
+            ts(r("ubt", k, 512, 4), r("ones"), r("ut", k, k + 1), O.mult)
+    zero(r("ct", 512, 784), r("onet", 0, 272))
 
     qz("tq", 0, 192, r("tbt"))
+    qz("uq", 0, 128, r("ubt"))
     mm(1, "tq", 0, "uq", 0, 128)
     mm(0, "uq", 0, "tq", 0, 192)
     mm(2, "tq", 64, "uq", 0, 128)
-    ts(r("pa", 0, 2), r("pi"), 3, O.arith_shift_right)
-    ts(r("pa", 2, 4), r("pi"), 7, O.bitwise_and)
-    ts(r("pa", 4, 6), r("pi"), 15, O.bitwise_and)
-    cp(r("cf", 2, 4), r("pa", 0, 2))
-    ts(r("cf", 4, 6), r("pa", 2, 4), 16.0, O.mult, r("cf", 2, 3), O.add)
-    ts(r("cf", 6, 8), r("pa", 2, 4), 4.0, O.is_ge)
-    ts(r("cf", 10, 12), r("cf", 4, 6), -128.0, O.add, r("cf", 6, 7), O.mult)
-    ts(r("cf", 12, 14), r("cf", 10, 12), 192.0, O.add)
-    cp(r("qf"), r("pa", 4, 6))
+    ts(r("wa"), r("ir", 0, 194), r("cf", 3, 4), O.is_equal, 256.0, O.mult)
+    tt(r("wm"), r("wm"), r("wa"), O.add)
+    move("lb", K, "tq", K, 80, "dpad", 64)
+    move("lc", K, "tq", K, 80, "dpad", 64)
 
-    def sort(src, sp0, sp1, n):
-        def lower(x, a=0, b=192):
-            return r(x[0], a, b, 1, 64, 128)
-        ts(r("ct", 0, 768, 4), src, sp0, O.is_gt)
-        tt(r("sm"), src, r("bm"), O.add)
-        tt(r("sm1", 0, 64, 1, 64), lower(src, 128), r("bm", 64, 128, 1, 64), O.add)
-        ts(r("ct", 1, 768, 4, 64), lower(src), sp1, O.is_gt)
-        ts(r("ct", 2, 768, 4), r("sm"), sp0, O.is_equal)
-        ts(r("ct", 515, 768, 4, 64), r("sm1", 0, 64, 1, 64), sp1, O.is_equal)
+    def sort_ops(src, sp0, sp1, n):
+        def lower(a=0, b=192):
+            return r(src[0], a, b, 1, 64, 128)
+        ops = [lambda: ts(r("ct", 0, 768, 4), src, sp0, O.is_gt),
+               lambda: tt(r("sm"), src, r("bm"), O.add),
+               lambda: tt(r("sm1", 0, 64, 1, 64), lower(128), r("bm", 64, 128, 1, 64), O.add),
+               lambda: ts(r("ct", 1, 768, 4, 64), lower(), sp1, O.is_gt),
+               lambda: ts(r("ct", 2, 768, 4), r("sm"), sp0, O.is_equal),
+               lambda: ts(r("ct", 515, 768, 4, 64), r("sm1", 0, 64, 1, 64), sp1, O.is_equal)]
         if n > 192:
-            ts(r("ct", 768, 769), sp0, 0.0, O.is_gt)
-            ts(r("ct", 769, 770, 1, 64), sp1, 0.0, O.is_gt)
-        qz("cq", 0, n, r("ct", 0, 4 * n))
-        mm(3, "oneq", 0, "cq", 0, n)
+            ops += [lambda: ts(r("ct", 768, 769), sp0, 0.0, O.is_gt),
+                    lambda: ts(r("ct", 769, 770, 1, 64), sp1, 0.0, O.is_gt)]
+        return ops + [lambda: qz("cq", 0, n, r("ct", 0, 4 * n)), lambda: mm(3, "oneq", 0, "cq", 0, n)]
 
-    def ranks():
-        tt(r("rd", 0, 192), r("ps3", 0, 192), r("dm"), O.mult)
-        scan(r("sc"), r("r16"), r("rd", 0, 192))
-        cp(r("rof"), r("sc", 15, 192, 16))
+    def ranks_ops():
+        return [lambda: tt(r("rd"), r("ps3", 0, 192), r("dm"), O.mult), lambda: scan(r("sc"), r("r16"), r("rd")),
+                lambda: cp(r("rof"), r("sc", 15, 192, 16))]
 
     def scatter(val):
         issue("v", [val, r("rof")], [r("prm")], lambda: V.tensor_copy(ap(r("prm")).indirect(ap(r("rof"))), ap(val)))
 
-    def order(out, a, b):
-        tt(r("pd", a, b), r("prm", a, b), r("dm", a, b), O.mult)
-        scan(r("sc2", a, b), r("r16", a, b), r("pd", a, b))
-        cp(out, r("sc2", a + 15, b, 16))
+    def order_ops(out, a, b):
+        return [lambda: tt(r("pd", a, b), r("prm", a, b), r("dm", a, b), O.mult),
+                lambda: scan(r("sc2", a, b), r("r16", a, b), r("pd", a, b)),
+                lambda: cp(out, r("sc2", a + 15, b, 16))]
 
-    sort(r("ps0", 0, 192), r("ps1", 0, 1), r("ps2", 0, 1, 1, 64), 194)
-    ts(r("wa"), r("ir", 0, 194), r("cf", 12, 13), O.is_equal, 256.0, O.mult)
-    ts(r("wm"), r("ir", 0, 194), r("cf", 4, 5), O.is_equal)
-    tt(r("wm"), r("wm"), r("wa"), O.add)
-    tt(r("rd"), r("ps3", 0, 194), r("wm"), O.mult)
-    issue("v", [r("rd")], [r("msgf", 0, 1)], lambda: V.tensor_reduce(ap(r("msgf", 0, 1)), ap(r("rd")), AxisListType.X, O.add))
-    cp(r("msg", 0, 1), r("msgf", 0, 1))
-    spread(r("msg", 0, 1), r("land", me, me + 1), "am")
-    ranks()
+    weave(sort_ops(r("ps0", 0, 192), r("ps1", 0, 1), r("ps2", 0, 1, 1, 64), 194))
+
+    lin(r("lf", 0, 4), r("m16"), 0.0, r("paf", 2, 3))
+    lin(r("cf", 5, 6), r("paf", 6, 7), 0.125, 0.0)
+    lin(r("lf", 4, 8), r("m16"), 0.125, r("cf", 5, 6))
+    lin(r("lf", 8, 12), r("lf", 0, 4), 8.0, 7.0)
+    lin(r("lf", 12, 16), r("lf", 4, 8), 8.0, 7.0)
+    lin(r("lf", 16, 17), r("paf", 10, 11), 1.0, 0.0)
+    lin(r("lf", 17, 18), r("paf", 10, 11), 1.0, r("paf", 8, 9))
+    lin(r("lf", 18, 24), r("ir", 0, 6), 1.0, 0.0)
+    lin(r("nw", 0, 3), r("m16", 0, 3), 1.0, r("paf", 4, 5))
+    for k in range(4):
+        zero(r("eht", 512 * k, 512 * k + 512), r("onet"))
+    lin(r("r8"), r("bi"), 1.0, 0.0, F.Sign)
+    lin(r("rsq"), r("r16", 0, 32), 1.0, 0.0, F.Sign)
+    lin(r("th"), r("wgt1"), 1.0 / 128, 0.0)
+    for x, c in (("key", -1e6), ("base", 0.0), ("c1", 0.0), ("i48", float(K * me))):
+        lin(r(x), r("ones", 0, 8), 0.0, c)
+    lin(r("ps"), r("ones", 0, 64), 0.0, 99.0)
+    lin(r("sw", 576, 584), r("ones", 0, 8), 0.0, BIG)
+    lin(r("tkq", 0, 1), r("paf", 4, 5), 6.0, 0.0)
+    lin(r("tkq", 1, 2), r("paf", 4, 5), 1.0, float(16 * me))
+    zero(r("rho", 72, 96), r("ones", 0, 24))
+    ts(r("idt"), r("ipd", 0, 128), 0.0, O.is_equal, 0.5, O.mult)
+    for k in range(4):
+        ac(r("eht", 513 * k, 512 * k + 512, 4), r("idt"))
+
+    tt(r("rdm"), r("ps3", 0, 194), r("wm"), O.mult)
+    issue("a", [r("rdm")], [r("junk"), r("msgf", 0, 1)], lambda: A.activation(
+        ap(r("junk")), ap(r("rdm")), F.Copy, accum_out=ap(r("msgf", 0, 1))))
+    my_land = r("land", 8 * me, 8 * me + 1)
+    weave(ranks_ops())
+    cp(my_land, r("msgf", 0, 1))
+    spread(my_land, my_land, "am")
     scatter(r("ir", 0, 192))
-    order(r("ol", 0, 3), 0, 48)
+    weave(order_ops(r("ol", 0, 3), 0, 48))
     pick("ls", 0, 48, "tq", 0, 192, r("ol", 0, 3), [(0, 192)])
     for x, y in zip(both("ls", 0, K), both("w0", K * me, K * me + K)):
         spread(x, y, "al")
     move("w0", K * me, "ls", 0, K, "dls")
-    order(r("ol", 6, 12), 96, 192)
-    pick("hb", 0, 96, "tq", 0, 192, r("ol", 6, 12), [(0, 192)])
-    for x, y in zip(("hb", "hb_s"), both("hp", 16 * me, 16 * me + 16)):
-        pieces(x, y, "ah")
-    move("hp", 16 * me, "hb", 16 * me, 16, "dhb")
-    order(r("om", 0, 3), 48, 96)
+    weave(order_ops(r("om", 0, 3), 48, 96))
+    cp(r("lists"), r("lf"))
     pick("nb", 0, 48, "tq", 0, 192, r("om", 0, 3), [(0, 192)])
-
-    iota(r("m16"), [[16, 12]], 0, 0)
-    iota(r("bi"), [[0, 8], [1, 6]], 0, 0)
-    iota(r("ai"), [[1, 8], [0, 6]], 0, 0)
-    ts(r("nw"), r("m16"), r("qf", 0, 1), O.add)
-    ts(r("hi", 0, 3), r("nw", 0, 3), 1.0 / 6, O.mult, -2.5 / 6, O.add)
-    ts(r("l2", 0, 3), r("hi", 0, 3), 1.0, O.mult)
-    ts(r("l4", 0, 3), r("hi", 0, 3), 6.0, O.mult, 5.0, O.add)
-    ts(r("wa", 0, 3), r("hi", 0, 3), -6.0, O.mult)
-    tt(r("wa", 4, 7), r("wa", 0, 3), r("nw", 0, 3), O.add)
-    ts(r("l1", 0, 3), r("wa", 4, 7), 1.0, O.mult)
-    ts(r("l3", 0, 3), r("wa", 4, 7), 6.0, O.mult, 5.0, O.add)
-    ts(r("r6"), r("bi"), 0.0, O.is_gt)
-    tt(r("wgt1"), r("bi"), r("ai"), O.subtract)
-    ts(r("wgt"), r("wgt1"), 48.0, O.mult)
-    ts(r("wgt1"), r("wgt1"), 16.0, O.mult)
-    for x in ("key", "ps", "c1", "base"):
-        fill(r(x), 0.0)
-    fill(r("vt"), 0.0)
-    fill(r("eht"), 0.0)
-    for k in range(4):
-        ts(r("eht", 513 * k, 512 * k + 512, 4), r("ipd", 0, 128), 0.0, O.is_equal, 0.5, O.mult)
-    qz("eq", 0, 512, r("eht"))
-    fill(r("nzt", 384, 704), 0.0)
+    fill(r("fb"), -1000000)
     qz("nq", 0, 176, r("nzt"))
-    qz("lb", 0, 128, r("vt"))
-    qz("lc", 0, 128, r("vt"))
+    qz("eq", 0, 512, r("eht"))
 
     def noise(t):
         for k in range(4):
             mm(4 + k, "eq", 128 * k, "nq", K * t, 128, True, False)
     noise(0)
+    l_mod, l_div, l_mod7, l_div7 = [r("lists", k, k + 3) for k in (0, 4, 8, 12)]
 
-    def places(w):
-        gather(r("k1"), r("key"), r("l1", 0, 3))
-        gather(r("k2"), r("key"), r("l2", 0, 3))
-        tt(r("gg", 0, 36), r("k1", 0, 36), r("k2", 0, 36), O.is_gt)
-        scan(r("ps", 0, 36), r("r6", 0, 36), r("gg", 0, 36))
-        gather(r("p1"), r("ps"), r("l3", 0, 3))
-        gather(r("p2"), r("ps"), r("l4", 0, 3))
-        tt(r("gw", 0, 36), r("gg", 0, 36), r(w, 0, 36), O.mult)
-        tt(r("su", 0, 36), r("p1", 0, 36), r("p2", 0, 36), O.add)
-        ts(r("ee", 0, 36), r("su", 0, 36), 5.0, O.is_equal)
-        tt(r("ew", 0, 36), r("ee", 0, 36), r("gw", 0, 36), O.mult)
-        scan(r("dts", 0, 36), r("r6", 0, 36), r("ew", 0, 36))
+    def places(key, w, even):
+        gather(r("k1"), key, l_mod)
+        gather(r("k2"), key, l_div)
+        if even:
+            tt(r("dd"), r("k1"), r("k2"), O.subtract)
+            tt(r("gg"), r("dd"), even, O.is_gt)
+        else:
+            tt(r("gg"), r("k1"), r("k2"), O.is_gt)
+        scan(r("ps", 0, 48), r("r8k"), r("gg"))
+        tt(r("gw"), r("gg"), r(w), O.mult)
+        gather(r("p1"), r("ps"), l_mod7)
+        gather(r("p2"), r("ps"), l_div7)
+        tt(r("su"), r("p1"), r("p2"), O.add)
+        ts(r("ee"), r("su"), 5.0, O.is_equal)
+        tt(r("ew"), r("ee"), r("gw"), O.mult)
+        scan(r("dts"), r("r8"), r("ew"), O.mult)
 
-    def note(k):
-        tt(r("od1", 0, 36), r("p1", 0, 36), r("ai", 0, 36), O.is_equal)
-        tt(r("od2", 0, 36), r("od1", 0, 36), r("bi", 0, 36), O.mult)
-        scan(r("od1", 0, 36), r("r6", 0, 36), r("od2", 0, 36))
-        cp(r("odt", 6 * k, 6 * k + 6), r("od1", 5, 36, 6))
+    def note_ops(k):
+        return [lambda: tt(r("od1"), r("p1"), r("ai"), O.is_equal), lambda: tt(r("od2"), r("od1"), r("bi"), O.mult),
+                lambda: scan(r("od1"), r("r8k"), r("od2")), lambda: cp(r("odt", 6 * k, 6 * k + 6), r("od1", 7, 48, 8))]
 
-    own = 6 * me + 5
+    own = 8 * me + 7
     my_dts, my_ps = r("dts", own, own + 1), r("ps", own, own + 1)
+    six = (0, 6)
 
-    def anew(buf, off, parts, end, out, o):
+    def anew(buf, off, parts, end):
         pick(buf, 0, 48, "w0", 0, end, off, parts)
         for k in range(4):
             mm(4 + k, "eq", 128 * k, buf, 0, 128, False, True)
@@ -384,22 +409,18 @@ def rank_program(g, core, T, topo):
             (cp if k % 2 == 0 else ac)(r("vt", k, 192, 4), r("ps%d" % (4 + k), 0, 48))
         qz(out, o, 128, r("vt"))
 
-    fill(r("i48"), float(K * me))
-    wait("v", "am", n_all)
-    cp(r("land", me, me + 1), r("msgf", 0, 1))
-    ts(r("hi", 0, 6), r("land", 0, 6), 1.0 / 256, O.mult, -127.5 / 256, O.add)
-    issue("g", [r("hi", 0, 6)], [r("fb", 0, 6)], lambda: g.partition_broadcast(
-        ap(r("fb", 0, 6)), ap(r("hi", 0, 6, 1, 0, 1)), 128))
-    ts(r("tmp", 0, 6), r("fb", 0, 6), 8.0, O.mult)
-    tt(r("key", 0, 6), r("tmp", 0, 6), r("ir", 0, 6), O.subtract)
-    places("wgt")
+    ts(r("hi", *six), r("land", 0, 48, 8), 1.0 / 256, O.mult, -127.5 / 256, O.add)
+    issue("g", [r("hi", *six)], [r("fb", *six)], lambda: g.partition_broadcast(
+        ap(r("fb", *six)), ap(r("hi", 0, 6, 1, 0, 1)), 128))
+    cp(r("v6", *six), r("land", 0, 48, 8))
+    places(r("fb"), "wgt", r("th"))
     ts(r("oll", 0, 3), r("nw", 0, 3), my_dts, O.add, r("i48", 0, 1), O.add)
 
-    dma("s", ("mdr", 0, 16, 0, 48, 1), r("land", 0, 6), "dmd")
+    dma("s", mdr, r("v6", *six), "dmd")
     for k in range(8):
-        dma("s", r("rw", 0, 48, 1, 16 * k, 16 * k + 16), ("mdr", 0, 16, 0, 48, 1), "drw", 128)
+        dma("s", r("rw", 0, 48, 1, 16 * k, 16 * k + 16), mdr, "drw", 128)
 
-    anew("lb", r("oll", 0, 3), [(0, 288)], 288, "nb", 64)
+    anew("lb", r("oll", 0, 3), [(0, 288)], 288)
     ts(r("tk", 0, 1), my_ps, 3.0, O.is_ge, 64.0, O.mult)
     ts(r("ox", 0, 3), r("nw", 0, 3), r("tk", 0, 1), O.add)
     pack("nb", 64)
@@ -407,67 +428,60 @@ def rank_program(g, core, T, topo):
     for x, y in zip(both("xs", 0, K), both("w0", LX + K * me, LX + K * me + K)):
         spread(x, y, "ax")
     move("w0", LX + K * me, "xs", 0, K, "dxs")
-    iota(r("ir", 196, 800), [[1, 604]], 196, 0)
-    iota(r("x48"), [[0, 6], [1, 48]], 0, 0)
-    iota(r("ri"), [[0, 16], [1, 6]], 0, 0)
     noise(1)
+    weave(order_ops(r("ol", 6, 12), 96, 192))
+    pick("hb", 0, 96, "tq", 0, 192, r("ol", 6, 12), [(0, 192)])
+    for x, y in zip(("hb", "hb_s"), both("hp", 16 * me, 16 * me + 16)):
+        pieces(x, y, "ah")
+    move("hp", 16 * me, "hb", 16 * me, 16, "dhb")
     mm(1, "uq", 0, "w0", 0, 288)
     ac(r("sw", 0, 288), r("ps1", 0, 288))
 
-    six = (0, 6)
-    ts(r("x48"), r("x48"), 0.0, O.is_gt)
-    ts(r("t0", *six), r("ps", 5, 36, 6), 3.0, O.is_ge)
-    ts(r("tmp", *six), r("dts", 5, 36, 6), 1.0 / 48, O.mult)
-    tt(r("hi", *six), r("tmp", *six), r("ir", *six), O.add)
-    cp(r("base", *six), r("hi", *six))
-    tt(r("kd", 0, 36), r("k1", 0, 36), r("k2", 0, 36), O.subtract)
-    tt(r("tmp", 0, 36), r("ee", 0, 36), r("gg", 0, 36), O.mult)
-    tt(r("kd", 0, 36), r("kd", 0, 36), r("tmp", 0, 36), O.mult)
-    scan(r("tmp", 0, 36), r("r6", 0, 36), r("kd", 0, 36))
-    tt(r("f8", *six), r("tmp", 5, 36, 6), r("key", *six), O.add)
-    tt(r("f8", *six), r("f8", *six), r("base", *six), O.add)
-    ts(r("apre", *six), r("f8", *six), float(-8 * (P - K)), O.add, 0.0, O.max)
-    tt(r("apre", *six), r("apre", *six), r("t0", *six), O.mult)
-    tt(r("apre", *six), r("f8", *six), r("apre", *six), O.subtract)
-    tt(r("apre", *six), r("apre", *six), r("ir", *six), O.subtract)
-    ts(r("t8", *six), r("t0", *six), 8.0, O.mult)
-    ts(r("c1", *six), r("t0", *six), float(LX), O.mult)
-    ts(r("f8", *six), r("ir", *six), float(K), O.mult)
-    tt(r("c1", *six), r("c1", *six), r("f8", *six), O.add)
-    gather(r("b1"), r("base"), r("l1", 0, 3))
-    gather(r("b2"), r("base"), r("l2", 0, 3))
-    tt(r("wb"), r("b1"), r("b2"), O.subtract)
-    ts(r("wb"), r("wb"), 16.0, O.mult)
-    ts(r("hrow", *six), r("base", *six), 16.0, O.mult, r("qf", 0, 1), O.add)
-    ts(r("tkq", 0, 1), r("qf", 0, 1), 6.0, O.mult)
-    ts(r("tkq", 1, 2), r("qf", 0, 1), float(16 * me), O.add)
-    ts(r("ob"), r("base", *six), r("tkq", 0, 1), O.add)
-    ts(r("oa"), r("ir", *six), 1.0, O.mult)
-    note(0)
-    fill(r("sw", 576, 584), BIG)
-    ts(r("cf", 14, 16), r("pi"), 64.0, O.is_ge, 64.0, O.mult)
-    ts(r("o32", 0, 1), r("pi", 0, 1), 1.0, O.mult)
-    ts(r("o32", 1, 2), r("pi", 0, 1), r("cf", 14, 15), O.add)
-    ts(r("qa"), r("ri"), 48.0, O.mult, 240.0, O.add)
-    ts(r("qb"), r("qa"), -1.0, O.mult, 480.0, O.add)
-    qz("wq", 0, 256, r("wt"))
-    fill(r("rho"), 0.0)
-    cp(r("vf"), r("rw"))
-    ts(r("hw"), r("rw"), 1.0 / 256, O.mult, -127.5 / 256, O.add)
-    ts(r("y0", 0, 48), r("hw"), -256.0, O.mult)
-    tt(r("rho", 0, 48), r("y0", 0, 48), r("vf"), O.add)
-    cp(r("rho", 48, 72), r("hw", 24, 48))
-    ts(r("y0"), r("rho"), 48.0, O.is_ge)
-    tt(r("y0"), r("y0"), r("qa"), O.mult)
-    ts(r("y0g"), r("rho"), 96.0, O.is_ge)
-    tt(r("y0g"), r("y0g"), r("qb"), O.mult)
-    tt(r("y0"), r("y0"), r("y0g"), O.add)
-    tt(r("y0"), r("y0"), r("rho"), O.add)
-    gather(r("y0g"), r("y0"), r("ob"))
-    gather(r("c1x"), r("c1"), r("oa"))
-    ts(r("loc"), r("y0g"), 48.0, O.is_lt)
-    tt(r("loc"), r("loc"), r("c1x"), O.mult)
-    tt(r("loc"), r("loc"), r("y0g"), O.add)
+    def after_scalar():
+        lin(r("hf"), r("hf"), 1.0, WHOLE)
+        lin(r("hf"), r("hf"), 1.0, -WHOLE)
+        lin(r("h2"), r("hf"), -256.0, 0.0)
+        lin(r("rho", 48, 72), r("hf", 24, 48), 1.0, 0.0)
+    where = [
+        lambda: ts(r("hf"), r("rw"), 1.0 / 256, O.mult, -127.5 / 256, O.add),
+        lambda: cp(r("vf"), r("rw")),
+        after_scalar,
+        lambda: tt(r("rho", 0, 48), r("h2"), r("vf"), O.add),
+        lambda: lin(r("s1"), r("rho"), 1000.0, -47000.0, F.Relu),
+        lambda: lin(r("s2"), r("rho"), 1000.0, -95000.0, F.Relu),
+        lambda: tt(r("s1"), r("s1"), r("qa"), O.min),
+        lambda: tt(r("s2"), r("s2"), r("qb"), O.min),
+        lambda: tt(r("y0"), r("s1"), r("rho"), O.add),
+        lambda: tt(r("y0"), r("y0"), r("s2"), O.add),
+        lambda: gather(r("y0g"), r("y0"), r("ob")),
+        lambda: ts(r("lt"), r("y0g"), 48.0, O.is_lt),
+        lambda: tt(r("lt"), r("lt"), r("c1x"), O.mult),
+        lambda: tt(r("y0g"), r("lt"), r("y0g"), O.add)]
+    fit = [
+        lambda: ts(r("t0", *six), r("ps", 7, 48, 8), 3.0, O.is_ge),
+        lambda: tt(r("kd"), r("ee"), r("gg"), O.mult),
+        lambda: tt(r("kd"), r("kd"), r("dd"), O.mult),
+        lambda: scan(r("fs"), r("r8"), r("kd"), O.mult),
+        lambda: tt(r("fn", *six), r("fs", 7, 48, 8), r("fb", *six), O.add),
+        lambda: lin(r("mx", *six), r("fn", *six), 1.0, float(K - P), F.Relu),
+        lambda: tt(r("mx", *six), r("mx", *six), r("t0", *six), O.mult),
+        lambda: tt(r("fn", *six), r("fn", *six), r("mx", *six), O.subtract),
+        lambda: lin(r("fn", *six), r("fn", *six), 8.0, 0.0),
+        lambda: tt(r("apre", *six), r("fn", *six), r("ir", *six), O.subtract),
+        lambda: lin(r("t8", *six), r("t0", *six), 8.0, 0.0)]
+    bases = [
+        lambda: ts(r("bt", *six), r("dts", 7, 48, 8), 1.0 / 48, O.mult),
+        lambda: tt(r("hi", *six), r("bt", *six), r("ir", *six), O.add),
+        lambda: ts(r("base", *six), r("hi", *six), 16.0, O.mult),
+        lambda: gather(r("b1"), r("base"), l_mod),
+        lambda: gather(r("b2"), r("base"), l_div),
+        lambda: ts(r("ob"), r("base", *six), 1.0 / 16, O.mult, r("tkq", 0, 1), O.add),
+        lambda: tt(r("wb"), r("b1"), r("b2"), O.subtract),
+        lambda: lin(r("hrow", *six), r("base", *six), 1.0, r("paf", 4, 5)),
+        lambda: lin(r("c1", *six), r("t0", *six), float(LX), 0.0),
+        lambda: tt(r("c1", *six), r("c1", *six), r("c48", *six), O.add),
+        lambda: gather(r("c1x"), r("c1"), r("lists", 18, 24))]
+    weave(fit, bases, note_ops(0), where)
 
     mm(0, "uq", 0, "w0", LX, 288)
     ts(r("pos"), r("ps0", 0, 288), 0.0, O.is_gt)
@@ -475,32 +489,36 @@ def rank_program(g, core, T, topo):
     scan(r("psc"), r("x48"), r("pos"))
     tt(r("np", *six), r("psc", 47, 288, 48), r("t8", *six), O.mult)
     tt(r("key", *six), r("np", *six), r("apre", *six), O.add)
-    places("wgt1")
+    places(r("key"), "wgt1", None)
     ts(r("og", 0, 1), r("tkq", 1, 2), my_dts, O.add)
-    gather(r("l16"), r("loc"), r("og", 0, 1))
+    tt(r("gw"), r("gg"), r("wb"), O.mult)
+    gather(r("l16"), r("y0g"), r("og", 0, 1))
+    tt(r("ew"), r("ee"), r("gw"), O.mult)
     ts(r("osl"), r("l16", 0, 12), float(HX), O.min)
     issue("a", [r("ir"), r("osl")], [r("lrow")], lambda: A.activation(ap(r("lrow")), ap(r("ir")).indirect(ap(r("osl"))), F.Copy))
-    tt(r("gw", 0, 36), r("gg", 0, 36), r("wb", 0, 36), O.mult)
-    tt(r("ew", 0, 36), r("ee", 0, 36), r("gw", 0, 36), O.mult)
-    scan(r("hd", 0, 36), r("r6", 0, 36), r("ew", 0, 36))
-    tt(r("hl", *six), r("hd", 5, 36, 6), r("hrow", *six), O.add)
-    cp(r("oh"), r("hl", *six))
-    pick("hs", 0, 96, "hp", 0, 96, r("oh"), [(0, 96)])
-    for x, y in zip(("hs", "hs_s"), both("w0", HX + 16 * me, HX + 16 * me + 16)):
-        pieces(x, y, "a3")
-    move("w0", HX + 16 * me, "hs", 16 * me, 16, "dhs")
-    gather(r("st"), r("sw"), r("osl"))
-    gather(r("g32"), r("st"), r("o32"))
-    tt(r("m32"), r("g32"), r("dm", 0, 32), O.mult)
-    scan(r("sq"), r("r16", 0, 32), r("m32"))
-    sort(r("st"), r("sq", 15, 16), r("sq", 31, 32, 1, 64), 192)
-    ranks()
+
+    def hop3():
+        pick("hs", 0, 96, "hp", 0, 96, r("oh"), [(0, 96)])
+        for x, y in zip(("hs", "hs_s"), both("w0", HX + 16 * me, HX + 16 * me + 16)):
+            pieces(x, y, "a3")
+        move("w0", HX + 16 * me, "hs", 16 * me, 16, "dhs")
+    weave([lambda: scan(r("hd"), r("r8"), r("ew"), O.mult),
+           lambda: tt(r("hl", *six), r("hd", 7, 48, 8), r("hrow", *six), O.add),
+           lambda: cp(r("oh"), r("hl", *six))],
+          [lambda: gather(r("st"), r("sw"), r("osl")),
+           lambda: gather(r("g32"), r("st"), r("lists", 16, 18)),
+           lambda: tt(r("m32"), r("g32"), r("dm", 0, 32), O.mult),
+           lambda: scan(r("sq"), r("rsq"), r("m32"), O.mult)])
+    weave(sort_ops(r("st"), r("sq", 15, 16), r("sq", 31, 32, 1, 64), 192))
+    hop3()
+    qz("wq", 0, 256, r("wt"))
+    weave(ranks_ops())
     scatter(r("lrow"))
-    order(r("ol1", 0, 3), 0, 48)
-    anew("lc", r("ol1", 0, 3), [(0, 576)], 576, "w0", NX)
+    weave(order_ops(r("ol1", 0, 3), 0, 48))
+    anew("lc", r("ol1", 0, 3), [(0, 576)], 576)
     ts(r("tk", 0, 1), my_dts, 0.0, O.not_equal)
-    ts(r("fm", 0, 12), r("sc", 15, 192, 16), 48.0, O.is_lt, r("tk", 0, 1), O.mult)
     ts(r("rk", 0, 12), r("sc", 15, 192, 16), float(NX), O.add)
+    ts(r("fm", 0, 12), r("sc", 15, 192, 16), 48.0, O.is_lt, r("tk", 0, 1), O.mult)
     tt(r("rk", 0, 12), r("rk", 0, 12), r("l16", 0, 12), O.subtract)
     tt(r("rk", 0, 12), r("rk", 0, 12), r("fm", 0, 12), O.mult)
     tt(r("fl", 0, 12), r("rk", 0, 12), r("l16", 0, 12), O.add)
@@ -517,7 +535,7 @@ def rank_program(g, core, T, topo):
     dma("s", T.y[:, 0:192], r("ysb", 0, 192), "dout", 128)
     ac(r("ysb", 192, 384), r("ps2", 0, 192))
     dma("a", T.y[:, 192:384], r("ysb", 192, 384), "dout", 128)
-    note(1)
+    weave(note_ops(1))
     dma("s", T.od[:, :], r("odt", 0, 12, 1, 0, 1), "dout", 128)
 
     for q in count:

@@ -1,5 +1,5 @@
 from concourse.bass import DstId, RemoteDMATransfer
-from concourse.mybir import dt, AluOpType as O, ActivationFunctionType as F
+from concourse.mybir import dt, AluOpType as O, AxisListType, ActivationFunctionType as F
 
 P, K, N = 192, 48, 6
 LX, HX, NX = 288, 576, 672
@@ -9,13 +9,13 @@ WHOLE = 12582912.0
 SCRATCH = {"mdr": ("dram", [16, 48], "uint16")}
 ARENA = {}
 for _d, _l in (
-        ("bfloat16", "ut 4 tbt 768 nzt 704 wt 1024 ubt 512 onet 512 eht 2048 vt 512 ct 784 idt 128"),
+        ("bfloat16", "ut 4 tbt 768 nzt 704 wt 1024 ubt 512 onet 512 eht 2048 vt 512 ct 784 idt 128 r16 192 x48 288 rd 192 sc 192 "
+                     "pos 288 psc 288"),
         ("int32", "ipd 196 pi 2 pa 12 ia 196 hi 8 fb 8"),
-        ("float32", "ir 800 m16 4 lf 24 bi 48 ai 48 r8k 48 r16 192 x48 288 ones 128 paf 12 cf 16 bm 192 dm 192 wm 194 wa 194 nw 4 "
-                    "r8 48 rsq 32 wgt 48 wgt1 48 th 48 c48 8 sm 192 sm1 64 rd 192 rdm 194 junk 194 sc 192 prm 192 pd 192 sc2 192 "
-                    "msgf 2 sw 584 st 192 g32 32 m32 32 sq 32 lrow 192 ysb 384 odt 16 pos 288 psc 288 ps 64 rho 96 qa 96 qb 96 "
-                    "y0 96"),
-        ("uint16", "land 48 v6 8 rw 48 lists 24 rof 12 ol 12 oll 4 om 4 ox 4 ob 6 og 2 osl 12 oh 6 ol1 4 ofin 12")):
+        ("float32", "ir 800 m16 4 lf 24 bi 48 ai 48 r8k 48 ones 128 paf 12 cf 16 bm 192 dm 192 wm 194 wa 194 nw 4 "
+                    "r8 48 rsq 32 wgt 48 wgt1 48 th 48 c48 8 sm 128 sm1 64 rdm 194 junk 194 prm 192 pd 192 sc2 192 "
+                    "msgf 2 sw 672 st 192 g32 32 m32 32 sq 32 lrow 192 ysb 384 odt 16 ps 64 rho 96 qa 96 qb 96 y0 96"),
+        ("uint16", "land 48 v6 8 rw 48 lists 24 rof 12 ol 12 oll 4 om 4 ox 4 ob 6 og 2 osl 16 oh 6 ol1 4 ofin 12")):
     _w = _l.split()
     for _k, _n in zip(_w[::2], _w[1::2]):
         SCRATCH[_k] = ("sbuf", [128, int(_n)], _d)
@@ -26,8 +26,8 @@ for _k, _n in zip(_w[::2], _w[1::2]):
 for _k in range(8):
     SCRATCH["ps%d" % _k] = ("psum", [128, 512], "float32")
 _o = 0
-for _n, _l in ((48, "k1 k2 dd gg gw p1 p2 su ee ew dts od1 od2 kd fs b1 b2 wb hd vf hf h2"), (96, "y0g c1x lt s1 s2"),
-               (8, "t0 bt base fn mx t8 apre c1 hrow np hl key tk tkq i48"), (16, "l16 rk fl fm")):
+for _n, _l in ((48, "k1 k2 dd gg gw p0 p1 p2 su ee ew dts od1 od2 kd fs b1 b2 wb hd vf hf h2"), (96, "y0g c1x lt s1 s2"),
+               (8, "t0 bt base fn mx t8 apre c1 hrow np hl key tk tkq i48 e6 x6 q1"), (16, "l16 rk fl fm")):
     for _k in _l.split():
         ARENA[_k] = (_o, _n)
         _o += _n
@@ -183,6 +183,9 @@ def rank_program(g, core, T, topo):
         for x, y in zip(both(dst, a, a + n), both(src, b, b + n)):
             dma("s", x, y, sem, total)
 
+    def idle():
+        pass
+
     others = [x for x in range(N) if x != me]
 
     def far_of(x):
@@ -298,11 +301,13 @@ def rank_program(g, core, T, topo):
     def sort_ops(src, sp0, sp1, n):
         def lower(a=0, b=192):
             return r(src[0], a, b, 1, 64, 128)
-        ops = [lambda: ts(r("ct", 0, 768, 4), src, sp0, O.is_gt),
-               lambda: tt(r("sm"), src, r("bm"), O.add),
+        left, right = r(src[0], 0, 128), r(src[0], 128, 192)
+        ops = [lambda: ts(r("ct", 0, 512, 4), left, sp0, O.is_gt),
+               lambda: tt(r("sm"), left, r("bm", 0, 128), O.add),
+               lambda: ts(r("ct", 512, 768, 4), right, sp0, O.is_ge),
                lambda: tt(r("sm1", 0, 64, 1, 64), lower(128), r("bm", 64, 128, 1, 64), O.add),
                lambda: ts(r("ct", 1, 768, 4, 64), lower(), sp1, O.is_gt),
-               lambda: ts(r("ct", 2, 768, 4), r("sm"), sp0, O.is_equal),
+               lambda: ts(r("ct", 2, 512, 4), r("sm"), sp0, O.is_equal),
                lambda: ts(r("ct", 515, 768, 4, 64), r("sm1", 0, 64, 1, 64), sp1, O.is_equal)]
         if n > 192:
             ops += [lambda: ts(r("ct", 768, 769), sp0, 0.0, O.is_gt),
@@ -332,25 +337,29 @@ def rank_program(g, core, T, topo):
     lin(r("lf", 17, 18), r("paf", 10, 11), 1.0, r("paf", 8, 9))
     lin(r("lf", 18, 24), r("ir", 0, 6), 1.0, 0.0)
     lin(r("nw", 0, 3), r("m16", 0, 3), 1.0, r("paf", 4, 5))
-    for k in range(4):
-        zero(r("eht", 512 * k, 512 * k + 512), r("onet"))
     lin(r("r8"), r("bi"), 1.0, 0.0, F.Sign)
     lin(r("rsq"), r("r16", 0, 32), 1.0, 0.0, F.Sign)
     lin(r("th"), r("wgt1"), 1.0 / 128, 0.0)
     for x, c in (("key", -1e6), ("base", 0.0), ("c1", 0.0), ("i48", float(K * me))):
         lin(r(x), r("ones", 0, 8), 0.0, c)
     lin(r("ps"), r("ones", 0, 64), 0.0, 99.0)
-    lin(r("sw", 576, 584), r("ones", 0, 8), 0.0, BIG)
+    lin(r("sw", HX, NX), r("ones", 0, 96), 0.0, BIG)
     lin(r("tkq", 0, 1), r("paf", 4, 5), 6.0, 0.0)
     lin(r("tkq", 1, 2), r("paf", 4, 5), 1.0, float(16 * me))
     zero(r("rho", 72, 96), r("ones", 0, 24))
     ts(r("idt"), r("ipd", 0, 128), 0.0, O.is_equal, 0.5, O.mult)
-    for k in range(4):
-        ac(r("eht", 513 * k, 512 * k + 512, 4), r("idt"))
+
+    def blank(a, b):
+        for k in range(a, b):
+            zero(r("eht", 512 * k, 512 * k + 512), r("onet"))
+    blank(0, 2)
 
     tt(r("rdm"), r("ps3", 0, 194), r("wm"), O.mult)
     issue("a", [r("rdm")], [r("junk"), r("msgf", 0, 1)], lambda: A.activation(
         ap(r("junk")), ap(r("rdm")), F.Copy, accum_out=ap(r("msgf", 0, 1))))
+    blank(2, 4)
+    for k in range(4):
+        ac(r("eht", 513 * k, 512 * k + 512, 4), r("idt"))
     my_land = r("land", 8 * me, 8 * me + 1)
     weave(ranks_ops())
     cp(my_land, r("msgf", 0, 1))
@@ -361,59 +370,54 @@ def rank_program(g, core, T, topo):
     for x, y in zip(both("ls", 0, K), both("w0", K * me, K * me + K)):
         spread(x, y, "al")
     move("w0", K * me, "ls", 0, K, "dls")
-    weave(order_ops(r("om", 0, 3), 48, 96))
-    cp(r("lists"), r("lf"))
+    weave(order_ops(r("om", 0, 3), 48, 96),
+          [lambda: qz("nq", 0, 176, r("nzt")), lambda: cp(r("lists"), r("lf")), lambda: fill(r("fb"), -1000000)])
     pick("nb", 0, 48, "tq", 0, 192, r("om", 0, 3), [(0, 192)])
-    fill(r("fb"), -1000000)
-    qz("nq", 0, 176, r("nzt"))
-    qz("eq", 0, 512, r("eht"))
+    qz("eq", 0, 256, r("eht", 0, 1024))
 
     def noise(t):
         for k in range(4):
             mm(4 + k, "eq", 128 * k, "nq", K * t, 128, True, False)
-    noise(0)
     l_mod, l_div, l_mod7, l_div7 = [r("lists", k, k + 3) for k in (0, 4, 8, 12)]
+    six, my_ps, my_dts = (0, 6), r("ps", 8 * me + 7, 8 * me + 8), r("q1", 0, 1)
 
     def places(key, w, even):
-        gather(r("k1"), key, l_mod)
-        gather(r("k2"), key, l_div)
         if even:
-            tt(r("dd"), r("k1"), r("k2"), O.subtract)
-            tt(r("gg"), r("dd"), even, O.is_gt)
+            first = [lambda: tt(r("dd"), r("k1"), r("k2"), O.subtract), lambda: tt(r("gg"), r("dd"), even, O.is_gt)]
         else:
-            tt(r("gg"), r("k1"), r("k2"), O.is_gt)
-        scan(r("ps", 0, 48), r("r8k"), r("gg"))
-        tt(r("gw"), r("gg"), r(w), O.mult)
-        gather(r("p1"), r("ps"), l_mod7)
-        gather(r("p2"), r("ps"), l_div7)
-        tt(r("su"), r("p1"), r("p2"), O.add)
-        ts(r("ee"), r("su"), 5.0, O.is_equal)
-        tt(r("ew"), r("ee"), r("gw"), O.mult)
-        scan(r("dts"), r("r8"), r("ew"), O.mult)
+            first = [lambda: tt(r("gg"), r("k1"), r("k2"), O.is_gt)]
+        return [lambda: gather(r("k1"), key, l_mod), lambda: gather(r("k2"), key, l_div)] + first + [
+            lambda: scan(r("ps", 0, 48), r("r8k"), r("gg")),
+            lambda: tt(r("gw"), r("gg"), r(w), O.mult),
+            lambda: ts(r("e6", *six), r("ps", 7, 48, 8), my_ps, O.add, 5.0, O.is_equal),
+            lambda: tt(r("x6", *six), r("e6", *six), r("gw", 8 * me, 8 * me + 6), O.mult),
+            lambda: issue("v", [r("x6", *six)], [my_dts], lambda: V.tensor_reduce(
+                ap(my_dts), ap(r("x6", *six)), AxisListType.X, O.add))]
 
-    def note_ops(k):
-        return [lambda: tt(r("od1"), r("p1"), r("ai"), O.is_equal), lambda: tt(r("od2"), r("od1"), r("bi"), O.mult),
+    def pairs(p):
+        return [lambda: gather(r(p), r("ps"), l_mod7), lambda: gather(r("p2"), r("ps"), l_div7),
+                lambda: tt(r("su"), r(p), r("p2"), O.add), lambda: ts(r("ee"), r("su"), 5.0, O.is_equal)]
+
+    def note_ops(k, p):
+        return [lambda: tt(r("od1"), r(p), r("ai"), O.is_equal), lambda: tt(r("od2"), r("od1"), r("bi"), O.mult),
                 lambda: scan(r("od1"), r("r8k"), r("od2")), lambda: cp(r("odt", 6 * k, 6 * k + 6), r("od1", 7, 48, 8))]
-
-    own = 8 * me + 7
-    my_dts, my_ps = r("dts", own, own + 1), r("ps", own, own + 1)
-    six = (0, 6)
 
     def anew(buf, off, parts, end):
         pick(buf, 0, 48, "w0", 0, end, off, parts)
         for k in range(4):
             mm(4 + k, "eq", 128 * k, buf, 0, 128, False, True)
 
-    def pack(out, o):
-        for k in range(4):
-            (cp if k % 2 == 0 else ac)(r("vt", k, 192, 4), r("ps%d" % (4 + k), 0, 48))
-        qz(out, o, 128, r("vt"))
+    def pack_ops(out, o):
+        return [lambda k=k: (cp if k % 2 == 0 else ac)(r("vt", k, 192, 4), r("ps%d" % (4 + k), 0, 48)) for k in range(4)] + [
+            lambda: qz(out, o, 128, r("vt"))]
 
+    cp(r("v6", *six), r("land", 0, 48, 8))
     ts(r("hi", *six), r("land", 0, 48, 8), 1.0 / 256, O.mult, -127.5 / 256, O.add)
     issue("g", [r("hi", *six)], [r("fb", *six)], lambda: g.partition_broadcast(
         ap(r("fb", *six)), ap(r("hi", 0, 6, 1, 0, 1)), 128))
-    cp(r("v6", *six), r("land", 0, 48, 8))
-    places(r("fb"), "wgt", r("th"))
+    qz("eq", 256, 256, r("eht", 1024, 2048))
+    noise(0)
+    weave(places(r("fb"), "wgt", r("th")))
     ts(r("oll", 0, 3), r("nw", 0, 3), my_dts, O.add, r("i48", 0, 1), O.add)
 
     dma("s", mdr, r("v6", *six), "dmd")
@@ -423,17 +427,20 @@ def rank_program(g, core, T, topo):
     anew("lb", r("oll", 0, 3), [(0, 288)], 288)
     ts(r("tk", 0, 1), my_ps, 3.0, O.is_ge, 64.0, O.mult)
     ts(r("ox", 0, 3), r("nw", 0, 3), r("tk", 0, 1), O.add)
-    pack("nb", 64)
+    pair = pairs("p0") + [lambda: tt(r("ew"), r("ee"), r("gw"), O.mult), lambda: scan(r("dts"), r("r8"), r("ew"), O.mult)]
+    weave(pair[:3])
+    weave(pack_ops("nb", 64), pair[3:])
     pick("xs", 0, 48, "nb", 0, 192, r("ox", 0, 3), [(0, 48), (64, 192)])
     for x, y in zip(both("xs", 0, K), both("w0", LX + K * me, LX + K * me + K)):
         spread(x, y, "ax")
     move("w0", LX + K * me, "xs", 0, K, "dxs")
     noise(1)
-    weave(order_ops(r("ol", 6, 12), 96, 192))
-    pick("hb", 0, 96, "tq", 0, 192, r("ol", 6, 12), [(0, 192)])
-    for x, y in zip(("hb", "hb_s"), both("hp", 16 * me, 16 * me + 16)):
-        pieces(x, y, "ah")
-    move("hp", 16 * me, "hb", 16 * me, 16, "dhb")
+
+    def highs():
+        pick("hb", 0, 96, "tq", 0, 192, r("ol", 6, 12), [(0, 192)])
+        for x, y in zip(("hb", "hb_s"), both("hp", 16 * me, 16 * me + 16)):
+            pieces(x, y, "ah")
+        move("hp", 16 * me, "hb", 16 * me, 16, "dhb")
     mm(1, "uq", 0, "w0", 0, 288)
     ac(r("sw", 0, 288), r("ps1", 0, 288))
 
@@ -481,7 +488,7 @@ def rank_program(g, core, T, topo):
         lambda: lin(r("c1", *six), r("t0", *six), float(LX), 0.0),
         lambda: tt(r("c1", *six), r("c1", *six), r("c48", *six), O.add),
         lambda: gather(r("c1x"), r("c1"), r("lists", 18, 24))]
-    weave(fit, bases, note_ops(0), where)
+    weave(fit, bases, order_ops(r("ol", 6, 12), 96, 192) + [highs], [idle] * 5 + where)
 
     mm(0, "uq", 0, "w0", LX, 288)
     ts(r("pos"), r("ps0", 0, 288), 0.0, O.is_gt)
@@ -489,41 +496,41 @@ def rank_program(g, core, T, topo):
     scan(r("psc"), r("x48"), r("pos"))
     tt(r("np", *six), r("psc", 47, 288, 48), r("t8", *six), O.mult)
     tt(r("key", *six), r("np", *six), r("apre", *six), O.add)
-    places(r("key"), "wgt1", None)
+    weave(places(r("key"), "wgt1", None), [idle, idle] + note_ops(0, "p0"))
     ts(r("og", 0, 1), r("tkq", 1, 2), my_dts, O.add)
-    tt(r("gw"), r("gg"), r("wb"), O.mult)
-    gather(r("l16"), r("y0g"), r("og", 0, 1))
-    tt(r("ew"), r("ee"), r("gw"), O.mult)
-    ts(r("osl"), r("l16", 0, 12), float(HX), O.min)
-    issue("a", [r("ir"), r("osl")], [r("lrow")], lambda: A.activation(ap(r("lrow")), ap(r("ir")).indirect(ap(r("osl"))), F.Copy))
+    gather(r("osl"), r("y0g"), r("og", 0, 1))
+    issue("a", [r("ir"), r("osl")], [r("lrow")], lambda: A.activation(
+        ap(r("lrow")), ap(r("ir")).indirect(ap(r("osl", 0, 12))), F.Copy))
 
     def hop3():
         pick("hs", 0, 96, "hp", 0, 96, r("oh"), [(0, 96)])
         for x, y in zip(("hs", "hs_s"), both("w0", HX + 16 * me, HX + 16 * me + 16)):
             pieces(x, y, "a3")
         move("w0", HX + 16 * me, "hs", 16 * me, 16, "dhs")
-    weave([lambda: scan(r("hd"), r("r8"), r("ew"), O.mult),
-           lambda: tt(r("hl", *six), r("hd", 7, 48, 8), r("hrow", *six), O.add),
-           lambda: cp(r("oh"), r("hl", *six))],
-          [lambda: gather(r("st"), r("sw"), r("osl")),
+    pair = pairs("p1") + [lambda: tt(r("ew"), r("ee"), r("gw"), O.mult), lambda: scan(r("hd"), r("r8"), r("ew"), O.mult),
+                          lambda: tt(r("hl", *six), r("hd", 7, 48, 8), r("hrow", *six), O.add),
+                          lambda: cp(r("oh"), r("hl", *six)), hop3]
+    weave([lambda: tt(r("gw"), r("gg"), r("wb"), O.mult)] + pair[:4],
+          [lambda: gather(r("st"), r("sw"), r("osl", 0, 12)),
            lambda: gather(r("g32"), r("st"), r("lists", 16, 18)),
            lambda: tt(r("m32"), r("g32"), r("dm", 0, 32), O.mult),
            lambda: scan(r("sq"), r("rsq"), r("m32"), O.mult)])
-    weave(sort_ops(r("st"), r("sq", 15, 16), r("sq", 31, 32, 1, 64), 192))
-    hop3()
-    qz("wq", 0, 256, r("wt"))
-    weave(ranks_ops())
+    weave(sort_ops(r("st"), r("sq", 15, 16), r("sq", 31, 32, 1, 64), 192), pair[4:])
+    weave(ranks_ops(), [lambda: gather(r("l16"), r("y0g"), r("og", 0, 1))] + note_ops(1, "p1")[:2])
     scatter(r("lrow"))
-    weave(order_ops(r("ol1", 0, 3), 0, 48))
+    last = [
+        lambda: ts(r("rk", 0, 12), r("sc", 15, 192, 16), float(NX), O.add),
+        lambda: ts(r("tk", 0, 1), my_dts, 0.0, O.not_equal),
+        lambda: tt(r("rk", 0, 12), r("rk", 0, 12), r("l16", 0, 12), O.subtract),
+        lambda: ts(r("fm", 0, 12), r("sc", 15, 192, 16), 48.0, O.is_lt, r("tk", 0, 1), O.mult),
+        lambda: tt(r("rk", 0, 12), r("rk", 0, 12), r("fm", 0, 12), O.mult),
+        lambda: tt(r("fl", 0, 12), r("rk", 0, 12), r("l16", 0, 12), O.add),
+        lambda: cp(r("ofin"), r("fl", 0, 12))]
+    weave(order_ops(r("ol1", 0, 3), 0, 48), last[:2])
     anew("lc", r("ol1", 0, 3), [(0, 576)], 576)
-    ts(r("tk", 0, 1), my_dts, 0.0, O.not_equal)
-    ts(r("rk", 0, 12), r("sc", 15, 192, 16), float(NX), O.add)
-    ts(r("fm", 0, 12), r("sc", 15, 192, 16), 48.0, O.is_lt, r("tk", 0, 1), O.mult)
-    tt(r("rk", 0, 12), r("rk", 0, 12), r("l16", 0, 12), O.subtract)
-    tt(r("rk", 0, 12), r("rk", 0, 12), r("fm", 0, 12), O.mult)
-    tt(r("fl", 0, 12), r("rk", 0, 12), r("l16", 0, 12), O.add)
-    cp(r("ofin"), r("fl", 0, 12))
-    pack("w0", NX)
+    weave(last[2:], note_ops(1, "p1")[2:])
+    qz("wq", 0, 256, r("wt"))
+    weave(pack_ops("w0", NX))
     pick("fin", 0, 192, "w0", 0, 800, r("ofin"), [(0, 800)])
 
     dma("s", T.oc[:, :], r("fin"), "dout", 128)
@@ -535,7 +542,6 @@ def rank_program(g, core, T, topo):
     dma("s", T.y[:, 0:192], r("ysb", 0, 192), "dout", 128)
     ac(r("ysb", 192, 384), r("ps2", 0, 192))
     dma("a", T.y[:, 192:384], r("ysb", 192, 384), "dout", 128)
-    weave(note_ops(1))
     dma("s", T.od[:, :], r("odt", 0, 12, 1, 0, 1), "dout", 128)
 
     for q in count:

@@ -3,31 +3,34 @@ from concourse.mybir import dt, AluOpType as O, AxisListType, ActivationFunction
 
 P, K, N = 192, 48, 6
 LX, HX, NX = 288, 576, 672
+TH = 32
 BIG = 1e29
 WHOLE = 12582912.0
+STEP = 2048.0
 
 SCRATCH = {"mdr": ("dram", [16, 48], "uint16")}
 ARENA = {}
 for _d, _l in (
-        ("bfloat16", "ut 4 tbt 768 nzt 704 wt 1024 ubt 512 onet 512 eht 2048 vt 512 ct 784 idt 128 r16 192 x48 288 rd 192 sc 192 "
-                     "pos 288 psc 288"),
-        ("int32", "ipd 196 pi 2 pa 12 ia 196 hi 8 fb 8"),
-        ("float32", "ir 800 m16 4 lf 24 bi 48 ai 48 r8k 48 ones 128 paf 12 cf 16 bm 192 dm 192 wm 194 wa 194 nw 4 "
-                    "r8 48 rsq 32 wgt 48 wgt1 48 th 48 c48 8 sm 128 sm1 64 rdm 194 junk 194 prm 192 pd 192 sc2 192 "
-                    "msgf 2 sw 672 st 192 g32 32 m32 32 sq 32 lrow 192 ysb 384 odt 16 ps 64 rho 96 qa 96 qb 96 y0 96"),
-        ("uint16", "land 48 v6 8 rw 48 lists 24 rof 12 ol 12 oll 4 om 4 ox 4 ob 6 og 2 osl 16 oh 6 ol1 4 ofin 12")):
+        ("bfloat16", "ut 4 tbt 768 nzt 704 wt 1024 ubt 512 onet 512 eht 2048 vt 512 ct 784 idt 128 x48 288 pos 288 psc 288"),
+        ("int32", "ipd 196 pi 2 pa 12 ia 32 hi 8 fb 16"),
+        ("float32", "ir 800 m16 4 t16 192 dq 192 ones 128 paf 12 cf 8 cn 16 bm 128 dm 32 wm 194 wa 194 nw 4 nws 4 ogc 2 nr8 8 "
+                    "rsq 32 c48 8 sm 128 sm1 64 rdm 194 junk 194 sc 192 prm 192 sc2 192 "
+                    "msgf 2 sw 672 st 192 m32 32 sq 32 lrow 192 ysb 384 odt 16 rho 96 qa 96 qb 96 y0 96"),
+        ("uint16", "land 48 v6 8 rw 48 l6 6 rof 12 ol 12 oll 4 om 4 ox 4 ob 6 og 2 osl 32 oh 6 ol1 4 ofin 12 pt 8")):
     _w = _l.split()
     for _k, _n in zip(_w[::2], _w[1::2]):
         SCRATCH[_k] = ("sbuf", [128, int(_n)], _d)
-_w = ("tq 192 nq 176 wq 256 uq 128 oneq 128 eq 512 cq 196 ls 48 nb 192 hb 96 hp 96 hs 96 lb 128 lc 128 xs 48 w0 800 fin 192").split()
+_w = ("tq 192 nq 176 wq 256 uq 128 oneq 128 eq 512 cq 196 ls 48 nb 192 hb 96 hp 192 hs 96 lb 128 lc 128 xs 48 w0 800 "
+      "fin 192").split()
 for _k, _n in zip(_w[::2], _w[1::2]):
     SCRATCH[_k] = ("sbuf", [128, int(_n)], "float8_e4m3fn_x4")
     SCRATCH[_k + "_s"] = ("sbuf", [128, int(_n)], "uint8")
 for _k in range(8):
     SCRATCH["ps%d" % _k] = ("psum", [128, 512], "float32")
 _o = 0
-for _n, _l in ((48, "k1 k2 dd gg gw p0 p1 p2 su ee ew dts od1 od2 kd fs b1 b2 wb hd vf hf h2"), (96, "y0g c1x lt s1 s2"),
-               (8, "t0 bt base fn mx t8 apre c1 hrow np hl key tk tkq i48 e6 x6 q1"), (16, "l16 rk fl fm")):
+for _n, _l in ((48, "vf hf h2"), (96, "y0g lt s1 s2"),
+               (16, "key ks zr0 zr1 wr0 wr1 wf wb fa b32 bz l16 rk fl fm"),
+               (8, "gt pl t5 t0 apre fan r96 r144 u1 v1 c1 tk")):
     for _k in _l.split():
         ARENA[_k] = (_o, _n)
         _o += _n
@@ -126,8 +129,11 @@ def rank_program(g, core, T, topo):
         else:
             issue("v", rs, [out], lambda: V.tensor_scalar(ap(out), ap(in0), num(s1), num(s2), op0, op1))
 
-    def tt(out, a, b, op):
-        issue("v", [a, b], [out], lambda: V.tensor_tensor(ap(out), ap(a), ap(b), op))
+    def tt(out, a, b, op, off=None):
+        if off is None:
+            issue("v", [a, b], [out], lambda: V.tensor_tensor(ap(out), ap(a), ap(b), op))
+        else:
+            issue("v", [a, b, off], [out], lambda: V.tensor_tensor(ap(out), ap(a).indirect(ap(off)), ap(b), op))
 
     def cp(out, in_):
         issue("v", [in_], [out], lambda: V.tensor_copy(ap(out), ap(in_)))
@@ -142,8 +148,19 @@ def rank_program(g, core, T, topo):
     def gather(out, win, off):
         issue("v", [win, off], [out], lambda: V.tensor_copy(ap(out), ap(win).indirect(ap(off))))
 
-    def scan(out, keep, add, op0=O.min):
-        issue("v", [keep, add], [out], lambda: V.tensor_tensor_scan(ap(out), ap(keep), ap(add), 0.0, op0, O.add))
+    def gather_a(out, win, off):
+        issue("a", [win, off], [out], lambda: A.activation(ap(out), ap(win).indirect(ap(off)), F.Copy))
+
+    def scatter(win, val, off):
+        issue("v", [val, off], [win], lambda: V.tensor_copy(ap(win).indirect(ap(off)), ap(val)))
+
+    def scan(out, keep, add, op0=O.min, op1=O.add):
+        issue("v", [keep, add], [out], lambda: V.tensor_tensor_scan(ap(out), ap(keep), ap(add), 0.0, op0, op1))
+
+    corr = r("cn", 0, 1)
+
+    def select(out, val, a, b):
+        scan(out, r("dq", a, b), val, O.add, O.max)
 
     def fill(x, c):
         issue("v", [], [x], lambda: V.memset(ap(x), c))
@@ -192,8 +209,12 @@ def rank_program(g, core, T, topo):
         return [y for y in range(N) if topo.chip(T.cores[y]) != topo.chip(T.cores[x])]
     far = far_of(me)
     near = [x for x in others if x not in far]
+    all_eng = topo.engines(core, T.cores[near[0]])
     out_eng = topo.engines(core, T.cores[far[0]])
-    in_eng = [e for e in topo.engines(core, T.cores[near[0]]) if e not in out_eng]
+    in_eng = [e for e in all_eng if e not in out_eng]
+
+    def third(x):
+        return [y for y in range(N) if y not in far_of(x)].index(x)
 
     def mask(es):
         return sum(1 << e for e in es)
@@ -212,30 +233,33 @@ def rank_program(g, core, T, topo):
     def spread(src, to, sem):
         send([(far, out_eng, src, to), (near, in_eng, src, to)], src, sem)
 
-    half = len(in_eng) // 2
+    half, quart = len(in_eng) // 2, len(out_eng) // 4
 
-    def far_share(x, y):
-        k = far_of(x).index(y)
-        n = [4 if j == x % 3 else 2 for j in range(3)]
-        return sum(n[:k]), n[k]
+    def far_n(x, y):
+        return 2 * quart if far_of(x)[x % 3] == y else quart
 
-    def share(y):
+    def share(y, k):
         if y in near:
             k = near.index(y)
             return in_eng[half * k:half * k + half]
-        a, n = far_share(me, y)
-        return out_eng[a:a + n]
+        if y == far[me % 3]:
+            return out_eng[2 * quart * k:2 * quart * k + 2 * quart]
+        i = [z for z in far if z != far[me % 3]].index(y) + 2 * (1 - k)
+        return out_eng[quart * i:quart * i + quart]
 
-    def pieces(name, to, sem):
-        send([([y], share(y), r(name, 16 * y, 16 * y + 16), to) for y in others], r(name), sem)
+    def piece(name, y):
+        return r(name, TH * third(y), TH * third(y) + TH)
 
+    h_all = len(all_eng) // 2
     n_all = sum(len(out_eng) if x in far else len(in_eng) for x in others)
-    n_pcs = sum(half if x in near else far_share(x, me)[1] for x in others)
-    for sem, tot, buf, base, w in (("al", 2 * n_all, "w0", 0, K), ("ax", 2 * n_all, "w0", LX, K), ("ah", 2 * n_pcs, "hp", 0, 16),
-                                   ("a3", 2 * n_pcs, "w0", HX, 16)):
+    n_pcs = sum(half if x in near else far_n(x, me) for x in others)
+    for sem, tot, whom, buf, base, w in (("al", 2 * n_all, others, "w0", lambda x: K * x, K),
+                                         ("ax", 2 * n_all, others, "w0", lambda x: LX + K * x, K),
+                                         ("ah", 2 * n_pcs, others, "hp", lambda x: TH * x, TH),
+                                         ("a3", 2 * h_all * len(near), near, "w0", lambda x: HX + TH * third(x), TH)):
         due[sem] = tot
-        for x in others:
-            for e in both(buf, base + w * x, base + w * x + w):
+        for x in whom:
+            for e in both(buf, base(x), base(x) + w):
                 wrote(e, (sem, tot))
     due["am"] = n_all
     for x in others:
@@ -252,13 +276,8 @@ def rank_program(g, core, T, topo):
     iota(r("pi"), [[0, 2]], 0, 1)
     iota(r("ipd"), [[1, 196]], 0, -1)
     iota(r("ir", 0, 196), [[1, 196]], 0, 0)
-    iota(r("r16"), [[0, 12], [1000, 16]], 0, 0)
+    iota(r("t16"), [[0, 12], [1, 16]], 0, 0)
     iota(r("m16"), [[16, 4]], 0, 0)
-    iota(r("bi"), [[0, 6], [1, 8]], 0, 0)
-    iota(r("ai"), [[1, 6], [0, 8]], 0, 0)
-    iota(r("r8k"), [[0, 6], [1000, 8]], 0, 0)
-    iota(r("wgt"), [[-48, 6], [48, 8]], 0, 0)
-    iota(r("wgt1"), [[-16, 6], [16, 8]], 0, 0)
     iota(r("qa"), [[0, 16], [48, 6]], 240, 0)
     iota(r("qb"), [[0, 16], [-48, 6]], 240, 0)
     iota(r("c48"), [[48, 8]], 0, 0)
@@ -268,86 +287,77 @@ def rank_program(g, core, T, topo):
     fill(r("ones"), 1.0)
     fill(r("onet"), 1.0)
     zero(r("ct", 0, 512), r("onet"))
-    qz("oneq", 0, 128, r("onet"))
     ts(r("pa", 0, 2), r("pi"), 3, O.arith_shift_right)
-    for k, b in enumerate((7, 15, 8, 64, 127)):
-        ts(r("pa", 2 * k + 2, 2 * k + 4), r("pi"), b, O.bitwise_and)
-    ts(r("ia"), r("ipd"), 15, O.bitwise_and)
-    cp(r("paf"), r("pa"))
-    ts(r("bm"), r("ipd", 0, 192), 0.0, O.is_le, 3e29, O.mult)
+    ts(r("pa", 2, 4), r("pi"), 7, O.bitwise_and)
+    ts(r("pa", 4, 6), r("pi"), 15, O.bitwise_and)
+    ts(r("pa", 6, 8), r("pi"), 4, O.arith_shift_right)
+    qz("oneq", 0, 128, r("onet"))
+    cp(r("paf", 0, 8), r("pa", 0, 8))
+    own = r("paf", 4, 5)
+    ts(r("bm"), r("ipd", 0, 128), 0.0, O.is_le, 3e29, O.mult)
     ts(r("cf", 0, 1), r("paf", 2, 3), 16.0, O.mult, r("paf", 0, 1), O.add)
     ts(r("cf", 1, 2), r("paf", 2, 3), 4.0, O.is_ge)
-    ts(r("dm"), r("ia", 0, 192), 0.0, O.is_equal)
-    ts(r("cf", 2, 3), r("cf", 0, 1), -128.0, O.add, r("cf", 1, 2), O.mult)
-    ts(r("wm"), r("ir", 0, 194), r("cf", 0, 1), O.is_equal)
-    ts(r("cf", 3, 4), r("cf", 2, 3), 192.0, O.add)
     for k in range(4):
         if k % 2:
             lin(r("ubt", k, 512, 4), r("ones"), 0.0, r("ut", k, k + 1))
         else:
             ts(r("ubt", k, 512, 4), r("ones"), r("ut", k, k + 1), O.mult)
+    ts(r("cf", 2, 3), r("cf", 0, 1), -128.0, O.add, r("cf", 1, 2), O.mult)
     zero(r("ct", 512, 784), r("onet", 0, 272))
+    lin(r("t16", 0, 192, 16), r("ones", 0, 12), 0.0, -1000.0)
+    lin(r("cn", 1, 2), own, 1.0, 0.5)
+    lin(corr, own, 32.0, -480.0, F.Square)
+    qz("uq", 0, 128, r("ubt"))
+    ts(r("cf", 3, 4), r("cf", 2, 3), 192.0, O.add)
 
     qz("tq", 0, 192, r("tbt"))
-    qz("uq", 0, 128, r("ubt"))
-    mm(1, "tq", 0, "uq", 0, 128)
     mm(0, "uq", 0, "tq", 0, 192)
+    mm(1, "tq", 0, "uq", 0, 128)
     mm(2, "tq", 64, "uq", 0, 128)
+    ts(r("wm"), r("ir", 0, 194), r("cf", 0, 1), O.is_equal)
     ts(r("wa"), r("ir", 0, 194), r("cf", 3, 4), O.is_equal, 256.0, O.mult)
-    tt(r("wm"), r("wm"), r("wa"), O.add)
     move("lb", K, "tq", K, 80, "dpad", 64)
     move("lc", K, "tq", K, 80, "dpad", 64)
 
-    def sort_ops(src, sp0, sp1, n):
-        def lower(a=0, b=192):
-            return r(src[0], a, b, 1, 64, 128)
-        left, right = r(src[0], 0, 128), r(src[0], 128, 192)
-        ops = [lambda: ts(r("ct", 0, 512, 4), left, sp0, O.is_gt),
-               lambda: tt(r("sm"), left, r("bm", 0, 128), O.add),
-               lambda: ts(r("ct", 512, 768, 4), right, sp0, O.is_ge),
-               lambda: tt(r("sm1", 0, 64, 1, 64), lower(128), r("bm", 64, 128, 1, 64), O.add),
-               lambda: ts(r("ct", 1, 768, 4, 64), lower(), sp1, O.is_gt),
-               lambda: ts(r("ct", 2, 512, 4), r("sm"), sp0, O.is_equal),
-               lambda: ts(r("ct", 515, 768, 4, 64), r("sm1", 0, 64, 1, 64), sp1, O.is_equal)]
-        if n > 192:
-            ops += [lambda: ts(r("ct", 768, 769), sp0, 0.0, O.is_gt),
-                    lambda: ts(r("ct", 769, 770, 1, 64), sp1, 0.0, O.is_gt)]
-        return ops + [lambda: qz("cq", 0, n, r("ct", 0, 4 * n)), lambda: mm(3, "oneq", 0, "cq", 0, n)]
+    def lower(src, a=0, b=192):
+        return r(src, a, b, 1, 64, 128)
 
-    def ranks_ops():
-        return [lambda: tt(r("rd"), r("ps3", 0, 192), r("dm"), O.mult), lambda: scan(r("sc"), r("r16"), r("rd")),
-                lambda: cp(r("rof"), r("sc", 15, 192, 16))]
+    def gt_ops(src, sp0, sp1):
+        return [lambda: ts(r("ct", 0, 512, 4), r(src, 0, 128), sp0, O.is_gt),
+                lambda: ts(r("ct", 512, 768, 4), r(src, 128, 192), sp0, O.is_ge),
+                lambda: ts(r("ct", 1, 768, 4, 64), lower(src), sp1, O.is_gt)]
 
-    def scatter(val):
-        issue("v", [val, r("rof")], [r("prm")], lambda: V.tensor_copy(ap(r("prm")).indirect(ap(r("rof"))), ap(val)))
+    def tie0(sp0):
+        ts(r("ct", 2, 512, 4), r("sm"), sp0, O.is_equal)
+
+    def low1(src):
+        tt(r("sm1", 0, 64, 1, 64), lower(src, 128), r("bm", 64, 128, 1, 64), O.add)
+
+    def tie1(sp1):
+        ts(r("ct", 515, 768, 4, 64), r("sm1", 0, 64, 1, 64), sp1, O.is_equal)
+
+    def rank_ops(n):
+        qz("cq", 0, n, r("ct", 0, 4 * n))
+        mm(3, "oneq", 0, "cq", 0, n)
 
     def order_ops(out, a, b):
-        return [lambda: tt(r("pd", a, b), r("prm", a, b), r("dm", a, b), O.mult),
-                lambda: scan(r("sc2", a, b), r("r16", a, b), r("pd", a, b)),
-                lambda: cp(out, r("sc2", a + 15, b, 16))]
+        return [lambda: select(r("sc2", a, b), r("prm", a, b), a, b),
+                lambda: ts(out, r("sc2", a + 15, b, 16), corr, O.subtract)]
 
-    weave(sort_ops(r("ps0", 0, 192), r("ps1", 0, 1), r("ps2", 0, 1, 1, 64), 194))
-
-    lin(r("lf", 0, 4), r("m16"), 0.0, r("paf", 2, 3))
-    lin(r("cf", 5, 6), r("paf", 6, 7), 0.125, 0.0)
-    lin(r("lf", 4, 8), r("m16"), 0.125, r("cf", 5, 6))
-    lin(r("lf", 8, 12), r("lf", 0, 4), 8.0, 7.0)
-    lin(r("lf", 12, 16), r("lf", 4, 8), 8.0, 7.0)
-    lin(r("lf", 16, 17), r("paf", 10, 11), 1.0, 0.0)
-    lin(r("lf", 17, 18), r("paf", 10, 11), 1.0, r("paf", 8, 9))
-    lin(r("lf", 18, 24), r("ir", 0, 6), 1.0, 0.0)
-    lin(r("nw", 0, 3), r("m16", 0, 3), 1.0, r("paf", 4, 5))
-    lin(r("r8"), r("bi"), 1.0, 0.0, F.Sign)
-    lin(r("rsq"), r("r16", 0, 32), 1.0, 0.0, F.Sign)
-    lin(r("th"), r("wgt1"), 1.0 / 128, 0.0)
-    for x, c in (("key", -1e6), ("base", 0.0), ("c1", 0.0), ("i48", float(K * me))):
-        lin(r(x), r("ones", 0, 8), 0.0, c)
-    lin(r("ps"), r("ones", 0, 64), 0.0, 99.0)
-    lin(r("sw", HX, NX), r("ones", 0, 96), 0.0, BIG)
-    lin(r("tkq", 0, 1), r("paf", 4, 5), 6.0, 0.0)
-    lin(r("tkq", 1, 2), r("paf", 4, 5), 1.0, float(16 * me))
-    zero(r("rho", 72, 96), r("ones", 0, 24))
-    ts(r("idt"), r("ipd", 0, 128), 0.0, O.is_equal, 0.5, O.mult)
+    s0, s1 = r("ps1", 0, 1), r("ps2", 0, 1, 1, 64)
+    gts = gt_ops("ps0", s0, s1)
+    tt(r("sm"), r("ps0", 0, 128), r("bm"), O.add)
+    low1("ps0")
+    gts[0]()
+    tie0(s0)
+    gts[1]()
+    ts(r("ct", 768, 769), s0, 0.0, O.is_gt)
+    gts[2]()
+    tie1(s1)
+    ts(r("ct", 769, 770, 1, 64), s1, 0.0, O.is_gt)
+    rank_ops(194)
+    tt(r("wm"), r("wm"), r("wa"), O.add)
+    ts(r("dq"), r("t16"), r("cn", 1, 2), O.subtract, STEP, O.mult)
 
     def blank(a, b):
         for k in range(a, b):
@@ -357,50 +367,60 @@ def rank_program(g, core, T, topo):
     tt(r("rdm"), r("ps3", 0, 194), r("wm"), O.mult)
     issue("a", [r("rdm")], [r("junk"), r("msgf", 0, 1)], lambda: A.activation(
         ap(r("junk")), ap(r("rdm")), F.Copy, accum_out=ap(r("msgf", 0, 1))))
-    blank(2, 4)
-    for k in range(4):
-        ac(r("eht", 513 * k, 512 * k + 512, 4), r("idt"))
     my_land = r("land", 8 * me, 8 * me + 1)
-    weave(ranks_ops())
+    select(r("sc"), r("ps3", 0, 192), 0, 192)
+    ts(r("rof"), r("sc", 15, 192, 16), corr, O.subtract)
     cp(my_land, r("msgf", 0, 1))
     spread(my_land, my_land, "am")
-    scatter(r("ir", 0, 192))
+    scatter(r("prm"), r("ir", 0, 192), r("rof"))
+    ts(r("idt"), r("ipd", 0, 128), 0.0, O.is_equal, 0.5, O.mult)
     weave(order_ops(r("ol", 0, 3), 0, 48))
     pick("ls", 0, 48, "tq", 0, 192, r("ol", 0, 3), [(0, 192)])
     for x, y in zip(both("ls", 0, K), both("w0", K * me, K * me + K)):
         spread(x, y, "al")
     move("w0", K * me, "ls", 0, K, "dls")
-    weave(order_ops(r("om", 0, 3), 48, 96),
-          [lambda: qz("nq", 0, 176, r("nzt")), lambda: cp(r("lists"), r("lf")), lambda: fill(r("fb"), -1000000)])
+
+    six = (0, 6)
+    blank(2, 4)
+    for k in range(4):
+        ac(r("eht", 513 * k, 512 * k + 512, 4), r("idt"))
+    lin(r("nr8", *six), r("ir", *six), -0.125, 0.0)
+    lin(r("key"), r("ones", 0, 16), 0.0, -100.0)
+    lin(r("cn", 2, 3), own, 1.0, -6.0, F.Relu)
+    lin(r("nw", 0, 3), r("m16", 0, 3), 1.0, own)
+    lin(r("nws", 0, 3), r("nw", 0, 3), 1.0 / K, 0.0)
+    weave([lambda: fill(r("fb"), 0)], order_ops(r("om", 0, 3), 48, 96),
+          [idle, lambda: qz("nq", 0, 176, r("nzt"))])
     pick("nb", 0, 48, "tq", 0, 192, r("om", 0, 3), [(0, 192)])
     qz("eq", 0, 256, r("eht", 0, 1024))
+    lin(r("cn", 4, 5), own, 6.0, 0.0)
+    lin(r("cn", 9, 10), own, 1.0, 16.0)
+    lin(r("rho", 72, 96), r("ones", 0, 24), 0.0, 0.0)
+    lin(r("rsq"), r("x48", 0, 32), 0.0, 1.0)
+    lin(r("rsq", 0, 32, 16), r("ones", 0, 2), 0.0, 0.0)
+    lin(r("cn", 6, 7), r("paf", 6, 7), 1.0 / 16, 0.0)
+    lin(r("ogc", 0, 1), own, 1.0 / 16, 0.0)
+    lin(r("sw", HX, NX), r("ones", 0, 96), 0.0, BIG)
 
     def noise(t):
         for k in range(4):
             mm(4 + k, "eq", 128 * k, "nq", K * t, 128, True, False)
-    l_mod, l_div, l_mod7, l_div7 = [r("lists", k, k + 3) for k in (0, 4, 8, 12)]
-    six, my_ps, my_dts = (0, 6), r("ps", 8 * me + 7, 8 * me + 8), r("q1", 0, 1)
 
-    def places(key, w, even):
-        if even:
-            first = [lambda: tt(r("dd"), r("k1"), r("k2"), O.subtract), lambda: tt(r("gg"), r("dd"), even, O.is_gt)]
-        else:
-            first = [lambda: tt(r("gg"), r("k1"), r("k2"), O.is_gt)]
-        return [lambda: gather(r("k1"), key, l_mod), lambda: gather(r("k2"), key, l_div)] + first + [
-            lambda: scan(r("ps", 0, 48), r("r8k"), r("gg")),
-            lambda: tt(r("gw"), r("gg"), r(w), O.mult),
-            lambda: ts(r("e6", *six), r("ps", 7, 48, 8), my_ps, O.add, 5.0, O.is_equal),
-            lambda: tt(r("x6", *six), r("e6", *six), r("gw", 8 * me, 8 * me + 6), O.mult),
-            lambda: issue("v", [r("x6", *six)], [my_dts], lambda: V.tensor_reduce(
-                ap(my_dts), ap(r("x6", *six)), AxisListType.X, O.add))]
+    def places(k):
+        pu, tpu = r("pt", 4 * k, 4 * k + 1), r("pt", 4 * k + 2, 4 * k + 3)
+        pl, t5 = r("pl", k, k + 1), r("t5", k, k + 1)
+        select(r("ks"), r("key"), 0, 16)
+        ts(r("gt", *six), r("key", *six), corr, O.add, r("ks", 15, 16), O.is_gt)
+        issue("v", [r("gt", *six)], [pl], lambda: V.tensor_reduce(ap(pl), ap(r("gt", *six)), AxisListType.X, O.add))
+        ts(pu, pl, r("cn", 2, 3), O.add)
+        ts(t5, pl, -1.0, O.mult, 5.0, O.add)
+        scatter(r("wr%d" % k), r("ir", 0, 16), pu)
+        ts(tpu, t5, pl, O.min)
+        gather(r("zr%d" % k), r("wr%d" % k), tpu)
+        return pu, tpu
 
-    def pairs(p):
-        return [lambda: gather(r(p), r("ps"), l_mod7), lambda: gather(r("p2"), r("ps"), l_div7),
-                lambda: tt(r("su"), r(p), r("p2"), O.add), lambda: ts(r("ee"), r("su"), 5.0, O.is_equal)]
-
-    def note_ops(k, p):
-        return [lambda: tt(r("od1"), r(p), r("ai"), O.is_equal), lambda: tt(r("od2"), r("od1"), r("bi"), O.mult),
-                lambda: scan(r("od1"), r("r8k"), r("od2")), lambda: cp(r("odt", 6 * k, 6 * k + 6), r("od1", 7, 48, 8))]
+    def note(k):
+        ac(r("odt", 6 * k, 6 * k + 6), r("wr%d" % k, *six))
 
     def anew(buf, off, parts, end):
         pick(buf, 0, 48, "w0", 0, end, off, parts)
@@ -408,41 +428,47 @@ def rank_program(g, core, T, topo):
             mm(4 + k, "eq", 128 * k, buf, 0, 128, False, True)
 
     def pack_ops(out, o):
-        return [lambda k=k: (cp if k % 2 == 0 else ac)(r("vt", k, 192, 4), r("ps%d" % (4 + k), 0, 48)) for k in range(4)] + [
+        return [lambda k=k: (cp if k % 2 else ac)(r("vt", k, 192, 4), r("ps%d" % (4 + k), 0, 48)) for k in range(4)] + [
             lambda: qz(out, o, 128, r("vt"))]
 
-    cp(r("v6", *six), r("land", 0, 48, 8))
+    ts(r("cn", 8, 9), own, 1.0, O.is_equal, 4.0 / 16, O.mult)
+    lin(r("ogc", 1, 2), r("cn", 8, 9), 1.0, r("cn", 6, 7))
+    cp(r("l6"), r("ir", *six))
+    ts(r("ia"), r("ipd", 0, 32), 15, O.bitwise_and)
+    ts(r("dm"), r("ia"), 0.0, O.is_equal)
     ts(r("hi", *six), r("land", 0, 48, 8), 1.0 / 256, O.mult, -127.5 / 256, O.add)
     issue("g", [r("hi", *six)], [r("fb", *six)], lambda: g.partition_broadcast(
         ap(r("fb", *six)), ap(r("hi", 0, 6, 1, 0, 1)), 128))
+    cp(r("v6", *six), r("land", 0, 48, 8))
     qz("eq", 256, 256, r("eht", 1024, 2048))
     noise(0)
-    weave(places(r("fb"), "wgt", r("th")))
-    ts(r("oll", 0, 3), r("nw", 0, 3), my_dts, O.add, r("i48", 0, 1), O.add)
+    tt(r("key", *six), r("fb", *six), r("nr8", *six), O.add)
+    pu, tpu = places(0)
+    ts(r("oll", 0, 3), r("nws", 0, 3), r("zr0", me, me + 1), O.add, float(K), O.mult)
 
     dma("s", mdr, r("v6", *six), "dmd")
     for k in range(8):
         dma("s", r("rw", 0, 48, 1, 16 * k, 16 * k + 16), mdr, "drw", 128)
 
-    anew("lb", r("oll", 0, 3), [(0, 288)], 288)
-    ts(r("tk", 0, 1), my_ps, 3.0, O.is_ge, 64.0, O.mult)
+    note(0)
+    ts(r("tk", 0, 1), r("zr0", me, me + 1), float(me), O.not_equal, 64.0, O.mult)
+    scatter(r("wf"), r("fb"), pu)
     ts(r("ox", 0, 3), r("nw", 0, 3), r("tk", 0, 1), O.add)
-    pair = pairs("p0") + [lambda: tt(r("ew"), r("ee"), r("gw"), O.mult), lambda: scan(r("dts"), r("r8"), r("ew"), O.mult)]
-    weave(pair[:3])
-    weave(pack_ops("nb", 64), pair[3:])
+    anew("lb", r("oll", 0, 3), [(0, 288)], 288)
+    gather(r("fa"), r("wf"), tpu)
+    tt(r("t0", *six), r("zr0", *six), r("ir", *six), O.not_equal)
+    weave(pack_ops("nb", 64))
     pick("xs", 0, 48, "nb", 0, 192, r("ox", 0, 3), [(0, 48), (64, 192)])
     for x, y in zip(both("xs", 0, K), both("w0", LX + K * me, LX + K * me + K)):
         spread(x, y, "ax")
     move("w0", LX + K * me, "xs", 0, K, "dxs")
     noise(1)
-
-    def highs():
-        pick("hb", 0, 96, "tq", 0, 192, r("ol", 6, 12), [(0, 192)])
-        for x, y in zip(("hb", "hb_s"), both("hp", 16 * me, 16 * me + 16)):
-            pieces(x, y, "ah")
-        move("hp", 16 * me, "hb", 16 * me, 16, "dhb")
+    weave(order_ops(r("ol", 6, 12), 96, 192), [lambda: ts(r("ob"), r("zr0", *six), r("cn", 4, 5), O.add)])
+    pick("hb", 0, 96, "tq", 0, 192, r("ol", 6, 12), [(0, 192)])
+    for k, (x, y) in enumerate(zip(("hb", "hb_s"), both("hp", TH * me, TH * me + TH))):
+        send([([z], share(z, k), piece(x, z), y) for z in others], r(x), "ah")
+    move("hp", TH * me, "hb", TH * third(me), TH, "dhb")
     mm(1, "uq", 0, "w0", 0, 288)
-    ac(r("sw", 0, 288), r("ps1", 0, 288))
 
     def after_scalar():
         lin(r("hf"), r("hf"), 1.0, WHOLE)
@@ -462,73 +488,74 @@ def rank_program(g, core, T, topo):
         lambda: tt(r("y0"), r("y0"), r("s2"), O.add),
         lambda: gather(r("y0g"), r("y0"), r("ob")),
         lambda: ts(r("lt"), r("y0g"), 48.0, O.is_lt),
-        lambda: tt(r("lt"), r("lt"), r("c1x"), O.mult),
-        lambda: tt(r("y0g"), r("lt"), r("y0g"), O.add)]
+        lambda: tt(r("s1"), r("c1"), r("lt"), O.mult, r("l6")),
+        lambda: tt(r("y0g"), r("s1"), r("y0g"), O.add)]
     fit = [
-        lambda: ts(r("t0", *six), r("ps", 7, 48, 8), 3.0, O.is_ge),
-        lambda: tt(r("kd"), r("ee"), r("gg"), O.mult),
-        lambda: tt(r("kd"), r("kd"), r("dd"), O.mult),
-        lambda: scan(r("fs"), r("r8"), r("kd"), O.mult),
-        lambda: tt(r("fn", *six), r("fs", 7, 48, 8), r("fb", *six), O.add),
-        lambda: lin(r("mx", *six), r("fn", *six), 1.0, float(K - P), F.Relu),
-        lambda: tt(r("mx", *six), r("mx", *six), r("t0", *six), O.mult),
-        lambda: tt(r("fn", *six), r("fn", *six), r("mx", *six), O.subtract),
-        lambda: lin(r("fn", *six), r("fn", *six), 8.0, 0.0),
-        lambda: tt(r("apre", *six), r("fn", *six), r("ir", *six), O.subtract),
-        lambda: lin(r("t8", *six), r("t0", *six), 8.0, 0.0)]
+        lambda: lin(r("r96", *six), r("fa", *six), 1.0, float(K - P + K), F.Relu),
+        lambda: lin(r("r144", *six), r("fa", *six), 1.0, float(K - P), F.Relu),
+        lambda: tt(r("fan", *six), r("fa", *six), r("nr8", *six), O.add),
+        lambda: tt(r("u1", *six), r("r96", *six), r("r144", *six), O.subtract),
+        lambda: tt(r("v1", *six), r("u1", *six), r("r144", *six), O.subtract),
+        lambda: tt(r("fan", *six), r("fan", *six), r("u1", *six), O.subtract),
+        lambda: tt(r("v1", *six), r("v1", *six), r("t0", *six), O.mult),
+        lambda: tt(r("apre", *six), r("fan", *six), r("v1", *six), O.add)]
     bases = [
-        lambda: ts(r("bt", *six), r("dts", 7, 48, 8), 1.0 / 48, O.mult),
-        lambda: tt(r("hi", *six), r("bt", *six), r("ir", *six), O.add),
-        lambda: ts(r("base", *six), r("hi", *six), 16.0, O.mult),
-        lambda: gather(r("b1"), r("base"), l_mod),
-        lambda: gather(r("b2"), r("base"), l_div),
-        lambda: ts(r("ob"), r("base", *six), 1.0 / 16, O.mult, r("tkq", 0, 1), O.add),
-        lambda: tt(r("wb"), r("b1"), r("b2"), O.subtract),
-        lambda: lin(r("hrow", *six), r("base", *six), 1.0, r("paf", 4, 5)),
         lambda: lin(r("c1", *six), r("t0", *six), float(LX), 0.0),
         lambda: tt(r("c1", *six), r("c1", *six), r("c48", *six), O.add),
-        lambda: gather(r("c1x"), r("c1"), r("lists", 18, 24))]
-    weave(fit, bases, order_ops(r("ol", 6, 12), 96, 192) + [highs], [idle] * 5 + where)
+        lambda: lin(r("b32"), r("zr0"), float(TH), 0.0),
+        lambda: ac(r("sw", 0, 288), r("ps1", 0, 288))]
+    weave(where, fit, [idle] * 2 + bases)
 
-    mm(0, "uq", 0, "w0", LX, 288)
-    ts(r("pos"), r("ps0", 0, 288), 0.0, O.is_gt)
-    ac(r("sw", 288, 576), r("ps0", 0, 288))
+    for k, a in ((0, 0), (2, 144)):
+        mm(k, "uq", 0, "w0", LX + a, 144)
+        ts(r("pos", a, a + 144), r("ps%d" % k, 0, 144), 0.0, O.is_gt)
+        ac(r("sw", LX + a, LX + a + 144), r("ps%d" % k, 0, 144))
     scan(r("psc"), r("x48"), r("pos"))
-    tt(r("np", *six), r("psc", 47, 288, 48), r("t8", *six), O.mult)
-    tt(r("key", *six), r("np", *six), r("apre", *six), O.add)
-    weave(places(r("key"), "wgt1", None), [idle, idle] + note_ops(0, "p0"))
-    ts(r("og", 0, 1), r("tkq", 1, 2), my_dts, O.add)
-    gather(r("osl"), r("y0g"), r("og", 0, 1))
-    issue("a", [r("ir"), r("osl")], [r("lrow")], lambda: A.activation(
-        ap(r("lrow")), ap(r("ir")).indirect(ap(r("osl", 0, 12))), F.Copy))
+    tt(r("key", *six), r("psc", 47, 288, 48), r("apre", *six), O.add)
+    pu, tpu = places(1)
+    my_z, ofs = r("zr1", me, me + 1), r("osl", 0, 12)
+    ts(r("og"), r("ogc"), my_z, O.add, 16.0, O.mult)
+    scatter(r("wb"), r("b32"), pu)
+    gather(r("osl"), r("y0g"), r("og"))
+    gather(r("bz"), r("wb"), tpu)
+    tt(r("m32"), r("sw"), r("dm"), O.mult, r("osl", 16, 18))
+    gather_a(r("st"), r("sw"), ofs)
+    tt(r("sm"), r("sw"), r("bm"), O.add, r("osl", 0, 8))
+    scan(r("sq"), r("rsq"), r("m32"), O.mult)
+    gather_a(r("lrow"), r("ir"), ofs)
+    note(1)
+    chip = min([me] + near)
+    ts(r("oh", 0, 6, 2), r("bz", chip, chip + 3), own, O.add)
+    s0, s1 = r("sq", 15, 16), r("sq", 31, 32, 1, 64)
+    gts = gt_ops("st", s0, s1)
+    tie0(s0)
+    ts(r("oh", 1, 6, 2), r("bz", chip, chip + 3), r("cn", 9, 10), O.add)
+    low1("st")
+    gts[0]()
+    gts[1]()
+    tie1(s1)
+    gts[2]()
+    rank_ops(192)
 
-    def hop3():
-        pick("hs", 0, 96, "hp", 0, 96, r("oh"), [(0, 96)])
-        for x, y in zip(("hs", "hs_s"), both("w0", HX + 16 * me, HX + 16 * me + 16)):
-            pieces(x, y, "a3")
-        move("w0", HX + 16 * me, "hs", 16 * me, 16, "dhs")
-    pair = pairs("p1") + [lambda: tt(r("ew"), r("ee"), r("gw"), O.mult), lambda: scan(r("hd"), r("r8"), r("ew"), O.mult),
-                          lambda: tt(r("hl", *six), r("hd", 7, 48, 8), r("hrow", *six), O.add),
-                          lambda: cp(r("oh"), r("hl", *six)), hop3]
-    weave([lambda: tt(r("gw"), r("gg"), r("wb"), O.mult)] + pair[:4],
-          [lambda: gather(r("st"), r("sw"), r("osl", 0, 12)),
-           lambda: gather(r("g32"), r("st"), r("lists", 16, 18)),
-           lambda: tt(r("m32"), r("g32"), r("dm", 0, 32), O.mult),
-           lambda: scan(r("sq"), r("rsq"), r("m32"), O.mult)])
-    weave(sort_ops(r("st"), r("sq", 15, 16), r("sq", 31, 32, 1, 64), 192), pair[4:])
-    weave(ranks_ops(), [lambda: gather(r("l16"), r("y0g"), r("og", 0, 1))] + note_ops(1, "p1")[:2])
-    scatter(r("lrow"))
+    pick("hs", 0, 96, "hp", 0, 192, r("oh"), [(0, 192)])
+    for x, y in zip(("hs", "hs_s"), both("w0", HX + TH * third(me), HX + TH * third(me) + TH)):
+        send([([z], all_eng[h_all * i:h_all * i + h_all], piece(x, z), y) for i, z in enumerate(near)], r(x), "a3")
+    move("w0", HX + TH * third(me), "hs", TH * third(me), TH, "dhs")
+    gather(r("l16"), r("y0g"), r("og", 0, 1))
+    ts(r("tk", 0, 1), my_z, float(me), O.not_equal)
+    select(r("sc"), r("ps3", 0, 192), 0, 192)
+    ts(r("rof"), r("sc", 15, 192, 16), corr, O.subtract)
+    scatter(r("prm"), r("lrow"), r("rof"))
     last = [
-        lambda: ts(r("rk", 0, 12), r("sc", 15, 192, 16), float(NX), O.add),
-        lambda: ts(r("tk", 0, 1), my_dts, 0.0, O.not_equal),
+        lambda: ts(r("rk", 0, 12), r("rof"), float(NX), O.add),
+        lambda: ts(r("fm", 0, 12), r("rof"), 48.0, O.is_lt, r("tk", 0, 1), O.mult),
         lambda: tt(r("rk", 0, 12), r("rk", 0, 12), r("l16", 0, 12), O.subtract),
-        lambda: ts(r("fm", 0, 12), r("sc", 15, 192, 16), 48.0, O.is_lt, r("tk", 0, 1), O.mult),
         lambda: tt(r("rk", 0, 12), r("rk", 0, 12), r("fm", 0, 12), O.mult),
         lambda: tt(r("fl", 0, 12), r("rk", 0, 12), r("l16", 0, 12), O.add),
         lambda: cp(r("ofin"), r("fl", 0, 12))]
     weave(order_ops(r("ol1", 0, 3), 0, 48), last[:2])
     anew("lc", r("ol1", 0, 3), [(0, 576)], 576)
-    weave(last[2:], note_ops(1, "p1")[2:])
+    weave(last[2:])
     qz("wq", 0, 256, r("wt"))
     weave(pack_ops("w0", NX))
     pick("fin", 0, 192, "w0", 0, 800, r("ofin"), [(0, 800)])

@@ -11,16 +11,16 @@ STEP = 2048.0
 SCRATCH = {"mdr": ("dram", [16, 48], "uint16")}
 ARENA = {}
 for _d, _l in (
-        ("bfloat16", "ut 4 tbt 768 nzt 704 wt 1024 ubt 512 onet 512 eht 2048 vt 512 ct 784 idt 128 x48 288 pos 288 psc 288"),
-        ("int32", "ipd 196 pi 2 pa 12 ia 32 hi 8 fb 16"),
-        ("float32", "ir 800 m16 4 t16 192 dq 192 ones 128 paf 12 cf 8 cn 16 bm 128 dm 32 wm 194 wa 194 nw 4 nws 4 ogc 2 nr8 8 "
-                    "rsq 32 c48 8 sm 128 sm1 64 rdm 194 junk 194 sc 192 prm 192 sc2 192 "
+        ("bfloat16", "ut 4 tbt 768 nzt 704 wt 1024 ubt 512 onet 516 eht 516 vt 512 ct 768 idt 128 x48 288 pos 288 psc 288"),
+        ("int32", "ipd 128 pi 2 pa 6 ia 32 hi 8 fb 16"),
+        ("float32", "ir 800 m16 4 t16 192 dq 192 ones 128 paf 6 cn 16 bm 128 dm 32 nw 4 nws 4 ogc 2 nr8 8 "
+                    "rsq 32 c48 8 sm 128 sm1 64 sg 192 sg1 192 sc 192 prm 192 sc2 192 "
                     "msgf 2 sw 672 st 192 m32 32 sq 32 lrow 192 ysb 384 odt 16 rho 96 qa 96 qb 96 y0 96"),
         ("uint16", "land 48 v6 8 rw 48 l6 6 rof 12 ol 12 oll 4 om 4 ox 4 ob 6 og 2 osl 32 oh 6 ol1 4 ofin 12 pt 8")):
     _w = _l.split()
     for _k, _n in zip(_w[::2], _w[1::2]):
         SCRATCH[_k] = ("sbuf", [128, int(_n)], _d)
-_w = ("tq 192 nq 176 wq 256 uq 128 oneq 128 eq 512 cq 196 ls 48 nb 192 hb 96 hp 192 hs 96 lb 128 lc 128 xs 48 w0 800 "
+_w = ("tq 192 nq 176 wq 256 uq 128 oneq 128 eq 512 cq 192 ls 48 nb 192 hb 96 hp 192 hs 96 lb 128 lc 128 xs 48 w0 800 "
       "fin 192").split()
 for _k, _n in zip(_w[::2], _w[1::2]):
     SCRATCH[_k] = ("sbuf", [128, int(_n)], "float8_e4m3fn_x4")
@@ -82,12 +82,13 @@ def rank_program(g, core, T, topo):
         need = {}
         for x in reads + writes:
             bank = SCRATCH[x[0]][0] == "psum"
-            hits = list(wr.get(x[0], ()))
-            if bank or x in writes:
-                hits += rd.get(x[0], ())
+            hits = [(y, tok) for y, tok in wr.get(x[0], ()) if meet(x, y) or bank and tok[0] != "c" + q]
+            if x in writes:
+                hits += [(y, tok) for y, tok in rd.get(x[0], ()) if meet(x, y) or bank and tok[0] != "c" + q]
+            elif bank:
+                hits += [(y, tok) for y, tok in rd.get(x[0], ()) if tok[0] != "c" + q]
             for y, tok in hits:
-                if meet(x, y) or bank and tok[0] != "c" + q:
-                    need[tok[0]] = max(need.get(tok[0], 0), tok[1])
+                need[tok[0]] = max(need.get(tok[0], 0), tok[1])
         for s in sorted(need):
             wait(q, s, need[s])
 
@@ -265,7 +266,6 @@ def rank_program(g, core, T, topo):
     for x in others:
         wrote(r("land", 8 * x, 8 * x + 1), ("am", n_all))
 
-    mdr = ("mdr", 0, 16, 0, 48, 1)
     dma("a", r("tbt"), T.tb[:, :], "dtb")
     dma("s", r("ut"), T.u[:, 0:4], "du")
     dma("s", r("nzt", 0, 384), T.nz[:, :], "dnz", 32)
@@ -274,50 +274,52 @@ def rank_program(g, core, T, topo):
     dma("s", r("wt"), T.w[:, :], "dw")
 
     iota(r("pi"), [[0, 2]], 0, 1)
-    iota(r("ipd"), [[1, 196]], 0, -1)
-    iota(r("ir", 0, 196), [[1, 196]], 0, 0)
+    iota(r("ipd"), [[1, 128]], 0, -1)
     iota(r("t16"), [[0, 12], [1, 16]], 0, 0)
+    iota(r("ir", 0, 192), [[1, 192]], 0, 0)
     iota(r("m16"), [[16, 4]], 0, 0)
     iota(r("qa"), [[0, 16], [48, 6]], 240, 0)
     iota(r("qb"), [[0, 16], [-48, 6]], 240, 0)
     iota(r("c48"), [[48, 8]], 0, 0)
-    iota(r("ir", 196, 800), [[1, 604]], 196, 0)
+    iota(r("ir", 192, 800), [[1, 608]], 192, 0)
     iota(r("x48"), [[0, 6], [1000, 48]], 0, 0)
 
     fill(r("ones"), 1.0)
     fill(r("onet"), 1.0)
-    zero(r("ct", 0, 512), r("onet"))
-    ts(r("pa", 0, 2), r("pi"), 3, O.arith_shift_right)
-    ts(r("pa", 2, 4), r("pi"), 7, O.bitwise_and)
+    zero(r("ct", 0, 512), r("onet", 0, 512))
+    ts(r("pa", 0, 2), r("pi"), 64, O.bitwise_and)
+    ts(r("pa", 2, 4), r("pi"), 4, O.arith_shift_right)
     ts(r("pa", 4, 6), r("pi"), 15, O.bitwise_and)
-    ts(r("pa", 6, 8), r("pi"), 4, O.arith_shift_right)
-    qz("oneq", 0, 128, r("onet"))
-    cp(r("paf", 0, 8), r("pa", 0, 8))
+    qz("oneq", 0, 128, r("onet", 0, 512))
+    cp(r("paf"), r("pa"))
     own = r("paf", 4, 5)
-    ts(r("bm"), r("ipd", 0, 128), 0.0, O.is_le, 3e29, O.mult)
-    ts(r("cf", 0, 1), r("paf", 2, 3), 16.0, O.mult, r("paf", 0, 1), O.add)
-    ts(r("cf", 1, 2), r("paf", 2, 3), 4.0, O.is_ge)
+    ts(r("bm"), r("ipd"), 0.0, O.is_le, 3e29, O.mult)
     for k in range(4):
         if k % 2:
             lin(r("ubt", k, 512, 4), r("ones"), 0.0, r("ut", k, k + 1))
         else:
             ts(r("ubt", k, 512, 4), r("ones"), r("ut", k, k + 1), O.mult)
-    ts(r("cf", 2, 3), r("cf", 0, 1), -128.0, O.add, r("cf", 1, 2), O.mult)
-    zero(r("ct", 512, 784), r("onet", 0, 272))
+    zero(r("ct", 512, 768), r("onet", 0, 256))
     lin(r("t16", 0, 192, 16), r("ones", 0, 12), 0.0, -1000.0)
     lin(r("cn", 1, 2), own, 1.0, 0.5)
     lin(corr, own, 32.0, -480.0, F.Square)
+    lin(r("cn", 10, 11), r("paf", 0, 1), -4.0, 256.0)
+    lin(r("cn", 11, 12), r("paf", 0, 1), 4.0, 0.0)
+    zero(r("eht"), r("onet"))
     qz("uq", 0, 128, r("ubt"))
-    ts(r("cf", 3, 4), r("cf", 2, 3), 192.0, O.add)
 
     qz("tq", 0, 192, r("tbt"))
     mm(0, "uq", 0, "tq", 0, 192)
     mm(1, "tq", 0, "uq", 0, 128)
     mm(2, "tq", 64, "uq", 0, 128)
-    ts(r("wm"), r("ir", 0, 194), r("cf", 0, 1), O.is_equal)
-    ts(r("wa"), r("ir", 0, 194), r("cf", 3, 4), O.is_equal, 256.0, O.mult)
+    mm(6, "uq", 0, "tq", 0, 192)
+    ts(r("dq"), r("t16"), r("cn", 1, 2), O.subtract, STEP, O.mult)
     move("lb", K, "tq", K, 80, "dpad", 64)
     move("lc", K, "tq", K, 80, "dpad", 64)
+
+    lin(r("sg"), r("ps6", 0, 192), 1.0, 0.0, F.Sign)
+    issue("a", [r("sg")], [r("sg1"), r("msgf", 0, 1)], lambda: A.activation(
+        ap(r("sg1")), ap(r("sg")), F.Relu, accum_out=ap(r("msgf", 0, 1))))
 
     def lower(src, a=0, b=192):
         return r(src, a, b, 1, 64, 128)
@@ -336,9 +338,9 @@ def rank_program(g, core, T, topo):
     def tie1(sp1):
         ts(r("ct", 515, 768, 4, 64), r("sm1", 0, 64, 1, 64), sp1, O.is_equal)
 
-    def rank_ops(n):
-        qz("cq", 0, n, r("ct", 0, 4 * n))
-        mm(3, "oneq", 0, "cq", 0, n)
+    def rank_ops():
+        qz("cq", 0, 192, r("ct"))
+        mm(3, "oneq", 0, "cq", 0, 192)
 
     def order_ops(out, a, b):
         return [lambda: select(r("sc2", a, b), r("prm", a, b), a, b),
@@ -351,29 +353,21 @@ def rank_program(g, core, T, topo):
     gts[0]()
     tie0(s0)
     gts[1]()
-    ts(r("ct", 768, 769), s0, 0.0, O.is_gt)
     gts[2]()
     tie1(s1)
-    ts(r("ct", 769, 770, 1, 64), s1, 0.0, O.is_gt)
-    rank_ops(194)
-    tt(r("wm"), r("wm"), r("wa"), O.add)
-    ts(r("dq"), r("t16"), r("cn", 1, 2), O.subtract, STEP, O.mult)
+    rank_ops()
+    mm(4, "cq", 0, "oneq", 0, 128)
+    mm(5, "cq", 64, "oneq", 0, 128)
+    ts(r("idt"), r("ipd"), 0.0, O.is_equal, 0.5, O.mult)
+    ac(r("eht", 3, 515, 4), r("idt"))
 
-    def blank(a, b):
-        for k in range(a, b):
-            zero(r("eht", 512 * k, 512 * k + 512), r("onet"))
-    blank(0, 2)
-
-    tt(r("rdm"), r("ps3", 0, 194), r("wm"), O.mult)
-    issue("a", [r("rdm")], [r("junk"), r("msgf", 0, 1)], lambda: A.activation(
-        ap(r("junk")), ap(r("rdm")), F.Copy, accum_out=ap(r("msgf", 0, 1))))
     my_land = r("land", 8 * me, 8 * me + 1)
     select(r("sc"), r("ps3", 0, 192), 0, 192)
+    ts(r("msgf", 1, 2), r("msgf", 0, 1), r("cn", 10, 11), O.mult, r("ps4", 0, 1), O.add)
     ts(r("rof"), r("sc", 15, 192, 16), corr, O.subtract)
-    cp(my_land, r("msgf", 0, 1))
+    ts(my_land, r("ps5", 0, 1), r("cn", 11, 12), O.mult, r("msgf", 1, 2), O.add)
     spread(my_land, my_land, "am")
     scatter(r("prm"), r("ir", 0, 192), r("rof"))
-    ts(r("idt"), r("ipd", 0, 128), 0.0, O.is_equal, 0.5, O.mult)
     weave(order_ops(r("ol", 0, 3), 0, 48))
     pick("ls", 0, 48, "tq", 0, 192, r("ol", 0, 3), [(0, 192)])
     for x, y in zip(both("ls", 0, K), both("w0", K * me, K * me + K)):
@@ -381,9 +375,6 @@ def rank_program(g, core, T, topo):
     move("w0", K * me, "ls", 0, K, "dls")
 
     six = (0, 6)
-    blank(2, 4)
-    for k in range(4):
-        ac(r("eht", 513 * k, 512 * k + 512, 4), r("idt"))
     lin(r("nr8", *six), r("ir", *six), -0.125, 0.0)
     lin(r("key"), r("ones", 0, 16), 0.0, -100.0)
     lin(r("cn", 2, 3), own, 1.0, -6.0, F.Relu)
@@ -392,15 +383,17 @@ def rank_program(g, core, T, topo):
     weave([lambda: fill(r("fb"), 0)], order_ops(r("om", 0, 3), 48, 96),
           [idle, lambda: qz("nq", 0, 176, r("nzt"))])
     pick("nb", 0, 48, "tq", 0, 192, r("om", 0, 3), [(0, 192)])
-    qz("eq", 0, 256, r("eht", 0, 1024))
     lin(r("cn", 4, 5), own, 6.0, 0.0)
     lin(r("cn", 9, 10), own, 1.0, 16.0)
     lin(r("rho", 72, 96), r("ones", 0, 24), 0.0, 0.0)
     lin(r("rsq"), r("x48", 0, 32), 0.0, 1.0)
     lin(r("rsq", 0, 32, 16), r("ones", 0, 2), 0.0, 0.0)
-    lin(r("cn", 6, 7), r("paf", 6, 7), 1.0 / 16, 0.0)
+    lin(r("cn", 6, 7), r("paf", 2, 3), 1.0 / 16, 0.0)
     lin(r("ogc", 0, 1), own, 1.0 / 16, 0.0)
     lin(r("sw", HX, NX), r("ones", 0, 96), 0.0, BIG)
+
+    def unit(k):
+        qz("eq", 128 * k, 128, r("eht", 3 - k, 515 - k))
 
     def noise(t):
         for k in range(4):
@@ -431,6 +424,9 @@ def rank_program(g, core, T, topo):
         return [lambda k=k: (cp if k % 2 else ac)(r("vt", k, 192, 4), r("ps%d" % (4 + k), 0, 48)) for k in range(4)] + [
             lambda: qz(out, o, 128, r("vt"))]
 
+    unit(0)
+    unit(1)
+    unit(2)
     ts(r("cn", 8, 9), own, 1.0, O.is_equal, 4.0 / 16, O.mult)
     lin(r("ogc", 1, 2), r("cn", 8, 9), 1.0, r("cn", 6, 7))
     cp(r("l6"), r("ir", *six))
@@ -440,15 +436,16 @@ def rank_program(g, core, T, topo):
     issue("g", [r("hi", *six)], [r("fb", *six)], lambda: g.partition_broadcast(
         ap(r("fb", *six)), ap(r("hi", 0, 6, 1, 0, 1)), 128))
     cp(r("v6", *six), r("land", 0, 48, 8))
-    qz("eq", 256, 256, r("eht", 1024, 2048))
+    unit(3)
     noise(0)
     tt(r("key", *six), r("fb", *six), r("nr8", *six), O.add)
     pu, tpu = places(0)
     ts(r("oll", 0, 3), r("nws", 0, 3), r("zr0", me, me + 1), O.add, float(K), O.mult)
 
-    dma("s", mdr, r("v6", *six), "dmd")
     for k in range(8):
-        dma("s", r("rw", 0, 48, 1, 16 * k, 16 * k + 16), mdr, "drw", 128)
+        dma("s", ("mdr", 0, 16, 6 * k, 6 * k + 6, 1), r("v6", 0, 6, 1, 16 * k, 16 * k + 16), "dmd", 128)
+    for k in range(8):
+        dma("s", r("rw", 0, 48, 1, 16 * k, 16 * k + 16), ("mdr", 0, 16, 0, 48, 1), "drw", 128)
 
     note(0)
     ts(r("tk", 0, 1), r("zr0", me, me + 1), float(me), O.not_equal, 64.0, O.mult)
@@ -524,27 +521,27 @@ def rank_program(g, core, T, topo):
     scan(r("sq"), r("rsq"), r("m32"), O.mult)
     gather_a(r("lrow"), r("ir"), ofs)
     note(1)
-    chip = min([me] + near)
-    ts(r("oh", 0, 6, 2), r("bz", chip, chip + 3), own, O.add)
     s0, s1 = r("sq", 15, 16), r("sq", 31, 32, 1, 64)
     gts = gt_ops("st", s0, s1)
-    tie0(s0)
-    ts(r("oh", 1, 6, 2), r("bz", chip, chip + 3), r("cn", 9, 10), O.add)
     low1("st")
+    tie0(s0)
     gts[0]()
     gts[1]()
-    tie1(s1)
     gts[2]()
-    rank_ops(192)
+    tie1(s1)
+    rank_ops()
 
+    chip = min([me] + near)
+    ts(r("oh", 0, 6, 2), r("bz", chip, chip + 3), own, O.add)
+    ts(r("oh", 1, 6, 2), r("bz", chip, chip + 3), r("cn", 9, 10), O.add)
     pick("hs", 0, 96, "hp", 0, 192, r("oh"), [(0, 192)])
     for x, y in zip(("hs", "hs_s"), both("w0", HX + TH * third(me), HX + TH * third(me) + TH)):
         send([([z], all_eng[h_all * i:h_all * i + h_all], piece(x, z), y) for i, z in enumerate(near)], r(x), "a3")
     move("w0", HX + TH * third(me), "hs", TH * third(me), TH, "dhs")
-    gather(r("l16"), r("y0g"), r("og", 0, 1))
-    ts(r("tk", 0, 1), my_z, float(me), O.not_equal)
     select(r("sc"), r("ps3", 0, 192), 0, 192)
+    gather(r("l16"), r("y0g"), r("og", 0, 1))
     ts(r("rof"), r("sc", 15, 192, 16), corr, O.subtract)
+    ts(r("tk", 0, 1), my_z, float(me), O.not_equal)
     scatter(r("prm"), r("lrow"), r("rof"))
     last = [
         lambda: ts(r("rk", 0, 12), r("rof"), float(NX), O.add),

@@ -2,25 +2,25 @@ from concourse.bass import DstId, RemoteDMATransfer
 from concourse.mybir import dt, AluOpType as O, AxisListType, ActivationFunctionType as F
 
 P, K, N = 192, 48, 6
-LX, HX, NX = 288, 576, 672
-TH = 32
+LX, HX, NX = 288, 576, 960
+TH = 96
 BIG = 1e29
-WHOLE = 12582912.0
 STEP = 2048.0
 
 SCRATCH = {"mdr": ("dram", [16, 48], "uint16")}
 ARENA = {}
 for _d, _l in (
-        ("bfloat16", "ut 4 tbt 768 nzt 704 wt 1024 ubt 512 onet 516 eht 516 vt 512 ct 768 idt 128 x48 288 pos 288 psc 288"),
-        ("int32", "ipd 128 pi 2 pa 6 ia 32 hi 8 fb 16"),
-        ("float32", "ir 800 m16 4 t16 192 dq 192 ones 128 paf 6 cn 16 bm 128 dm 32 nw 4 nws 4 ogc 2 nr8 8 "
+        ("bfloat16", "ut 4 tbt 768 nzt 704 wt 1024 ubt 512 onet 516 eht 516 vt 512 vn 768 ct 768 idt 128 x48 288 pos 288 psc 288"),
+        ("int32", "ipd 128 pi 2 pa 6 ia 32 hi 8 fb 16 hw 54"),
+        ("float32", "ir 800 m16 4 t16 192 dq 192 ones 128 paf 6 cn 16 bm 128 dm 32 nw 4 nws 4 nr8 8 "
                     "rsq 32 c48 8 sm 128 sm1 64 sg 192 sg1 192 sc 192 prm 192 sc2 192 "
-                    "msgf 2 sw 672 st 192 m32 32 sq 32 lrow 192 ysb 384 odt 16 rho 96 qa 96 qb 96 y0 96"),
-        ("uint16", "land 48 v6 8 rw 48 l6 6 rof 12 ol 12 oll 4 om 4 ox 4 ob 6 og 2 osl 32 oh 6 ol1 4 ofin 12 pt 8")):
+                    "msgf 2 sw 968 dn 192 d0 192 d1 192 g2 192 g3 192 v1r 16 rke 16 cnx 12 n6 6 bzf 16 sgn 192 "
+                    "st 192 m32 32 sq 32 ysb 384 odt 16 rho 96 hq 16 ca 96 hb 96 hc 96 sb 96 sd 96 rg 96 pio 4"),
+        ("uint16", "land 48 v6 8 rw 54 l6 6 rof 12 ol 12 oll 4 om 4 ox 4 ob 6 zg 16 osl 16 oh 12 ofz 12 roc 12 ofin 12 pt 8")):
     _w = _l.split()
     for _k, _n in zip(_w[::2], _w[1::2]):
         SCRATCH[_k] = ("sbuf", [128, int(_n)], _d)
-_w = ("tq 192 nq 176 wq 256 uq 128 oneq 128 eq 512 cq 192 ls 48 nb 192 hb 96 hp 192 hs 96 lb 128 lc 128 xs 48 w0 800 "
+_w = ("tq 192 nq 176 wq 256 uq 128 oneq 128 eq 512 cq 192 ls 48 nb 192 hp 192 hs 192 lb 128 tz 192 xs 48 w0 1152 "
       "fin 192").split()
 for _k, _n in zip(_w[::2], _w[1::2]):
     SCRATCH[_k] = ("sbuf", [128, int(_n)], "float8_e4m3fn_x4")
@@ -28,16 +28,16 @@ for _k, _n in zip(_w[::2], _w[1::2]):
 for _k in range(8):
     SCRATCH["ps%d" % _k] = ("psum", [128, 512], "float32")
 _o = 0
-for _n, _l in ((48, "vf hf h2"), (96, "y0g lt s1 s2"),
-               (16, "key ks zr0 zr1 wr0 wr1 wf wb fa b32 bz l16 rk fl fm"),
-               (8, "gt pl t5 t0 apre fan r96 r144 u1 v1 c1 tk")):
+for _n, _l in ((54, "vf h2"), (96, "y0g yt"),
+               (16, "key ks zr0 zr1 wr0 wr1 wf wb wc cz fa b32 l16 dlt fl fm"),
+               (8, "gt pl t5 t0 apre fan r96 r144 u1 v1 c1 bz cb hb2 hc2 tk")):
     for _k in _l.split():
         ARENA[_k] = (_o, _n)
-        _o += _n
+        _o += _n + (-_n) % 8
 SCRATCH["ar"] = ("sbuf", [128, _o], "float32")
 
-DMAS = ["du", "dtb", "dnz", "dw", "dpv", "dpad", "dls", "dhb", "dmd", "drw", "dxs", "dhs", "dout"]
-SEMAPHORES = ["cv", "ca", "ct", "cg", "am", "al", "ah", "ax", "a3", "left"] + DMAS
+DMAS = ["du", "dtb", "dnz", "dw", "dpv", "dpad", "dls", "dhb", "dmd", "drw", "dxs", "dout"]
+SEMAPHORES = ["cv", "ca", "ct", "cg", "am", "al", "ah", "ax", "an", "a3", "left"] + DMAS
 
 
 def r(name, a=0, b=None, step=1, p=0, q=128):
@@ -149,8 +149,8 @@ def rank_program(g, core, T, topo):
     def gather(out, win, off):
         issue("v", [win, off], [out], lambda: V.tensor_copy(ap(out), ap(win).indirect(ap(off))))
 
-    def gather_a(out, win, off):
-        issue("a", [win, off], [out], lambda: A.activation(ap(out), ap(win).indirect(ap(off)), F.Copy))
+    def gather_a(out, win, off, scale=1.0):
+        issue("a", [win, off], [out], lambda: A.activation(ap(out), ap(win).indirect(ap(off)), F.Identity, scale=scale))
 
     def scatter(win, val, off):
         issue("v", [val, off], [win], lambda: V.tensor_copy(ap(win).indirect(ap(off)), ap(val)))
@@ -204,6 +204,8 @@ def rank_program(g, core, T, topo):
     def idle():
         pass
 
+    sh = me % 2
+    e6, em = (sh, sh + 6), me + sh
     others = [x for x in range(N) if x != me]
 
     def far_of(x):
@@ -216,6 +218,7 @@ def rank_program(g, core, T, topo):
 
     def third(x):
         return [y for y in range(N) if y not in far_of(x)].index(x)
+    mate = [x for x in far if third(x) == third(me)][0]
 
     def mask(es):
         return sum(1 << e for e in es)
@@ -224,39 +227,22 @@ def rank_program(g, core, T, topo):
         a = topo.addr(T.cores[x])
         return DstId(rid=a[0], pnc=a[1])
 
-    def send(transfers, src, sem):
+    def send(transfers, src):
         before("g", [src], [])
         due["left"] = due.get("left", 0) + sum(len(e[1]) for e in transfers)
         g.remote_dma_fused([RemoteDMATransfer(dst_ids=[dst(y) for y in x], dma_engine_mask=mask(es), remote_sem=T.sem[sem],
-                                              srcs=[ap(s)], dsts=[ap(to)] * len(x)) for x, es, s, to in transfers],
+                                              srcs=[ap(s)], dsts=[ap(to)] * len(x)) for x, es, s, to, sem in transfers],
                            local_sem=T.sem["left"])
 
-    def spread(src, to, sem):
-        send([(far, out_eng, src, to), (near, in_eng, src, to)], src, sem)
-
-    half, quart = len(in_eng) // 2, len(out_eng) // 4
-
-    def far_n(x, y):
-        return 2 * quart if far_of(x)[x % 3] == y else quart
-
-    def share(y, k):
-        if y in near:
-            k = near.index(y)
-            return in_eng[half * k:half * k + half]
-        if y == far[me % 3]:
-            return out_eng[2 * quart * k:2 * quart * k + 2 * quart]
-        i = [z for z in far if z != far[me % 3]].index(y) + 2 * (1 - k)
-        return out_eng[quart * i:quart * i + quart]
-
-    def piece(name, y):
-        return r(name, TH * third(y), TH * third(y) + TH)
+    def spread(src, to, sem, sem2=None):
+        send([(far, out_eng, src, to, sem), (near, in_eng, src, to, sem2 or sem)], src)
 
     h_all = len(all_eng) // 2
     n_all = sum(len(out_eng) if x in far else len(in_eng) for x in others)
-    n_pcs = sum(half if x in near else far_n(x, me) for x in others)
     for sem, tot, whom, buf, base, w in (("al", 2 * n_all, others, "w0", lambda x: K * x, K),
-                                         ("ax", 2 * n_all, others, "w0", lambda x: LX + K * x, K),
-                                         ("ah", 2 * n_pcs, others, "hp", lambda x: TH * x, TH),
+                                         ("ax", 2 * len(out_eng) * len(far), far, "w0", lambda x: LX + K * x, K),
+                                         ("an", 2 * len(in_eng) * len(near), near, "w0", lambda x: LX + K * x, K),
+                                         ("ah", 2 * len(out_eng), [mate], "hp", lambda x: TH, TH),
                                          ("a3", 2 * h_all * len(near), near, "w0", lambda x: HX + TH * third(x), TH)):
         due[sem] = tot
         for x in whom:
@@ -266,8 +252,8 @@ def rank_program(g, core, T, topo):
     for x in others:
         wrote(r("land", 8 * x, 8 * x + 1), ("am", n_all))
 
-    dma("a", r("tbt"), T.tb[:, :], "dtb")
     dma("s", r("ut"), T.u[:, 0:4], "du")
+    dma("s", r("tbt"), T.tb[:, :], "dtb")
     dma("s", r("nzt", 0, 384), T.nz[:, :], "dnz", 32)
     dma("s", r("nzt", 384, 704), T.nz[:, 0:320], "dnz", 32)
     dma("s", r("vt", 192, 512), T.tb[:, 0:320], "dpv")
@@ -278,9 +264,10 @@ def rank_program(g, core, T, topo):
     iota(r("t16"), [[0, 12], [1, 16]], 0, 0)
     iota(r("ir", 0, 192), [[1, 192]], 0, 0)
     iota(r("m16"), [[16, 4]], 0, 0)
-    iota(r("qa"), [[0, 16], [48, 6]], 240, 0)
-    iota(r("qb"), [[0, 16], [-48, 6]], 240, 0)
+    iota(r("n6"), [[16, 6]], 0, 0)
     iota(r("c48"), [[48, 8]], 0, 0)
+    iota(r("rke"), [[1, 16]], -sh, 0)
+    iota(r("cnx"), [[16, 12]], NX, 0)
     iota(r("ir", 192, 800), [[1, 608]], 192, 0)
     iota(r("x48"), [[0, 6], [1000, 48]], 0, 0)
 
@@ -294,11 +281,15 @@ def rank_program(g, core, T, topo):
     cp(r("paf"), r("pa"))
     own = r("paf", 4, 5)
     ts(r("bm"), r("ipd"), 0.0, O.is_le, 3e29, O.mult)
+    for k, (a, b) in enumerate(((7.5, 1.0), (11.5, -5.0), (12.5, 4.0))):
+        ts(r("pio", k, k + 1), own, a, O.is_gt, b, O.mult)
+    for k in range(3):
+        tt(r("pio", 3, 4), r("pio", k, k + 1), r("pio", 3, 4) if k else own, O.add)
     for k in range(4):
         if k % 2:
             lin(r("ubt", k, 512, 4), r("ones"), 0.0, r("ut", k, k + 1))
         else:
-            ts(r("ubt", k, 512, 4), r("ones"), r("ut", k, k + 1), O.mult)
+            ts(r("ubt", k, 512, 4), r("onet", 0, 128), r("ut", k, k + 1), O.mult)
     zero(r("ct", 512, 768), r("onet", 0, 256))
     lin(r("t16", 0, 192, 16), r("ones", 0, 12), 0.0, -1000.0)
     lin(r("cn", 1, 2), own, 1.0, 0.5)
@@ -314,8 +305,7 @@ def rank_program(g, core, T, topo):
     mm(2, "tq", 64, "uq", 0, 128)
     mm(6, "uq", 0, "tq", 0, 192)
     ts(r("dq"), r("t16"), r("cn", 1, 2), O.subtract, STEP, O.mult)
-    move("lb", K, "tq", K, 80, "dpad", 64)
-    move("lc", K, "tq", K, 80, "dpad", 64)
+    move("lb", K, "tq", K, 80, "dpad", 32)
 
     lin(r("sg"), r("ps6", 0, 192), 1.0, 0.0, F.Sign)
     issue("a", [r("sg")], [r("sg1"), r("msgf", 0, 1)], lambda: A.activation(
@@ -384,36 +374,44 @@ def rank_program(g, core, T, topo):
           [idle, lambda: qz("nq", 0, 176, r("nzt"))])
     pick("nb", 0, 48, "tq", 0, 192, r("om", 0, 3), [(0, 192)])
     lin(r("cn", 4, 5), own, 6.0, 0.0)
-    lin(r("cn", 9, 10), own, 1.0, 16.0)
-    lin(r("rho", 72, 96), r("ones", 0, 24), 0.0, 0.0)
+    lin(r("v1r"), r("rke"), 16.0, r("pio", 3, 4))
+    lin(r("cn", 6, 7), corr, 1.0, float(K))
+    lin(r("cn", 7, 8), r("ones", 0, 1), 0.0, 0.5 - K)
+    lin(r("cn", 8, 9), r("ones", 0, 1), 0.0, 0.5 - 2 * K)
+    lin(r("cn", 9, 10), r("pio", 3, 4), 1.0, 16.0 * me)
+    zero(r("hq"), r("ones", 0, 16))
+    for x in range(N):
+        lin(r("hq", x + sh, x + sh + 1), r("ones", 0, 1), 0.0, float(HX + TH * (3 if x == mate else third(x)) - 2 * K))
+    lin(r("cnx"), r("cnx"), 1.0, own)
+    lin(r("rho", 84, 96), r("ones", 0, 12), 0.0, 0.0)
     lin(r("rsq"), r("x48", 0, 32), 0.0, 1.0)
     lin(r("rsq", 0, 32, 16), r("ones", 0, 2), 0.0, 0.0)
-    lin(r("cn", 6, 7), r("paf", 2, 3), 1.0 / 16, 0.0)
-    lin(r("ogc", 0, 1), own, 1.0 / 16, 0.0)
-    lin(r("sw", HX, NX), r("ones", 0, 96), 0.0, BIG)
+    lin(r("sw", HX, NX + 8), r("ir", 0, 392), 0.0, BIG)
 
     def unit(k):
         qz("eq", 128 * k, 128, r("eht", 3 - k, 515 - k))
 
-    def noise(t):
+    def noise(t, stop):
         for k in range(4):
-            mm(4 + k, "eq", 128 * k, "nq", K * t, 128, True, False)
+            mm(4 + k, "eq", 128 * k, "nq", K * t, 128, True, stop)
 
-    def places(k):
+    def places(k, val, zr):
         pu, tpu = r("pt", 4 * k, 4 * k + 1), r("pt", 4 * k + 2, 4 * k + 3)
         pl, t5 = r("pl", k, k + 1), r("t5", k, k + 1)
         select(r("ks"), r("key"), 0, 16)
-        ts(r("gt", *six), r("key", *six), corr, O.add, r("ks", 15, 16), O.is_gt)
+        ts(r("gt", *six), r("key", *e6), corr, O.add, r("ks", 15, 16), O.is_gt)
         issue("v", [r("gt", *six)], [pl], lambda: V.tensor_reduce(ap(pl), ap(r("gt", *six)), AxisListType.X, O.add))
         ts(pu, pl, r("cn", 2, 3), O.add)
         ts(t5, pl, -1.0, O.mult, 5.0, O.add)
-        scatter(r("wr%d" % k), r("ir", 0, 16), pu)
+        scatter(r("wr%d" % k), val, pu)
         ts(tpu, t5, pl, O.min)
-        gather(r("zr%d" % k), r("wr%d" % k), tpu)
+        if k:
+            scatter(r("wb"), r("b32"), pu)
+        gather(zr, r("wr%d" % k), tpu)
         return pu, tpu
 
-    def note(k):
-        ac(r("odt", 6 * k, 6 * k + 6), r("wr%d" % k, *six))
+    def note(k, scale):
+        lin(r("odt", 6 * k, 6 * k + 6), r("wr%d" % k, *six), scale, 0.0)
 
     def anew(buf, off, parts, end):
         pick(buf, 0, 48, "w0", 0, end, off, parts)
@@ -427,70 +425,54 @@ def rank_program(g, core, T, topo):
     unit(0)
     unit(1)
     unit(2)
-    ts(r("cn", 8, 9), own, 1.0, O.is_equal, 4.0 / 16, O.mult)
-    lin(r("ogc", 1, 2), r("cn", 8, 9), 1.0, r("cn", 6, 7))
     cp(r("l6"), r("ir", *six))
     ts(r("ia"), r("ipd", 0, 32), 15, O.bitwise_and)
     ts(r("dm"), r("ia"), 0.0, O.is_equal)
     ts(r("hi", *six), r("land", 0, 48, 8), 1.0 / 256, O.mult, -127.5 / 256, O.add)
-    issue("g", [r("hi", *six)], [r("fb", *six)], lambda: g.partition_broadcast(
-        ap(r("fb", *six)), ap(r("hi", 0, 6, 1, 0, 1)), 128))
+    issue("g", [r("hi", *six)], [r("fb", *e6)], lambda: g.partition_broadcast(
+        ap(r("fb", *e6)), ap(r("hi", 0, 6, 1, 0, 1)), 128))
     cp(r("v6", *six), r("land", 0, 48, 8))
     unit(3)
-    noise(0)
-    tt(r("key", *six), r("fb", *six), r("nr8", *six), O.add)
-    pu, tpu = places(0)
-    ts(r("oll", 0, 3), r("nws", 0, 3), r("zr0", me, me + 1), O.add, float(K), O.mult)
-
+    noise(0, False)
+    tt(r("key", *e6), r("fb", *e6), r("nr8", *six), O.add)
+    pu, tpu = places(0, r("rke"), r("zr0"))
+    ts(r("oll", 0, 3), r("nws", 0, 3), r("zr0", em, em + 1), O.add, float(K), O.mult)
+    cp(r("rw", 48, 54), r("v6", *six))
     for k in range(8):
         dma("s", ("mdr", 0, 16, 6 * k, 6 * k + 6, 1), r("v6", 0, 6, 1, 16 * k, 16 * k + 16), "dmd", 128)
     for k in range(8):
         dma("s", r("rw", 0, 48, 1, 16 * k, 16 * k + 16), ("mdr", 0, 16, 0, 48, 1), "drw", 128)
 
-    note(0)
-    ts(r("tk", 0, 1), r("zr0", me, me + 1), float(me), O.not_equal, 64.0, O.mult)
+    note(0, 1.0)
+    ts(r("tk", 0, 1), r("zr0", em, em + 1), float(me), O.not_equal, 64.0, O.mult)
     scatter(r("wf"), r("fb"), pu)
     ts(r("ox", 0, 3), r("nw", 0, 3), r("tk", 0, 1), O.add)
     anew("lb", r("oll", 0, 3), [(0, 288)], 288)
     gather(r("fa"), r("wf"), tpu)
-    tt(r("t0", *six), r("zr0", *six), r("ir", *six), O.not_equal)
+    scatter(r("wc"), r("hq"), pu)
+    tt(r("t0", *six), r("zr0", *e6), r("ir", *six), O.not_equal)
+    gather(r("cz"), r("wc"), tpu)
     weave(pack_ops("nb", 64))
     pick("xs", 0, 48, "nb", 0, 192, r("ox", 0, 3), [(0, 48), (64, 192)])
     for x, y in zip(both("xs", 0, K), both("w0", LX + K * me, LX + K * me + K)):
-        spread(x, y, "ax")
+        spread(x, y, "ax", "an")
     move("w0", LX + K * me, "xs", 0, K, "dxs")
-    noise(1)
-    weave(order_ops(r("ol", 6, 12), 96, 192), [lambda: ts(r("ob"), r("zr0", *six), r("cn", 4, 5), O.add)])
-    pick("hb", 0, 96, "tq", 0, 192, r("ol", 6, 12), [(0, 192)])
-    for k, (x, y) in enumerate(zip(("hb", "hb_s"), both("hp", TH * me, TH * me + TH))):
-        send([([z], share(z, k), piece(x, z), y) for z in others], r(x), "ah")
-    move("hp", TH * me, "hb", TH * third(me), TH, "dhb")
+    noise(1, True)
+    for k in range(4):
+        ac(r("dn", K * k, K * k + K), r("ps%d" % (4 + k), 0, K))
+    weave(order_ops(r("ol", 6, 12), 96, 192), [lambda: ts(r("ob"), r("zr0", *e6), r("cn", 4, 5), O.add)])
+    pick("hp", 0, TH, "tq", 0, 192, r("ol", 6, 12), [(0, 192)])
+    for x, y in zip(both("hp", 0, TH), both("hp", TH, 2 * TH)):
+        send([([mate], out_eng, x, y, "ah")], x)
+    move("w0", HX + TH * third(me), "hp", 0, TH, "dhb", 64)
+    move("w0", HX + TH * 3, "hp", TH, TH, "dhb", 64)
     mm(1, "uq", 0, "w0", 0, 288)
+    qz("wq", 0, 256, r("wt"))
 
-    def after_scalar():
-        lin(r("hf"), r("hf"), 1.0, WHOLE)
-        lin(r("hf"), r("hf"), 1.0, -WHOLE)
-        lin(r("h2"), r("hf"), -256.0, 0.0)
-        lin(r("rho", 48, 72), r("hf", 24, 48), 1.0, 0.0)
-    where = [
-        lambda: ts(r("hf"), r("rw"), 1.0 / 256, O.mult, -127.5 / 256, O.add),
-        lambda: cp(r("vf"), r("rw")),
-        after_scalar,
-        lambda: tt(r("rho", 0, 48), r("h2"), r("vf"), O.add),
-        lambda: lin(r("s1"), r("rho"), 1000.0, -47000.0, F.Relu),
-        lambda: lin(r("s2"), r("rho"), 1000.0, -95000.0, F.Relu),
-        lambda: tt(r("s1"), r("s1"), r("qa"), O.min),
-        lambda: tt(r("s2"), r("s2"), r("qb"), O.min),
-        lambda: tt(r("y0"), r("s1"), r("rho"), O.add),
-        lambda: tt(r("y0"), r("y0"), r("s2"), O.add),
-        lambda: gather(r("y0g"), r("y0"), r("ob")),
-        lambda: ts(r("lt"), r("y0g"), 48.0, O.is_lt),
-        lambda: tt(r("s1"), r("c1"), r("lt"), O.mult, r("l6")),
-        lambda: tt(r("y0g"), r("s1"), r("y0g"), O.add)]
     fit = [
-        lambda: lin(r("r96", *six), r("fa", *six), 1.0, float(K - P + K), F.Relu),
-        lambda: lin(r("r144", *six), r("fa", *six), 1.0, float(K - P), F.Relu),
-        lambda: tt(r("fan", *six), r("fa", *six), r("nr8", *six), O.add),
+        lambda: lin(r("r96", *six), r("fa", *e6), 1.0, float(K - P + K), F.Relu),
+        lambda: lin(r("r144", *six), r("fa", *e6), 1.0, float(K - P), F.Relu),
+        lambda: tt(r("fan", *six), r("fa", *e6), r("nr8", *six), O.add),
         lambda: tt(r("u1", *six), r("r96", *six), r("r144", *six), O.subtract),
         lambda: tt(r("v1", *six), r("u1", *six), r("r144", *six), O.subtract),
         lambda: tt(r("fan", *six), r("fan", *six), r("u1", *six), O.subtract),
@@ -498,73 +480,113 @@ def rank_program(g, core, T, topo):
         lambda: tt(r("apre", *six), r("fan", *six), r("v1", *six), O.add)]
     bases = [
         lambda: lin(r("c1", *six), r("t0", *six), float(LX), 0.0),
+        lambda: lin(r("bz", *six), r("zr0", *e6), float(K), float(LX - K)),
         lambda: tt(r("c1", *six), r("c1", *six), r("c48", *six), O.add),
-        lambda: lin(r("b32"), r("zr0"), float(TH), 0.0),
+        lambda: tt(r("hc2", *six), r("cz", *e6), r("bz", *six), O.subtract),
+        lambda: tt(r("hb2", *six), r("bz", *six), r("c1", *six), O.subtract),
+        lambda: tt(r("cb", *six), r("cz", *e6), r("c1", *six), O.add),
+        lambda: gather_a(r("hc"), r("hc2"), r("l6"), 0.5),
+        lambda: gather_a(r("hb"), r("hb2"), r("l6"), 0.5),
+        lambda: gather_a(r("ca"), r("cb"), r("l6"), 0.5),
+        lambda: ts(r("bzf"), r("zr0"), *((min(far) - 0.5, O.is_gt) if me < min(far) else (max(far) + 0.5, O.is_lt)), TH, O.mult),
+        lambda: lin(r("b32"), r("bzf"), 1.0, own),
         lambda: ac(r("sw", 0, 288), r("ps1", 0, 288))]
-    weave(where, fit, [idle] * 2 + bases)
+    where = [
+        lambda: ts(r("hw"), r("rw"), 1.0 / 256, O.mult, -127.5 / 256, O.add),
+        lambda: cp(r("vf"), r("rw")),
+        lambda: ts(r("h2"), r("hw"), -256.0, O.mult),
+        lambda: cp(r("rho", 54, 84), r("hw", 24, 54)),
+        lambda: tt(r("rho", 0, 54), r("h2"), r("vf"), O.add),
+        lambda: gather_a(r("rg"), r("rho"), r("ob")),
+        lambda: tt(r("yt"), r("rho"), r("ca"), O.add, r("ob")),
+        lambda: lin(r("sb"), r("rg"), 1.0, r("cn", 7, 8), F.Sign),
+        lambda: lin(r("sd"), r("rg"), 1.0, r("cn", 8, 9), F.Sign),
+        lambda: tt(r("sb"), r("sb"), r("hb"), O.mult),
+        lambda: tt(r("sd"), r("sd"), r("hc"), O.mult),
+        lambda: tt(r("yt"), r("yt"), r("sb"), O.add),
+        lambda: tt(r("y0g"), r("yt"), r("sd"), O.add)]
+    weave(bases, fit)
+    weave(where)
 
-    for k, a in ((0, 0), (2, 144)):
+    chip = min([me] + near)
+    for k, a in ((0, K * chip), (2, K * min(far))):
         mm(k, "uq", 0, "w0", LX + a, 144)
         ts(r("pos", a, a + 144), r("ps%d" % k, 0, 144), 0.0, O.is_gt)
         ac(r("sw", LX + a, LX + a + 144), r("ps%d" % k, 0, 144))
-    scan(r("psc"), r("x48"), r("pos"))
-    tt(r("key", *six), r("psc", 47, 288, 48), r("apre", *six), O.add)
-    pu, tpu = places(1)
-    my_z, ofs = r("zr1", me, me + 1), r("osl", 0, 12)
-    ts(r("og"), r("ogc"), my_z, O.add, 16.0, O.mult)
-    scatter(r("wb"), r("b32"), pu)
-    gather(r("osl"), r("y0g"), r("og"))
-    gather(r("bz"), r("wb"), tpu)
-    tt(r("m32"), r("sw"), r("dm"), O.mult, r("osl", 16, 18))
+        scan(r("psc", a, a + 144), r("x48", a, a + 144), r("pos", a, a + 144))
+    tt(r("key", *e6), r("psc", 47, 288, 48), r("apre", *six), O.add)
+    pu, tpu = places(1, r("v1r"), r("zg"))
+    og, ofs = r("zg", em, em + 1), r("osl", 0, 12)
+    gather(r("bzf"), r("wb"), tpu)
+    gather(r("osl"), r("y0g"), og)
+
+    def holder(i):
+        x = near[i] + sh
+        ts(r("oh", 6 * i, 6 * i + 6), r("n6"), r("bzf", x, x + 1), O.add)
+    holder(0)
+    tt(r("m32"), r("sw"), r("dm"), O.mult, r("osl", 12, 14))
     gather_a(r("st"), r("sw"), ofs)
-    tt(r("sm"), r("sw"), r("bm"), O.add, r("osl", 0, 8))
+    gather_a(r("l16"), r("y0g"), og)
+    holder(1)
     scan(r("sq"), r("rsq"), r("m32"), O.mult)
-    gather_a(r("lrow"), r("ir"), ofs)
-    note(1)
     s0, s1 = r("sq", 15, 16), r("sq", 31, 32, 1, 64)
+
+    pick("hs", 0, 2 * TH, "hp", 0, 192, r("oh"), [(0, 192)])
+    for x, y in zip(("hs", "hs_s"), both("w0", HX + TH * third(me), HX + TH * third(me) + TH)):
+        send([([z], all_eng[h_all * i:h_all * i + h_all], r(x, TH * i, TH * i + TH), y, "a3") for i, z in enumerate(near)],
+             r(x))
+
+    tt(r("sm"), r("st", 0, 128), r("bm"), O.add)
+    lin(r("sgn", 0, 192, 1, 64), lower("st"), -1.0, s1, F.Sign)
+    lin(r("ct", 1, 768, 4, 64), r("sgn", 0, 192, 1, 64), -1.0, 0.0, F.Relu)
     gts = gt_ops("st", s0, s1)
     low1("st")
     tie0(s0)
     gts[0]()
     gts[1]()
-    gts[2]()
     tie1(s1)
+    ts(r("ofz"), ofs, float(HX - 1), O.min)
     rank_ops()
 
-    chip = min([me] + near)
-    ts(r("oh", 0, 6, 2), r("bz", chip, chip + 3), own, O.add)
-    ts(r("oh", 1, 6, 2), r("bz", chip, chip + 3), r("cn", 9, 10), O.add)
-    pick("hs", 0, 96, "hp", 0, 192, r("oh"), [(0, 192)])
-    for x, y in zip(("hs", "hs_s"), both("w0", HX + TH * third(me), HX + TH * third(me) + TH)):
-        send([([z], all_eng[h_all * i:h_all * i + h_all], piece(x, z), y) for i, z in enumerate(near)], r(x), "a3")
-    move("w0", HX + TH * third(me), "hs", TH * third(me), TH, "dhs")
+    pick("tz", 0, 192, "w0", 0, 576, r("ofz"), [(0, 576)])
+    note(1, 1.0 / 16)
+    for k in range(4):
+        mm(4 + k, "eq", 128 * k, "tz", 0, 192)
+    for k in range(2):
+        ac(r("d%d" % k), r("ps%d" % (4 + k), 0, 192))
     select(r("sc"), r("ps3", 0, 192), 0, 192)
-    gather(r("l16"), r("y0g"), r("og", 0, 1))
-    ts(r("rof"), r("sc", 15, 192, 16), corr, O.subtract)
-    ts(r("tk", 0, 1), my_z, float(me), O.not_equal)
-    scatter(r("prm"), r("lrow"), r("rof"))
-    last = [
-        lambda: ts(r("rk", 0, 12), r("rof"), float(NX), O.add),
-        lambda: ts(r("fm", 0, 12), r("rof"), 48.0, O.is_lt, r("tk", 0, 1), O.mult),
-        lambda: tt(r("rk", 0, 12), r("rk", 0, 12), r("l16", 0, 12), O.subtract),
-        lambda: tt(r("rk", 0, 12), r("rk", 0, 12), r("fm", 0, 12), O.mult),
-        lambda: tt(r("fl", 0, 12), r("rk", 0, 12), r("l16", 0, 12), O.add),
-        lambda: cp(r("ofin"), r("fl", 0, 12))]
-    weave(order_ops(r("ol1", 0, 3), 0, 48), last[:2])
-    anew("lc", r("ol1", 0, 3), [(0, 576)], 576)
-    weave(last[2:])
-    qz("wq", 0, 256, r("wt"))
-    weave(pack_ops("w0", NX))
-    pick("fin", 0, 192, "w0", 0, 800, r("ofin"), [(0, 800)])
+    ts(r("tk", 0, 1), r("zg", em, em + 1), r("cn", 9, 10), O.not_equal)
+    ts(r("roc"), r("sc", 15, 192, 16), corr, O.subtract, K - 1.0, O.min)
+    tt(r("dlt", 0, 12), r("cnx"), r("l16", 0, 12), O.subtract)
+    ts(r("fm", 0, 12), r("sc", 15, 192, 16), r("cn", 6, 7), O.is_lt, r("tk", 0, 1), O.mult)
+    for k in (2, 3):
+        gather_a(r("g%d" % k), r("dn", K * k, K * k + K), r("roc"))
+
+    def make(k):
+        if k < 2:
+            tt(r("vn", k, 768, 4), r("dn", K * k, K * k + K), r("d%d" % k), O.add, r("roc"))
+        else:
+            tt(r("vn", k, 768, 4), r("ps%d" % (4 + k), 0, 192), r("g%d" % k), O.add)
+    make(0)
+    tt(r("fl", 0, 12), r("fm", 0, 12), r("dlt", 0, 12), O.mult)
+    make(1)
+    tt(r("fl", 0, 12), r("fl", 0, 12), r("l16", 0, 12), O.add)
+    make(2)
+    make(3)
+    cp(r("ofin"), r("fl", 0, 12))
+    qz("w0", NX, 192, r("vn"))
+    pick("fin", 0, 192, "w0", 0, 1152, r("ofin"), [(0, 1152)])
 
     dma("s", T.oc[:, :], r("fin"), "dout", 128)
     mm(1, "wq", 0, "fin", 0, 192)
-    mm(2, "wq", 128, "fin", 0, 192)
+    mm(2, "wq", 128, "fin", 0, 128)
+    mm(3, "wq", 128, "fin", 64, 128)
     for k in range(4):
         dma("s" if k < 2 else "a", T.osc[4 * k:4 * k + 4, :], r("fin_s", 0, 192, 1, 32 * k, 32 * k + 4), "dout", 128)
     cp(r("ysb", 0, 192), r("ps1", 0, 192))
     dma("s", T.y[:, 0:192], r("ysb", 0, 192), "dout", 128)
-    ac(r("ysb", 192, 384), r("ps2", 0, 192))
+    ac(r("ysb", 192, 320), r("ps2", 0, 128))
+    cp(r("ysb", 320, 384), r("ps3", 64, 128))
     dma("a", T.y[:, 192:384], r("ysb", 192, 384), "dout", 128)
     dma("s", T.od[:, :], r("odt", 0, 12, 1, 0, 1), "dout", 128)
 

from concourse.bass import DstId, RemoteDMATransfer
from concourse.mybir import dt, AluOpType as O, AxisListType, ActivationFunctionType as F

P, K, N = 192, 48, 6
LX, HX, NX = 288, 576, 960
TH = 96
BIG = 1e29
STEP = 2048.0

SCRATCH = {"mdr": ("dram", [16, 48], "uint16")}
ARENA = {}
for _d, _l in (
        ("bfloat16", "ut 4 tbt 768 nzt 704 wt 1024 ubt 512 onet 516 eht 516 vt 512 vn 768 ct 768 idt 128 x48 288 pos 288 psc 288"),
        ("int32", "ipd 128 pi 2 pa 6 ia 32 hi 8 fb 16 hw 54"),
        ("float32", "ir 800 m16 4 t16 192 dq 192 ones 128 paf 6 cn 16 bm 128 dm 32 nw 4 nws 4 nr8 8 "
                    "rsq 32 c48 8 sm 128 sm1 64 sg 192 sg1 192 sc 192 prm 192 sc2 192 "
                    "msgf 2 sw 968 dn 192 d0 192 d1 192 g2 192 g3 192 v1r 16 rke 16 cnx 12 n6 6 bzf 16 sgn 192 "
                    "st 192 m32 32 sq 32 ysb 384 odt 16 rho 96 hq 16 ca 96 hb 96 hc 96 sb 96 sd 96 rg 96 pio 4"),
        ("uint16", "land 48 v6 8 rw 54 l6 6 rof 12 ol 12 oll 4 om 4 ox 4 ob 6 zg 16 osl 16 oh 12 ofz 12 roc 12 ofin 12 pt 8")):
    _w = _l.split()
    for _k, _n in zip(_w[::2], _w[1::2]):
        SCRATCH[_k] = ("sbuf", [128, int(_n)], _d)
_w = ("tq 192 nq 176 wq 256 uq 128 oneq 128 eq 512 cq 192 ls 48 nb 192 hp 192 hs 192 lb 128 tz 192 xs 48 w0 1152 "
      "fin 192").split()
for _k, _n in zip(_w[::2], _w[1::2]):
    SCRATCH[_k] = ("sbuf", [128, int(_n)], "float8_e4m3fn_x4")
    SCRATCH[_k + "_s"] = ("sbuf", [128, int(_n)], "uint8")
for _k in range(8):
    SCRATCH["ps%d" % _k] = ("psum", [128, 512], "float32")
_o = 0
for _n, _l in ((54, "vf h2"), (96, "y0g yt"),
               (16, "key ks zr0 zr1 wr0 wr1 wf wb wc cz fa b32 l16 dlt fl fm"),
               (8, "gt pl t5 t0 apre fan r96 r144 u1 v1 c1 bz cb hb2 hc2 tk")):
    for _k in _l.split():
        ARENA[_k] = (_o, _n)
        _o += _n + (-_n) % 8
SCRATCH["ar"] = ("sbuf", [128, _o], "float32")

DMAS = ["du", "dtb", "dnz", "dw", "dpv", "dpad", "dls", "dhb", "dmd", "drw", "dxs", "dout"]
SEMAPHORES = ["cv", "ca", "ct", "cg", "am", "al", "ah", "ax", "an", "a3", "left"] + DMAS


def r(name, a=0, b=None, step=1, p=0, q=128):
    o, n = ARENA[name] if name in ARENA else (0, SCRATCH[name][1][1])
    return ("ar" if name in ARENA else name, p, q, o + a, o + (n if b is None else b), step)


def meet(x, y):
    return (x[0] == y[0] and x[1] < y[2] and y[1] < x[2] and x[3] < y[4] and y[3] < x[4]
            and not (x[5] == y[5] and (x[3] - y[3]) % x[5]))


def covers(x, y):
    return x[1] <= y[1] and y[2] <= x[2] and x[3] <= y[3] and y[4] <= x[4] and (x[5] == 1 or x[5] == y[5] and x[3] == y[3])


def weave(*chains):
    for k in range(max(len(c) for c in chains)):
        for c in chains:
            if k < len(c):
                c[k]()


def rank_program(g, core, T, topo):
    me = T.rank_of(core)
    if me is None:
        return
    queue = {"v": g.vector, "a": g.scalar, "t": g.tensor, "g": g, "s": g.sync}
    V, A, X = g.vector, g.scalar, g.tensor
    count = {"v": 0, "a": 0, "t": 0, "g": 0}
    clk = {q: {} for q in queue}
    snap, wr, rd, due = {}, {}, {}, {}

    def wait(q, s, v):
        if clk[q].get(s, 0) < v:
            queue[q].wait_ge(T.sem[s], v)
            for s2, v2 in snap.get((s, v), {}).items():
                clk[q][s2] = max(clk[q].get(s2, 0), v2)
            clk[q][s] = v

    def before(q, reads, writes):
        need = {}
        for x in reads + writes:
            bank = SCRATCH[x[0]][0] == "psum"
            hits = [(y, tok) for y, tok in wr.get(x[0], ()) if meet(x, y) or bank and tok[0] != "c" + q]
            if x in writes:
                hits += [(y, tok) for y, tok in rd.get(x[0], ()) if meet(x, y) or bank and tok[0] != "c" + q]
            elif bank:
                hits += [(y, tok) for y, tok in rd.get(x[0], ()) if tok[0] != "c" + q]
            for y, tok in hits:
                need[tok[0]] = max(need.get(tok[0], 0), tok[1])
        for s in sorted(need):
            wait(q, s, need[s])

    def wrote(x, tok):
        for d in (wr, rd):
            d[x[0]] = [e for e in d.get(x[0], ()) if not covers(x, e[0])]
        wr[x[0]].append((x, tok))

    def issue(q, reads, writes, fn, sem=None, total=0):
        before(q, reads, writes)
        if sem is None:
            count[q] += 1
            tok = ("c" + q, count[q])
            fn().then_inc(T.sem[tok[0]], 1)
            snap[tok] = dict(clk[q])
        else:
            tok = (sem, total)
            fn().then_inc(T.sem[sem], 16)
            due[sem] = total
        for x in reads:
            rd.setdefault(x[0], []).append((x, tok))
        for x in writes:
            wrote(x, tok)

    def ap(x, bits=None):
        v = T[x[0]][x[1]:x[2], x[3]:x[4]:x[5]] if x[5] > 1 else T[x[0]][x[1]:x[2], x[3]:x[4]]
        return v.bitcast(bits or dt.uint8) if SCRATCH[x[0]][2] == "float8_e4m3fn_x4" else v

    def mx(x):
        return T[x[0]][:, x[3]:x[4]]

    def num(s):
        return ap(s) if isinstance(s, tuple) else s

    def ts(out, in0, s1, op0, s2=None, op1=None):
        rs = [in0] + [s for s in (s1, s2) if isinstance(s, tuple)]
        if op1 is None:
            issue("v", rs, [out], lambda: V.tensor_scalar(ap(out), ap(in0), num(s1), None, op0))
        else:
            issue("v", rs, [out], lambda: V.tensor_scalar(ap(out), ap(in0), num(s1), num(s2), op0, op1))

    def tt(out, a, b, op, off=None):
        if off is None:
            issue("v", [a, b], [out], lambda: V.tensor_tensor(ap(out), ap(a), ap(b), op))
        else:
            issue("v", [a, b, off], [out], lambda: V.tensor_tensor(ap(out), ap(a).indirect(ap(off)), ap(b), op))

    def cp(out, in_):
        issue("v", [in_], [out], lambda: V.tensor_copy(ap(out), ap(in_)))

    def ac(out, in_):
        issue("a", [in_], [out], lambda: A.activation(ap(out), ap(in_), F.Copy))

    def lin(out, in_, scale, bias, func=F.Identity):
        rs = [in_] + ([bias] if isinstance(bias, tuple) else [])
        issue("a", rs, [out], lambda: A.activation(ap(out), ap(in_), func, bias=num(bias), scale=scale))

    def gather(out, win, off):
        issue("v", [win, off], [out], lambda: V.tensor_copy(ap(out), ap(win).indirect(ap(off))))

    def gather_a(out, win, off, scale=1.0):
        issue("a", [win, off], [out], lambda: A.activation(ap(out), ap(win).indirect(ap(off)), F.Identity, scale=scale))

    def scatter(win, val, off):
        issue("v", [val, off], [win], lambda: V.tensor_copy(ap(win).indirect(ap(off)), ap(val)))

    def scan(out, keep, add, op0=O.min, op1=O.add):
        issue("v", [keep, add], [out], lambda: V.tensor_tensor_scan(ap(out), ap(keep), ap(add), 0.0, op0, op1))

    corr = r("cn", 0, 1)

    def select(out, val, a, b):
        scan(out, r("dq", a, b), val, O.add, O.max)

    def fill(x, c):
        issue("v", [], [x], lambda: V.memset(ap(x), c))

    def zero(x, src):
        lin(x, src, 0.0, 0.0)

    def both(name, a, b):
        return [r(name, a, b), r(name + "_s", a, b)]

    def qz(cod, o, n, tile):
        c, s = both(cod, o, o + n)
        issue("v", [tile], [c, s], lambda: V.quantize_mx(mx(c), mx(s), ap(tile)))

    def mm(k, lhs, lo, rhs, ro, n, start=True, stop=True):
        w, x, out = both(lhs, lo, lo + 128), both(rhs, ro, ro + n), r("ps%d" % k, 0, n)
        issue("t", w + x, [out], lambda: X.matmul_mx(ap(out), mx(w[0]), mx(w[1]), mx(x[0]), mx(x[1]), start, stop))

    def pick(dst, c, n, src, a, b, off, parts):
        do, so, wc, ws = r(dst, c, c + n), r(dst + "_s", c, c + n), r(src, a, b), r(src + "_s", a, b)
        issue("v", [r(src, x, y) for x, y in parts] + [off], [do], lambda: V.tensor_copy(
            ap(do, dt.uint32), ap(wc, dt.uint32).indirect(ap(off))))
        issue("a", [r(src + "_s", x, y) for x, y in parts] + [off], [so], lambda: A.activation(
            ap(so), ap(ws).indirect(ap(off)), F.Copy))

    def iota(x, pattern, base, cm):
        if SCRATCH[x[0]][2] == "int32":
            issue("g", [], [x], lambda: g.iota(ap(x), pattern, base, cm))
        else:
            issue("g", [], [x], lambda: g.iota(ap(x), pattern, base, cm, allow_small_or_imprecise_dtypes=True))

    def dma(q, out, in_, sem, total=16):
        issue(q, [in_] if isinstance(in_, tuple) else [], [out] if isinstance(out, tuple) else [],
              lambda: queue[q].dma_start(num(out), num(in_)), sem, total)

    def move(dst, a, src, b, n, sem, total=32):
        for x, y in zip(both(dst, a, a + n), both(src, b, b + n)):
            dma("s", x, y, sem, total)

    def idle():
        pass

    sh = me % 2
    e6, em = (sh, sh + 6), me + sh
    others = [x for x in range(N) if x != me]

    def far_of(x):
        return [y for y in range(N) if topo.chip(T.cores[y]) != topo.chip(T.cores[x])]
    far = far_of(me)
    near = [x for x in others if x not in far]
    all_eng = topo.engines(core, T.cores[near[0]])
    out_eng = topo.engines(core, T.cores[far[0]])
    in_eng = [e for e in all_eng if e not in out_eng]

    def third(x):
        return [y for y in range(N) if y not in far_of(x)].index(x)
    mate = [x for x in far if third(x) == third(me)][0]

    def mask(es):
        return sum(1 << e for e in es)

    def dst(x):
        a = topo.addr(T.cores[x])
        return DstId(rid=a[0], pnc=a[1])

    def send(transfers, src):
        before("g", [src], [])
        due["left"] = due.get("left", 0) + sum(len(e[1]) for e in transfers)
        g.remote_dma_fused([RemoteDMATransfer(dst_ids=[dst(y) for y in x], dma_engine_mask=mask(es), remote_sem=T.sem[sem],
                                              srcs=[ap(s)], dsts=[ap(to)] * len(x)) for x, es, s, to, sem in transfers],
                           local_sem=T.sem["left"])

    def spread(src, to, sem, sem2=None):
        send([(far, out_eng, src, to, sem), (near, in_eng, src, to, sem2 or sem)], src)

    h_all = len(all_eng) // 2
    n_all = sum(len(out_eng) if x in far else len(in_eng) for x in others)
    for sem, tot, whom, buf, base, w in (("al", 2 * n_all, others, "w0", lambda x: K * x, K),
                                         ("ax", 2 * len(out_eng) * len(far), far, "w0", lambda x: LX + K * x, K),
                                         ("an", 2 * len(in_eng) * len(near), near, "w0", lambda x: LX + K * x, K),
                                         ("ah", 2 * len(out_eng), [mate], "hp", lambda x: TH, TH),
                                         ("a3", 2 * h_all * len(near), near, "w0", lambda x: HX + TH * third(x), TH)):
        due[sem] = tot
        for x in whom:
            for e in both(buf, base(x), base(x) + w):
                wrote(e, (sem, tot))
    due["am"] = n_all
    for x in others:
        wrote(r("land", 8 * x, 8 * x + 1), ("am", n_all))

    dma("s", r("ut"), T.u[:, 0:4], "du")
    dma("s", r("tbt"), T.tb[:, :], "dtb")
    dma("s", r("nzt", 0, 384), T.nz[:, :], "dnz", 32)
    dma("s", r("nzt", 384, 704), T.nz[:, 0:320], "dnz", 32)
    dma("s", r("vt", 192, 512), T.tb[:, 0:320], "dpv")
    dma("s", r("wt"), T.w[:, :], "dw")

    iota(r("pi"), [[0, 2]], 0, 1)
    iota(r("ipd"), [[1, 128]], 0, -1)
    iota(r("t16"), [[0, 12], [1, 16]], 0, 0)
    iota(r("ir", 0, 192), [[1, 192]], 0, 0)
    iota(r("m16"), [[16, 4]], 0, 0)
    iota(r("n6"), [[16, 6]], 0, 0)
    iota(r("c48"), [[48, 8]], 0, 0)
    iota(r("rke"), [[1, 16]], -sh, 0)
    iota(r("cnx"), [[16, 12]], NX, 0)
    iota(r("ir", 192, 800), [[1, 608]], 192, 0)
    iota(r("x48"), [[0, 6], [1000, 48]], 0, 0)

    fill(r("ones"), 1.0)
    fill(r("onet"), 1.0)
    zero(r("ct", 0, 512), r("onet", 0, 512))
    ts(r("pa", 0, 2), r("pi"), 64, O.bitwise_and)
    ts(r("pa", 2, 4), r("pi"), 4, O.arith_shift_right)
    ts(r("pa", 4, 6), r("pi"), 15, O.bitwise_and)
    qz("oneq", 0, 128, r("onet", 0, 512))
    cp(r("paf"), r("pa"))
    own = r("paf", 4, 5)
    ts(r("bm"), r("ipd"), 0.0, O.is_le, 3e29, O.mult)
    for k, (a, b) in enumerate(((7.5, 1.0), (11.5, -5.0), (12.5, 4.0))):
        ts(r("pio", k, k + 1), own, a, O.is_gt, b, O.mult)
    for k in range(3):
        tt(r("pio", 3, 4), r("pio", k, k + 1), r("pio", 3, 4) if k else own, O.add)
    for k in range(4):
        if k % 2:
            lin(r("ubt", k, 512, 4), r("ones"), 0.0, r("ut", k, k + 1))
        else:
            ts(r("ubt", k, 512, 4), r("onet", 0, 128), r("ut", k, k + 1), O.mult)
    zero(r("ct", 512, 768), r("onet", 0, 256))
    lin(r("t16", 0, 192, 16), r("ones", 0, 12), 0.0, -1000.0)
    lin(r("cn", 1, 2), own, 1.0, 0.5)
    lin(corr, own, 32.0, -480.0, F.Square)
    lin(r("cn", 10, 11), r("paf", 0, 1), -4.0, 256.0)
    lin(r("cn", 11, 12), r("paf", 0, 1), 4.0, 0.0)
    zero(r("eht"), r("onet"))
    qz("uq", 0, 128, r("ubt"))

    qz("tq", 0, 192, r("tbt"))
    mm(0, "uq", 0, "tq", 0, 192)
    mm(1, "tq", 0, "uq", 0, 128)
    mm(2, "tq", 64, "uq", 0, 128)
    mm(6, "uq", 0, "tq", 0, 192)
    ts(r("dq"), r("t16"), r("cn", 1, 2), O.subtract, STEP, O.mult)
    move("lb", K, "tq", K, 80, "dpad", 32)

    lin(r("sg"), r("ps6", 0, 192), 1.0, 0.0, F.Sign)
    issue("a", [r("sg")], [r("sg1"), r("msgf", 0, 1)], lambda: A.activation(
        ap(r("sg1")), ap(r("sg")), F.Relu, accum_out=ap(r("msgf", 0, 1))))

    def lower(src, a=0, b=192):
        return r(src, a, b, 1, 64, 128)

    def gt_ops(src, sp0, sp1):
        return [lambda: ts(r("ct", 0, 512, 4), r(src, 0, 128), sp0, O.is_gt),
                lambda: ts(r("ct", 512, 768, 4), r(src, 128, 192), sp0, O.is_ge),
                lambda: ts(r("ct", 1, 768, 4, 64), lower(src), sp1, O.is_gt)]

    def tie0(sp0):
        ts(r("ct", 2, 512, 4), r("sm"), sp0, O.is_equal)

    def low1(src):
        tt(r("sm1", 0, 64, 1, 64), lower(src, 128), r("bm", 64, 128, 1, 64), O.add)

    def tie1(sp1):
        ts(r("ct", 515, 768, 4, 64), r("sm1", 0, 64, 1, 64), sp1, O.is_equal)

    def rank_ops():
        qz("cq", 0, 192, r("ct"))
        mm(3, "oneq", 0, "cq", 0, 192)

    def order_ops(out, a, b):
        return [lambda: select(r("sc2", a, b), r("prm", a, b), a, b),
                lambda: ts(out, r("sc2", a + 15, b, 16), corr, O.subtract)]

    s0, s1 = r("ps1", 0, 1), r("ps2", 0, 1, 1, 64)
    gts = gt_ops("ps0", s0, s1)
    tt(r("sm"), r("ps0", 0, 128), r("bm"), O.add)
    low1("ps0")
    gts[0]()
    tie0(s0)
    gts[1]()
    gts[2]()
    tie1(s1)
    rank_ops()
    mm(4, "cq", 0, "oneq", 0, 128)
    mm(5, "cq", 64, "oneq", 0, 128)
    ts(r("idt"), r("ipd"), 0.0, O.is_equal, 0.5, O.mult)
    ac(r("eht", 3, 515, 4), r("idt"))

    my_land = r("land", 8 * me, 8 * me + 1)
    select(r("sc"), r("ps3", 0, 192), 0, 192)
    ts(r("msgf", 1, 2), r("msgf", 0, 1), r("cn", 10, 11), O.mult, r("ps4", 0, 1), O.add)
    ts(r("rof"), r("sc", 15, 192, 16), corr, O.subtract)
    ts(my_land, r("ps5", 0, 1), r("cn", 11, 12), O.mult, r("msgf", 1, 2), O.add)
    spread(my_land, my_land, "am")
    scatter(r("prm"), r("ir", 0, 192), r("rof"))
    weave(order_ops(r("ol", 0, 3), 0, 48))
    pick("ls", 0, 48, "tq", 0, 192, r("ol", 0, 3), [(0, 192)])
    for x, y in zip(both("ls", 0, K), both("w0", K * me, K * me + K)):
        spread(x, y, "al")
    move("w0", K * me, "ls", 0, K, "dls")

    six = (0, 6)
    lin(r("nr8", *six), r("ir", *six), -0.125, 0.0)
    lin(r("key"), r("ones", 0, 16), 0.0, -100.0)
    lin(r("cn", 2, 3), own, 1.0, -6.0, F.Relu)
    lin(r("nw", 0, 3), r("m16", 0, 3), 1.0, own)
    lin(r("nws", 0, 3), r("nw", 0, 3), 1.0 / K, 0.0)
    weave([lambda: fill(r("fb"), 0)], order_ops(r("om", 0, 3), 48, 96),
          [idle, lambda: qz("nq", 0, 176, r("nzt"))])
    pick("nb", 0, 48, "tq", 0, 192, r("om", 0, 3), [(0, 192)])
    lin(r("cn", 4, 5), own, 6.0, 0.0)
    lin(r("v1r"), r("rke"), 16.0, r("pio", 3, 4))
    lin(r("cn", 6, 7), corr, 1.0, float(K))
    lin(r("cn", 7, 8), r("ones", 0, 1), 0.0, 0.5 - K)
    lin(r("cn", 8, 9), r("ones", 0, 1), 0.0, 0.5 - 2 * K)
    lin(r("cn", 9, 10), r("pio", 3, 4), 1.0, 16.0 * me)
    zero(r("hq"), r("ones", 0, 16))
    for x in range(N):
        lin(r("hq", x + sh, x + sh + 1), r("ones", 0, 1), 0.0, float(HX + TH * (3 if x == mate else third(x)) - 2 * K))
    lin(r("cnx"), r("cnx"), 1.0, own)
    lin(r("rho", 84, 96), r("ones", 0, 12), 0.0, 0.0)
    lin(r("rsq"), r("x48", 0, 32), 0.0, 1.0)
    lin(r("rsq", 0, 32, 16), r("ones", 0, 2), 0.0, 0.0)
    lin(r("sw", HX, NX + 8), r("ir", 0, 392), 0.0, BIG)

    def unit(k):
        qz("eq", 128 * k, 128, r("eht", 3 - k, 515 - k))

    def noise(t, stop):
        for k in range(4):
            mm(4 + k, "eq", 128 * k, "nq", K * t, 128, True, stop)

    def places(k, val, zr):
        pu, tpu = r("pt", 4 * k, 4 * k + 1), r("pt", 4 * k + 2, 4 * k + 3)
        pl, t5 = r("pl", k, k + 1), r("t5", k, k + 1)
        select(r("ks"), r("key"), 0, 16)
        ts(r("gt", *six), r("key", *e6), corr, O.add, r("ks", 15, 16), O.is_gt)
        issue("v", [r("gt", *six)], [pl], lambda: V.tensor_reduce(ap(pl), ap(r("gt", *six)), AxisListType.X, O.add))
        ts(pu, pl, r("cn", 2, 3), O.add)
        ts(t5, pl, -1.0, O.mult, 5.0, O.add)
        scatter(r("wr%d" % k), val, pu)
        ts(tpu, t5, pl, O.min)
        if k:
            scatter(r("wb"), r("b32"), pu)
        gather(zr, r("wr%d" % k), tpu)
        return pu, tpu

    def note(k, scale):
        lin(r("odt", 6 * k, 6 * k + 6), r("wr%d" % k, *six), scale, 0.0)

    def anew(buf, off, parts, end):
        pick(buf, 0, 48, "w0", 0, end, off, parts)
        for k in range(4):
            mm(4 + k, "eq", 128 * k, buf, 0, 128, False, True)

    def pack_ops(out, o):
        return [lambda k=k: (cp if k % 2 else ac)(r("vt", k, 192, 4), r("ps%d" % (4 + k), 0, 48)) for k in range(4)] + [
            lambda: qz(out, o, 128, r("vt"))]

    unit(0)
    unit(1)
    unit(2)
    cp(r("l6"), r("ir", *six))
    ts(r("ia"), r("ipd", 0, 32), 15, O.bitwise_and)
    ts(r("dm"), r("ia"), 0.0, O.is_equal)
    ts(r("hi", *six), r("land", 0, 48, 8), 1.0 / 256, O.mult, -127.5 / 256, O.add)
    issue("g", [r("hi", *six)], [r("fb", *e6)], lambda: g.partition_broadcast(
        ap(r("fb", *e6)), ap(r("hi", 0, 6, 1, 0, 1)), 128))
    cp(r("v6", *six), r("land", 0, 48, 8))
    unit(3)
    noise(0, False)
    tt(r("key", *e6), r("fb", *e6), r("nr8", *six), O.add)
    pu, tpu = places(0, r("rke"), r("zr0"))
    ts(r("oll", 0, 3), r("nws", 0, 3), r("zr0", em, em + 1), O.add, float(K), O.mult)
    cp(r("rw", 48, 54), r("v6", *six))
    for k in range(8):
        dma("s", ("mdr", 0, 16, 6 * k, 6 * k + 6, 1), r("v6", 0, 6, 1, 16 * k, 16 * k + 16), "dmd", 128)
    for k in range(8):
        dma("s", r("rw", 0, 48, 1, 16 * k, 16 * k + 16), ("mdr", 0, 16, 0, 48, 1), "drw", 128)

    note(0, 1.0)
    ts(r("tk", 0, 1), r("zr0", em, em + 1), float(me), O.not_equal, 64.0, O.mult)
    scatter(r("wf"), r("fb"), pu)
    ts(r("ox", 0, 3), r("nw", 0, 3), r("tk", 0, 1), O.add)
    anew("lb", r("oll", 0, 3), [(0, 288)], 288)
    gather(r("fa"), r("wf"), tpu)
    scatter(r("wc"), r("hq"), pu)
    tt(r("t0", *six), r("zr0", *e6), r("ir", *six), O.not_equal)
    gather(r("cz"), r("wc"), tpu)
    weave(pack_ops("nb", 64))
    pick("xs", 0, 48, "nb", 0, 192, r("ox", 0, 3), [(0, 48), (64, 192)])
    for x, y in zip(both("xs", 0, K), both("w0", LX + K * me, LX + K * me + K)):
        spread(x, y, "ax", "an")
    move("w0", LX + K * me, "xs", 0, K, "dxs")
    noise(1, True)
    for k in range(4):
        ac(r("dn", K * k, K * k + K), r("ps%d" % (4 + k), 0, K))
    weave(order_ops(r("ol", 6, 12), 96, 192), [lambda: ts(r("ob"), r("zr0", *e6), r("cn", 4, 5), O.add)])
    pick("hp", 0, TH, "tq", 0, 192, r("ol", 6, 12), [(0, 192)])
    for x, y in zip(both("hp", 0, TH), both("hp", TH, 2 * TH)):
        send([([mate], out_eng, x, y, "ah")], x)
    move("w0", HX + TH * third(me), "hp", 0, TH, "dhb", 64)
    move("w0", HX + TH * 3, "hp", TH, TH, "dhb", 64)
    mm(1, "uq", 0, "w0", 0, 288)
    qz("wq", 0, 256, r("wt"))

    fit = [
        lambda: lin(r("r96", *six), r("fa", *e6), 1.0, float(K - P + K), F.Relu),
        lambda: lin(r("r144", *six), r("fa", *e6), 1.0, float(K - P), F.Relu),
        lambda: tt(r("fan", *six), r("fa", *e6), r("nr8", *six), O.add),
        lambda: tt(r("u1", *six), r("r96", *six), r("r144", *six), O.subtract),
        lambda: tt(r("v1", *six), r("u1", *six), r("r144", *six), O.subtract),
        lambda: tt(r("fan", *six), r("fan", *six), r("u1", *six), O.subtract),
        lambda: tt(r("v1", *six), r("v1", *six), r("t0", *six), O.mult),
        lambda: tt(r("apre", *six), r("fan", *six), r("v1", *six), O.add)]
    bases = [
        lambda: lin(r("c1", *six), r("t0", *six), float(LX), 0.0),
        lambda: lin(r("bz", *six), r("zr0", *e6), float(K), float(LX - K)),
        lambda: tt(r("c1", *six), r("c1", *six), r("c48", *six), O.add),
        lambda: tt(r("hc2", *six), r("cz", *e6), r("bz", *six), O.subtract),
        lambda: tt(r("hb2", *six), r("bz", *six), r("c1", *six), O.subtract),
        lambda: tt(r("cb", *six), r("cz", *e6), r("c1", *six), O.add),
        lambda: gather_a(r("hc"), r("hc2"), r("l6"), 0.5),
        lambda: gather_a(r("hb"), r("hb2"), r("l6"), 0.5),
        lambda: gather_a(r("ca"), r("cb"), r("l6"), 0.5),
        lambda: ts(r("bzf"), r("zr0"), *((min(far) - 0.5, O.is_gt) if me < min(far) else (max(far) + 0.5, O.is_lt)), TH, O.mult),
        lambda: lin(r("b32"), r("bzf"), 1.0, own),
        lambda: ac(r("sw", 0, 288), r("ps1", 0, 288))]
    where = [
        lambda: ts(r("hw"), r("rw"), 1.0 / 256, O.mult, -127.5 / 256, O.add),
        lambda: cp(r("vf"), r("rw")),
        lambda: ts(r("h2"), r("hw"), -256.0, O.mult),
        lambda: cp(r("rho", 54, 84), r("hw", 24, 54)),
        lambda: tt(r("rho", 0, 54), r("h2"), r("vf"), O.add),
        lambda: gather_a(r("rg"), r("rho"), r("ob")),
        lambda: tt(r("yt"), r("rho"), r("ca"), O.add, r("ob")),
        lambda: lin(r("sb"), r("rg"), 1.0, r("cn", 7, 8), F.Sign),
        lambda: lin(r("sd"), r("rg"), 1.0, r("cn", 8, 9), F.Sign),
        lambda: tt(r("sb"), r("sb"), r("hb"), O.mult),
        lambda: tt(r("sd"), r("sd"), r("hc"), O.mult),
        lambda: tt(r("yt"), r("yt"), r("sb"), O.add),
        lambda: tt(r("y0g"), r("yt"), r("sd"), O.add)]
    weave(bases, fit)
    weave(where)

    chip = min([me] + near)
    for k, a in ((0, K * chip), (2, K * min(far))):
        mm(k, "uq", 0, "w0", LX + a, 144)
        ts(r("pos", a, a + 144), r("ps%d" % k, 0, 144), 0.0, O.is_gt)
        ac(r("sw", LX + a, LX + a + 144), r("ps%d" % k, 0, 144))
        scan(r("psc", a, a + 144), r("x48", a, a + 144), r("pos", a, a + 144))
    tt(r("key", *e6), r("psc", 47, 288, 48), r("apre", *six), O.add)
    pu, tpu = places(1, r("v1r"), r("zg"))
    og, ofs = r("zg", em, em + 1), r("osl", 0, 12)
    gather(r("bzf"), r("wb"), tpu)
    gather(r("osl"), r("y0g"), og)

    def holder(i):
        x = near[i] + sh
        ts(r("oh", 6 * i, 6 * i + 6), r("n6"), r("bzf", x, x + 1), O.add)
    holder(0)
    tt(r("m32"), r("sw"), r("dm"), O.mult, r("osl", 12, 14))
    gather_a(r("st"), r("sw"), ofs)
    gather_a(r("l16"), r("y0g"), og)
    holder(1)
    scan(r("sq"), r("rsq"), r("m32"), O.mult)
    s0, s1 = r("sq", 15, 16), r("sq", 31, 32, 1, 64)

    pick("hs", 0, 2 * TH, "hp", 0, 192, r("oh"), [(0, 192)])
    for x, y in zip(("hs", "hs_s"), both("w0", HX + TH * third(me), HX + TH * third(me) + TH)):
        send([([z], all_eng[h_all * i:h_all * i + h_all], r(x, TH * i, TH * i + TH), y, "a3") for i, z in enumerate(near)],
             r(x))

    tt(r("sm"), r("st", 0, 128), r("bm"), O.add)
    lin(r("sgn", 0, 192, 1, 64), lower("st"), -1.0, s1, F.Sign)
    lin(r("ct", 1, 768, 4, 64), r("sgn", 0, 192, 1, 64), -1.0, 0.0, F.Relu)
    gts = gt_ops("st", s0, s1)
    low1("st")
    tie0(s0)
    gts[0]()
    gts[1]()
    tie1(s1)
    ts(r("ofz"), ofs, float(HX - 1), O.min)
    rank_ops()

    pick("tz", 0, 192, "w0", 0, 576, r("ofz"), [(0, 576)])
    note(1, 1.0 / 16)
    for k in range(4):
        mm(4 + k, "eq", 128 * k, "tz", 0, 192)
    for k in range(2):
        ac(r("d%d" % k), r("ps%d" % (4 + k), 0, 192))
    select(r("sc"), r("ps3", 0, 192), 0, 192)
    ts(r("tk", 0, 1), r("zg", em, em + 1), r("cn", 9, 10), O.not_equal)
    ts(r("roc"), r("sc", 15, 192, 16), corr, O.subtract, K - 1.0, O.min)
    tt(r("dlt", 0, 12), r("cnx"), r("l16", 0, 12), O.subtract)
    ts(r("fm", 0, 12), r("sc", 15, 192, 16), r("cn", 6, 7), O.is_lt, r("tk", 0, 1), O.mult)
    for k in (2, 3):
        gather_a(r("g%d" % k), r("dn", K * k, K * k + K), r("roc"))

    def make(k):
        if k < 2:
            tt(r("vn", k, 768, 4), r("dn", K * k, K * k + K), r("d%d" % k), O.add, r("roc"))
        else:
            tt(r("vn", k, 768, 4), r("ps%d" % (4 + k), 0, 192), r("g%d" % k), O.add)
    make(0)
    tt(r("fl", 0, 12), r("fm", 0, 12), r("dlt", 0, 12), O.mult)
    make(1)
    tt(r("fl", 0, 12), r("fl", 0, 12), r("l16", 0, 12), O.add)
    make(2)
    make(3)
    cp(r("ofin"), r("fl", 0, 12))
    qz("w0", NX, 192, r("vn"))
    pick("fin", 0, 192, "w0", 0, 1152, r("ofin"), [(0, 1152)])

    dma("s", T.oc[:, :], r("fin"), "dout", 128)
    mm(1, "wq", 0, "fin", 0, 192)
    mm(2, "wq", 128, "fin", 0, 128)
    mm(3, "wq", 128, "fin", 64, 128)
    for k in range(4):
        dma("s" if k < 2 else "a", T.osc[4 * k:4 * k + 4, :], r("fin_s", 0, 192, 1, 32 * k, 32 * k + 4), "dout", 128)
    cp(r("ysb", 0, 192), r("ps1", 0, 192))
    dma("s", T.y[:, 0:192], r("ysb", 0, 192), "dout", 128)
    ac(r("ysb", 192, 320), r("ps2", 0, 128))
    cp(r("ysb", 320, 384), r("ps3", 64, 128))
    dma("a", T.y[:, 192:384], r("ysb", 192, 384), "dout", 128)
    dma("s", T.od[:, :], r("odt", 0, 12, 1, 0, 1), "dout", 128)

    for q in count:
        due["c" + q] = count[q]
    for s in sorted(due):
        g.wait_ge(T.sem[s], due[s])
